import numpy as np
import ml_dtypes


def mxq(x, axis, fmt="e4m3"):
    dtype, down = {"e4m3": (ml_dtypes.float8_e4m3fn, 7), "e5m2": (ml_dtypes.float8_e5m2, 14)}[fmt]
    v = np.moveaxis(np.asarray(x, np.float32).astype(ml_dtypes.bfloat16).astype(np.float64), axis, -1)
    blocks = v.reshape(v.shape[:-1] + (-1, 32))
    amax = np.abs(blocks).max(-1, keepdims=True)
    byte = np.maximum(np.where(amax > 0, np.frexp(amax)[1] - 1 + 127, 0) - down, 1)
    scale = np.exp2(byte - 127.0)
    codes = (blocks / scale).astype(np.float32).astype(dtype).astype(np.float64)
    return np.moveaxis((codes * scale).reshape(v.shape), -1, axis)


WIDE = False


def mx_kscale(k):
    if not WIDE:
        return np.ones(k)
    levels = np.array([10, -10, 5, -5, 0])
    if k % 512:
        return np.exp2(np.random.permutation(np.resize(levels, k // 32))).repeat(32)
    a = np.empty((k // 512, 16))
    for p in range(k // 512):
        a[p, :8] = np.random.permutation(np.resize(levels, 8))
        for g in range(8):
            far = levels[np.abs(levels - a[p, g]) >= 10]
            a[p, g + 8] = far[np.random.randint(len(far))]
    return np.exp2(a.ravel()).repeat(32)


def f64(x):
    return np.asarray(x).astype(np.float64)


def striped(idx):
    return np.tile(idx.reshape(-1, 16).T, (8, 1)).astype(np.uint16)


def unstriped(offs):
    return offs[:16].T.reshape(-1).astype(np.int64)


def pack_weight(w):
    k, n = w.shape
    w = f64(np.asarray(w, np.float32).astype(ml_dtypes.bfloat16)).reshape(k // 32, 32, n)
    amax = np.abs(w).max(1)
    byte = np.clip(np.where(amax > 0, np.frexp(amax)[1] - 1 + 127 - 7, 1), 1, 254)
    scaled = (w * np.exp2(127.0 - byte)[:, None, :]).reshape(k, n).astype(np.float32)
    words = np.ascontiguousarray(scaled.reshape(k // 512, 128, 4, n).transpose(0, 1, 3, 2)).astype(ml_dtypes.float8_e4m3fn).view(np.uint8)
    return words, np.ascontiguousarray(byte.astype(np.uint8).reshape(k // 512, 16, n))


def unpack_weight(words, scales):
    g, p, n, _ = words.shape
    vals = np.ascontiguousarray(words).view(ml_dtypes.float8_e4m3fn).astype(np.float64) * np.repeat(np.exp2(scales.astype(np.float64) - 127.0), 8, axis=1)[..., None]
    return vals.transpose(0, 1, 3, 2).reshape(g * 512, n)


K, T, D, H, N = 512, 1024, 2, 512, 128
P = 2 ** 7


def setup_inputs():
    n = np.random.standard_normal
    s = mx_kscale(K)[:, None]
    u = mx_kscale(H)
    packed_xT = pack_weight(n((K, T)) * s)
    return {
        "x_words": packed_xT[0],
        "x_scales": packed_xT[1],
        "w1": (n((K, H)) / np.sqrt(K) / s * u).astype(np.float32),
        "w2": (n((H, N)) / np.sqrt(H) / u[:, None]).astype(np.float32),
        "gate": (np.tile(np.random.uniform(0.2, 1.0, (D, 1, T)) / np.sqrt(D), (1, P, 1))).astype(np.float32),
        "pos1": striped(np.random.permutation(T)),
        "pos2": striped(np.random.permutation(T)),
    }


def reference(x_words, x_scales, w1, w2, gate, pos1, pos2):
    xq = unpack_weight(x_words, x_scales)
    h = mxq(f64(w1), 0, "e4m3").T @ xq
    z = h - (h[:, unstriped(pos1)] * f64(gate)[0, :1] + h[:, unstriped(pos2)] * f64(gate)[1, :1])
    return mxq(f64(w2), 0, "e4m3").T @ mxq(z, 0, "e4m3")

@@ -1,0 +1,184 @@
+from contextlib import ExitStack
+
+import concourse.mybir as mybir
+from concourse.masks import make_identity
+
+K, T, H, N = 512, 1024, 512, 128
+FLOPS = 2 * K * H * T + 2 * H * N * T
+
+F32 = mybir.dt.float32
+BF16 = mybir.dt.bfloat16
+I32 = mybir.dt.int32
+U32 = mybir.dt.uint32
+U16 = mybir.dt.uint16
+U8 = mybir.dt.uint8
+FP8X4 = mybir.dt.float8_e4m3fn_x4
+MULT = mybir.AluOpType.mult
+COPY = mybir.ActivationFunctionType.Copy
+
+P = 128
+PACK = 4
+BANK = 512
+LIST_ROWS = 16
+CHUNKS = (512, 256, 128, 128)
+
+
+def tile_picked_wlapl_none_l_kernel(
+    tc, x_words, x_scales, w1, w2, gate, pos1, pos2, out
+):
+    nc = tc.nc
+    with ExitStack() as ctx:
+        keep = ctx.enter_context(tc.tile_pool(name="keep", bufs=1))
+        psum = ctx.enter_context(tc.psum_pool(name="psum", bufs=4))
+
+        x_plane = keep.tile([P, T], U8, name="x_plane", align_bytes=64)
+        nc.vector.memset(x_plane[:].bitcast(I32), 0)
+        for q in range(4):
+            nc.scalar.dma_start(
+                out=x_plane[32 * q : 32 * q + 4, :].bitcast(I32),
+                in_=x_scales[0, 4 * q : 4 * q + 4, :].bitcast(I32),
+            )
+
+        gate_cols = keep.tile([P, 2, 8], F32, name="gate_cols")
+        nc.sync.dma_start(out=gate_cols[:], in_=gate[:, 0, :].rearrange("d (p j) -> p d j", j=8))
+
+        w_raw = [keep.tile([P, PACK, P], F32, name=f"w_raw{t}") for t in range(5)]
+        w1_rows = w1.rearrange("(p j) c -> p j c", j=PACK)
+        x_flat = x_words[0].rearrange("p n t -> p (n t)").bitcast(I32)
+        x_codes = [keep.tile([P, BANK], U32, name=f"x_codes{c}", align_bytes=64) for c in range(2)]
+        nc.sync.dma_start(out=w_raw[0][:], in_=w1_rows[:, :, 0:P])
+        for c in range(2):
+            nc.sync.dma_start(out=x_codes[c][:].bitcast(I32), in_=x_flat[:, c * BANK : (c + 1) * BANK])
+        lists = [keep.tile([P, T // LIST_ROWS], U16, name=f"list{d}") for d in range(2)]
+        nc.sync.dma_start(lists[0][:], pos1)
+        nc.sync.dma_start(lists[1][:], pos2)
+        for t in range(1, 4):
+            nc.sync.dma_start(out=w_raw[t][:], in_=w1_rows[:, :, t * P : (t + 1) * P])
+        nc.sync.dma_start(out=w_raw[4][:], in_=w2.rearrange("(p j) c -> p j c", j=PACK))
+
+        ident = keep.tile([P, P], F32, name="ident")
+        make_identity(nc, ident[:])
+
+        neg_gate = [keep.tile([P, T], F32, name=f"neg_gate{d}") for d in range(2)]
+        for d in range(2):
+            for half in range(2):
+                bank = psum.tile([P, 4, P], F32, name="z_t", tag="z_t")
+                for j in range(4):
+                    col = 4 * half + j
+                    nc.tensor.transpose(
+                        bank[:, j, :], gate_cols[:, d, col : col + 1].to_broadcast([P, P]), ident[:]
+                    )
+                nc.scalar.activation(
+                    out=neg_gate[d][:].rearrange("q (n j) -> q n j", j=8)[:, :, 4 * half : 4 * half + 4],
+                    in_=bank[:].rearrange("q j n -> q n j"),
+                    func=COPY,
+                    scale=-1.0,
+                )
+
+        w_codes = [keep.tile([P, P], U32, name=f"w_codes{t}", align_bytes=64) for t in range(5)]
+        w_plane = [keep.tile([P, P], U8, name=f"w_plane{t}", align_bytes=64) for t in range(5)]
+
+        def quantise_weight(t):
+            grouped = keep.tile([P, P, PACK], BF16, name=f"w_grouped{t}", align_bytes=64)
+            nc.vector.tensor_copy(
+                out=grouped[:].rearrange("p (c i) j -> p c j i", i=4),
+                in_=w_raw[t][:].rearrange("p j (c i) -> p c j i", i=4),
+            )
+            nc.vector.quantize_mx(
+                out=w_codes[t][:].bitcast(FP8X4),
+                scales=w_plane[t][:],
+                in_=grouped[:].rearrange("p c j -> p (c j)"),
+            )
+
+        h = [keep.tile([P, T], F32, name=f"h{t}") for t in range(4)]
+
+        def project(t):
+            for c in range(2):
+                cols = slice(c * BANK, (c + 1) * BANK)
+                acc = psum.tile([P, BANK], F32, name="acc", tag="acc")
+                nc.tensor.matmul_mx(
+                    out=acc[:],
+                    lhsT=w_codes[t][:].bitcast(FP8X4),
+                    lhsT_scale=w_plane[t][:],
+                    rhs=x_codes[c][:].bitcast(FP8X4),
+                    rhs_scale=x_plane[:, cols],
+                    start=True,
+                    stop=True,
+                )
+                if t == 0 and c == 1:
+                    nc.vector.tensor_copy(out=h[t][:, cols], in_=acc[:])
+                else:
+                    nc.scalar.copy(out=h[t][:, cols], in_=acc[:])
+
+        for t in range(4):
+            quantise_weight(t)
+            project(t)
+        quantise_weight(4)
+
+        def gather_and_sum(v0, width, t, banks):
+            terms = []
+            for d in range(2):
+                term = keep.tile([P, width], F32, name=f"term{v0}_{t}_{d}")
+                nc.vector.tensor_tensor(
+                    term[:],
+                    h[t][:].indirect(lists[d][:, v0 // LIST_ROWS : (v0 + width) // LIST_ROWS]),
+                    neg_gate[d][:, v0 : v0 + width],
+                    MULT,
+                )
+                terms.append(term)
+            sources = [h[t][:, v0 : v0 + width], terms[0][:], terms[1][:]]
+            for s, source in enumerate(sources):
+                for b, bank in enumerate(banks):
+                    nc.tensor.matmul(
+                        bank[:, t * P : (t + 1) * P],
+                        source[:, b * P : (b + 1) * P],
+                        ident[:],
+                        start=(s == 0),
+                        stop=(s == 2),
+                        is_transpose=True,
+                    )
+
+        def finish(v0, width, banks):
+            z_bf = keep.tile([P, width, PACK], BF16, name=f"z_bf{v0}", align_bytes=64)
+            z_words = z_bf[:].rearrange("p v j -> p (v j)").bitcast(F32).rearrange("p (v u) -> p v u", u=2)
+            for b0 in range(0, len(banks), 2):
+                pair = banks[b0 : b0 + 2]
+                back = psum.tile([P, 2, 2, P], F32, name="acc", tag="acc")
+                for b, bank in enumerate(pair):
+                    rows = keep.tile([P, 2, P, 2], BF16, name=f"z_rows{v0}_{b0 + b}")
+                    nc.scalar.copy(out=rows[:], in_=bank[:].rearrange("v (p u e) -> v u p e", u=2, e=2))
+                    words = rows[:].rearrange("v u p e -> v (u p e)").bitcast(F32)
+                    for u in range(2):
+                        nc.tensor.transpose(back[:, b, u, :], words[:, u * P : (u + 1) * P], ident[:])
+                nc.scalar.copy(
+                    out=z_words[:, b0 * P : (b0 + len(pair)) * P, :].rearrange("p (b v) u -> p b v u", v=P),
+                    in_=back[:, 0 : len(pair), :, :].rearrange("p b u v -> p b v u"),
+                )
+            z_codes = keep.tile([P, width], U32, name=f"z_codes{v0}", align_bytes=64)
+            z_plane = keep.tile([P, width], U8, name=f"z_plane{v0}", align_bytes=64)
+            nc.vector.quantize_mx(
+                out=z_codes[:].bitcast(FP8X4),
+                scales=z_plane[:],
+                in_=z_bf[:].rearrange("p v j -> p (v j)"),
+            )
+            acc = psum.tile([P, BANK], F32, name="acc", tag="acc")
+            nc.tensor.matmul_mx(
+                out=acc[:, 0:width],
+                lhsT=w_codes[4][:].bitcast(FP8X4),
+                lhsT_scale=w_plane[4][:],
+                rhs=z_codes[:].bitcast(FP8X4),
+                rhs_scale=z_plane[:],
+                start=True,
+                stop=True,
+            )
+            result = keep.tile([P, width], F32, name=f"result{v0}")
+            nc.scalar.copy(out=result[:], in_=acc[:, 0:width])
+            nc.sync.dma_start(out=out[:, v0 : v0 + width], in_=result[:])
+
+        v0 = 0
+        for width in CHUNKS:
+            banks = [psum.tile([P, BANK], F32, name="z_t", tag="z_t") for b in range(width // P)]
+            for t in range(4):
+                gather_and_sum(v0, width, t, banks)
+            finish(v0, width, banks)
+            v0 = v0 + width

@@ -20,7 +20,11 @@ P = 128
 PACK = 4
 BANK = 512
 LIST_ROWS = 16
+RING = 1024
 CHUNKS = (512, 256, 128, 128)
+SUM_BANKS = (0, 1, 2, 3, 4, 5, 1, 3)
+BACK_BANKS = (6, 7)
+LAST_BANK = 5
 
 
 def tile_picked_wlapl_none_l_kernel(
@@ -29,40 +33,44 @@ def tile_picked_wlapl_none_l_kernel(
     nc = tc.nc
     with ExitStack() as ctx:
         keep = ctx.enter_context(tc.tile_pool(name="keep", bufs=1))
-        psum = ctx.enter_context(tc.psum_pool(name="psum", bufs=4))
+        psum = ctx.enter_context(tc.psum_pool(name="psum", bufs=1))
+        banks = [psum.tile([P, BANK], F32, name=f"bank{b}") for b in range(8)]
 
         x_plane = keep.tile([P, T], U8, name="x_plane", align_bytes=64)
-        nc.vector.memset(x_plane[:].bitcast(I32), 0)
+        nc.gpsimd.memset(x_plane[:].bitcast(I32), 0)
+
+        gate_cols = keep.tile([P, 2, 8], F32, name="gate_cols")
+        nc.scalar.dma_start(out=gate_cols[:], in_=gate[:, 0, :].rearrange("d (p j) -> p d j", j=8))
         for q in range(4):
             nc.scalar.dma_start(
                 out=x_plane[32 * q : 32 * q + 4, :].bitcast(I32),
                 in_=x_scales[0, 4 * q : 4 * q + 4, :].bitcast(I32),
             )
 
-        gate_cols = keep.tile([P, 2, 8], F32, name="gate_cols")
-        nc.sync.dma_start(out=gate_cols[:], in_=gate[:, 0, :].rearrange("d (p j) -> p d j", j=8))
-
-        w_raw = [keep.tile([P, PACK, P], F32, name=f"w_raw{t}") for t in range(5)]
         w1_rows = w1.rearrange("(p j) c -> p j c", j=PACK)
-        x_flat = x_words[0].rearrange("p n t -> p (n t)").bitcast(I32)
-        x_codes = [keep.tile([P, BANK], U32, name=f"x_codes{c}", align_bytes=64) for c in range(2)]
-        nc.sync.dma_start(out=w_raw[0][:], in_=w1_rows[:, :, 0:P])
-        for c in range(2):
-            nc.sync.dma_start(out=x_codes[c][:].bitcast(I32), in_=x_flat[:, c * BANK : (c + 1) * BANK])
+        w1_first = keep.tile([P, PACK, P], F32, name="w1_first")
+        w1_second = keep.tile([P, PACK, P], F32, name="w1_second")
+        w1_rest = keep.tile([P, PACK, 2 * P], F32, name="w1_rest")
+        w2_raw = keep.tile([P, PACK, P], F32, name="w2_raw")
+        x_codes = keep.tile([P, T], U32, name="x_codes", align_bytes=64)
         lists = [keep.tile([P, T // LIST_ROWS], U16, name=f"list{d}") for d in range(2)]
+        nc.sync.dma_start(out=w1_first[:], in_=w1_rows[:, :, 0:P])
+        nc.sync.dma_start(out=x_codes[:].bitcast(I32), in_=x_words[0].rearrange("p n t -> p (n t)").bitcast(I32))
+        nc.sync.dma_start(out=w1_second[:], in_=w1_rows[:, :, P : 2 * P])
         nc.sync.dma_start(lists[0][:], pos1)
         nc.sync.dma_start(lists[1][:], pos2)
-        for t in range(1, 4):
-            nc.sync.dma_start(out=w_raw[t][:], in_=w1_rows[:, :, t * P : (t + 1) * P])
-        nc.sync.dma_start(out=w_raw[4][:], in_=w2.rearrange("(p j) c -> p j c", j=PACK))
+        nc.sync.dma_start(out=w1_rest[:], in_=w1_rows[:, :, 2 * P : 4 * P])
+        nc.sync.dma_start(out=w2_raw[:], in_=w2.rearrange("(p j) c -> p j c", j=PACK))
+        w_raw = [w1_first[:], w1_second[:], w1_rest[:, :, 0:P], w1_rest[:, :, P : 2 * P], w2_raw[:]]
 
         ident = keep.tile([P, P], F32, name="ident")
         make_identity(nc, ident[:])
 
         neg_gate = [keep.tile([P, T], F32, name=f"neg_gate{d}") for d in range(2)]
-        for d in range(2):
+
+        def spread_gate(d):
             for half in range(2):
-                bank = psum.tile([P, 4, P], F32, name="z_t", tag="z_t")
+                bank = banks[4 + 2 * d + half][:].rearrange("q (j n) -> q j n", j=4)
                 for j in range(4):
                     col = 4 * half + j
                     nc.tensor.transpose(
@@ -70,7 +78,7 @@ def tile_picked_wlapl_none_l_kernel(
                     )
                 nc.scalar.activation(
                     out=neg_gate[d][:].rearrange("q (n j) -> q n j", j=8)[:, :, 4 * half : 4 * half + 4],
-                    in_=bank[:].rearrange("q j n -> q n j"),
+                    in_=bank.rearrange("q j n -> q n j"),
                     func=COPY,
                     scale=-1.0,
                 )
@@ -80,10 +88,13 @@ def tile_picked_wlapl_none_l_kernel(
 
         def quantise_weight(t):
             grouped = keep.tile([P, P, PACK], BF16, name=f"w_grouped{t}", align_bytes=64)
-            nc.vector.tensor_copy(
-                out=grouped[:].rearrange("p (c i) j -> p c j i", i=4),
-                in_=w_raw[t][:].rearrange("p j (c i) -> p c j i", i=4),
-            )
+            if t in (2, 3, 4):
+                nc.scalar.copy(out=grouped[:], in_=w_raw[t].rearrange("p j c -> p c j"))
+            else:
+                nc.vector.tensor_copy(
+                    out=grouped[:].rearrange("p (c i) j -> p c j i", i=4),
+                    in_=w_raw[t].rearrange("p j (c i) -> p c j i", i=4),
+                )
             nc.vector.quantize_mx(
                 out=w_codes[t][:].bitcast(FP8X4),
                 scales=w_plane[t][:],
@@ -95,42 +106,50 @@ def tile_picked_wlapl_none_l_kernel(
         def project(t):
             for c in range(2):
                 cols = slice(c * BANK, (c + 1) * BANK)
-                acc = psum.tile([P, BANK], F32, name="acc", tag="acc")
+                acc = banks[4 + 2 * (t % 2) + c]
                 nc.tensor.matmul_mx(
                     out=acc[:],
                     lhsT=w_codes[t][:].bitcast(FP8X4),
                     lhsT_scale=w_plane[t][:],
-                    rhs=x_codes[c][:].bitcast(FP8X4),
+                    rhs=x_codes[:, cols].bitcast(FP8X4),
                     rhs_scale=x_plane[:, cols],
                     start=True,
                     stop=True,
                 )
-                if t == 0 and c == 1:
+                if t == 0 and c == 0:
                     nc.vector.tensor_copy(out=h[t][:, cols], in_=acc[:])
                 else:
                     nc.scalar.copy(out=h[t][:, cols], in_=acc[:])
 
+        spread_gate(0)
+        spread_gate(1)
         for t in range(4):
             quantise_weight(t)
             project(t)
         quantise_weight(4)
 
-        def gather_and_sum(v0, width, t, banks):
+        ring = keep.tile([P, RING], F32, name="ring")
+
+        def sum_bank(block, t):
+            return banks[LAST_BANK if (block, t) == (T // P - 1, 3) else SUM_BANKS[block]]
+
+        def gather_and_sum(v0, width, t):
             terms = []
             for d in range(2):
-                term = keep.tile([P, width], F32, name=f"term{v0}_{t}_{d}")
+                at = (8 * v0 + (2 * t + d) * width) % RING
+                term = ring[:, at : at + width]
                 nc.vector.tensor_tensor(
-                    term[:],
+                    term,
                     h[t][:].indirect(lists[d][:, v0 // LIST_ROWS : (v0 + width) // LIST_ROWS]),
                     neg_gate[d][:, v0 : v0 + width],
                     MULT,
                 )
                 terms.append(term)
-            sources = [h[t][:, v0 : v0 + width], terms[0][:], terms[1][:]]
+            sources = [h[t][:, v0 : v0 + width], terms[0], terms[1]]
             for s, source in enumerate(sources):
-                for b, bank in enumerate(banks):
+                for b in range(width // P):
                     nc.tensor.matmul(
-                        bank[:, t * P : (t + 1) * P],
+                        sum_bank(v0 // P + b, t)[:, t * P : (t + 1) * P],
                         source[:, b * P : (b + 1) * P],
                         ident[:],
                         start=(s == 0),
@@ -138,22 +157,23 @@ def tile_picked_wlapl_none_l_kernel(
                         is_transpose=True,
                     )
 
-        def finish(v0, width, banks):
+        def finish(v0, width, turn):
+            blocks = width // P
             z_bf = keep.tile([P, width, PACK], BF16, name=f"z_bf{v0}", align_bytes=64)
-            z_words = z_bf[:].rearrange("p v j -> p (v j)").bitcast(F32).rearrange("p (v u) -> p v u", u=2)
-            for b0 in range(0, len(banks), 2):
-                pair = banks[b0 : b0 + 2]
-                back = psum.tile([P, 2, 2, P], F32, name="acc", tag="acc")
-                for b, bank in enumerate(pair):
-                    rows = keep.tile([P, 2, P, 2], BF16, name=f"z_rows{v0}_{b0 + b}")
-                    nc.scalar.copy(out=rows[:], in_=bank[:].rearrange("v (p u e) -> v u p e", u=2, e=2))
-                    words = rows[:].rearrange("v u p e -> v (u p e)").bitcast(F32)
-                    for u in range(2):
-                        nc.tensor.transpose(back[:, b, u, :], words[:, u * P : (u + 1) * P], ident[:])
-                nc.scalar.copy(
-                    out=z_words[:, b0 * P : (b0 + len(pair)) * P, :].rearrange("p (b v) u -> p b v u", v=P),
-                    in_=back[:, 0 : len(pair), :, :].rearrange("p b u v -> p b v u"),
-                )
+            z_words = z_bf[:].rearrange("p v j -> p (v j)").bitcast(F32).rearrange("p (b v u) -> p b v u", u=2, v=P)
+            back = banks[BACK_BANKS[turn % 2]][:].rearrange("p (b u v) -> p b u v", u=2, v=P)
+            for b in range(blocks):
+                rows = keep.tile([P, 2, P, 2], BF16, name=f"z_rows{v0}_{b}")
+                block = v0 // P + b
+                for t0, t1 in ((0, 3), (3, 4)) if block == T // P - 1 else ((0, 4),):
+                    nc.scalar.copy(
+                        out=rows[:, :, 32 * t0 : 32 * t1, :],
+                        in_=sum_bank(block, t0)[:, t0 * P : t1 * P].rearrange("v (p u e) -> v u p e", u=2, e=2),
+                    )
+                words = rows[:].rearrange("v u p e -> v (u p e)").bitcast(F32)
+                for u in range(2):
+                    nc.tensor.transpose(back[:, b, u, :], words[:, u * P : (u + 1) * P], ident[:])
+            nc.scalar.copy(out=z_words, in_=back[:, 0:blocks, :, :].rearrange("p b u v -> p b v u"))
             z_codes = keep.tile([P, width], U32, name=f"z_codes{v0}", align_bytes=64)
             z_plane = keep.tile([P, width], U8, name=f"z_plane{v0}", align_bytes=64)
             nc.vector.quantize_mx(
@@ -161,7 +181,7 @@ def tile_picked_wlapl_none_l_kernel(
                 scales=z_plane[:],
                 in_=z_bf[:].rearrange("p v j -> p (v j)"),
             )
-            acc = psum.tile([P, BANK], F32, name="acc", tag="acc")
+            acc = banks[SUM_BANKS[v0 // P]]
             nc.tensor.matmul_mx(
                 out=acc[:, 0:width],
                 lhsT=w_codes[4][:].bitcast(FP8X4),
@@ -173,12 +193,15 @@ def tile_picked_wlapl_none_l_kernel(
             )
             result = keep.tile([P, width], F32, name=f"result{v0}")
             nc.scalar.copy(out=result[:], in_=acc[:, 0:width])
-            nc.sync.dma_start(out=out[:, v0 : v0 + width], in_=result[:])
+            queue = nc.scalar if v0 + width == T else nc.sync
+            queue.dma_start(out=out[:, v0 : v0 + width], in_=result[:])
 
         v0 = 0
+        turn = 0
         for width in CHUNKS:
-            banks = [psum.tile([P, BANK], F32, name="z_t", tag="z_t") for b in range(width // P)]
             for t in range(4):
-                gather_and_sum(v0, width, t, banks)
-            finish(v0, width, banks)
+                gather_and_sum(v0, width, t)
+            for f0 in range(v0, v0 + width, 2 * P):
+                finish(f0, min(2 * P, width), turn)
+                turn = turn + 1
             v0 = v0 + width

@@ -19,12 +19,21 @@ COPY = mybir.ActivationFunctionType.Copy
 P = 128
 PACK = 4
 BANK = 512
+PARTS = H // P
+LISTS = 2
 LIST_ROWS = 16
-RING = 1024
+QUADRANT = 32
+W2 = PARTS
+EARLY_WEIGHTS = 3
+LAST_BLOCK = T // P - 1
+LAST_PART = PARTS - 1
+
 CHUNKS = (512, 256, 128, 128)
-SUM_BANKS = (0, 1, 2, 3, 4, 5, 1, 3)
-BACK_BANKS = (6, 7)
-LAST_BANK = 5
+RING = 2048
+
+SUM_BANKS = (0, 1, 2, 3, 6, 7, 1, 3)
+LAST_BANK = 7
+WORK_BANKS = (4, 5)
 
 
 def tile_picked_wlapl_none_l_kernel(
@@ -36,108 +45,108 @@ def tile_picked_wlapl_none_l_kernel(
         psum = ctx.enter_context(tc.psum_pool(name="psum", bufs=1))
         banks = [psum.tile([P, BANK], F32, name=f"bank{b}") for b in range(8)]
 
-        x_plane = keep.tile([P, T], U8, name="x_plane", align_bytes=64)
-        nc.gpsimd.memset(x_plane[:].bitcast(I32), 0)
-
-        gate_cols = keep.tile([P, 2, 8], F32, name="gate_cols")
-        nc.scalar.dma_start(out=gate_cols[:], in_=gate[:, 0, :].rearrange("d (p j) -> p d j", j=8))
-        for q in range(4):
-            nc.scalar.dma_start(
-                out=x_plane[32 * q : 32 * q + 4, :].bitcast(I32),
-                in_=x_scales[0, 4 * q : 4 * q + 4, :].bitcast(I32),
-            )
+        x_scale_rows = keep.tile([P, T], U8, name="x_scale_rows", align_bytes=64)
+        nc.gpsimd.memset(x_scale_rows[:].bitcast(I32), 0)
 
         w1_rows = w1.rearrange("(p j) c -> p j c", j=PACK)
-        w1_first = keep.tile([P, PACK, P], F32, name="w1_first")
-        w1_second = keep.tile([P, PACK, P], F32, name="w1_second")
-        w1_rest = keep.tile([P, PACK, 2 * P], F32, name="w1_rest")
-        w2_raw = keep.tile([P, PACK, P], F32, name="w2_raw")
+        stage = [keep.tile([P, PACK, P], F32, name=f"stage{s}") for s in range(2)]
+        gate_stage = keep.tile([P, LISTS, 2 * PACK], F32, name="gate_stage")
+        gate_cols = gate_stage[:, :, 0:PACK]
+        w_raw = [stage[w % 2][:] for w in range(W2 + 1)]
+        w_source = [w1_rows[:, :, t * P : (t + 1) * P] for t in range(PARTS)]
+        w_source.append(w2.rearrange("(p j) c -> p j c", j=PACK))
+
         x_codes = keep.tile([P, T], U32, name="x_codes", align_bytes=64)
-        lists = [keep.tile([P, T // LIST_ROWS], U16, name=f"list{d}") for d in range(2)]
-        nc.sync.dma_start(out=w1_first[:], in_=w1_rows[:, :, 0:P])
-        nc.sync.dma_start(out=x_codes[:].bitcast(I32), in_=x_words[0].rearrange("p n t -> p (n t)").bitcast(I32))
-        nc.sync.dma_start(out=w1_second[:], in_=w1_rows[:, :, P : 2 * P])
+        lists = [keep.tile([P, T // LIST_ROWS], U16, name=f"list{d}") for d in range(LISTS)]
+        nc.sync.dma_start(out=w_raw[0], in_=w_source[0])
+        nc.sync.dma_start(out=gate_cols, in_=gate[:, 0, 0:BANK].rearrange("d (p j) -> p d j", j=PACK))
         nc.sync.dma_start(lists[0][:], pos1)
         nc.sync.dma_start(lists[1][:], pos2)
-        nc.sync.dma_start(out=w1_rest[:], in_=w1_rows[:, :, 2 * P : 4 * P])
-        nc.sync.dma_start(out=w2_raw[:], in_=w2.rearrange("(p j) c -> p j c", j=PACK))
-        w_raw = [w1_first[:], w1_second[:], w1_rest[:, :, 0:P], w1_rest[:, :, P : 2 * P], w2_raw[:]]
+        nc.sync.dma_start(out=x_codes[:].bitcast(I32), in_=x_words[0].rearrange("p n j -> p (n j)").bitcast(I32))
+        nc.sync.dma_start(out=w_raw[1], in_=w_source[1])
+        for q in range(P // QUADRANT):
+            nc.sync.dma_start(
+                out=x_scale_rows[QUADRANT * q : QUADRANT * q + 4, :].bitcast(I32),
+                in_=x_scales[0, 4 * q : 4 * q + 4, :].bitcast(I32),
+            )
 
         ident = keep.tile([P, P], F32, name="ident")
         make_identity(nc, ident[:])
 
-        neg_gate = [keep.tile([P, T], F32, name=f"neg_gate{d}") for d in range(2)]
+        neg_gate = [keep.tile([P, T], F32, name=f"neg_gate{d}") for d in range(LISTS)]
+        w_codes = [keep.tile([P, P], U32, name=f"w_codes{w}", align_bytes=64) for w in range(W2 + 1)]
+        w_scales = [keep.tile([P, P], U8, name=f"w_scales{w}", align_bytes=64) for w in range(W2 + 1)]
+        first_terms = [keep.tile([P, BANK], F32, name=f"first_term{d}", align_bytes=64) for d in range(LISTS)]
+        h = [keep.tile([P, T], F32, name=f"h{t}") for t in range(PARTS)]
+        ring = keep.tile([P, RING], F32, name="ring")
 
-        def spread_gate(d):
-            for half in range(2):
-                bank = banks[4 + 2 * d + half][:].rearrange("q (j n) -> q j n", j=4)
-                for j in range(4):
-                    col = 4 * half + j
-                    nc.tensor.transpose(
-                        bank[:, j, :], gate_cols[:, d, col : col + 1].to_broadcast([P, P]), ident[:]
-                    )
+        def spread_first_gates():
+            for d in range(LISTS):
+                bank = banks[WORK_BANKS[d]][:].rearrange("r (j p) -> r j p", j=PACK)
+                for j in range(PACK):
+                    nc.tensor.transpose(bank[:, j, :], gate_cols[:, d, j : j + 1].to_broadcast([P, P]), ident[:])
                 nc.scalar.activation(
-                    out=neg_gate[d][:].rearrange("q (n j) -> q n j", j=8)[:, :, 4 * half : 4 * half + 4],
-                    in_=bank.rearrange("q j n -> q n j"),
+                    out=neg_gate[d][:, 0:BANK].rearrange("r (p j) -> r p j", j=PACK),
+                    in_=bank.rearrange("r j p -> r p j"),
                     func=COPY,
                     scale=-1.0,
                 )
 
-        w_codes = [keep.tile([P, P], U32, name=f"w_codes{t}", align_bytes=64) for t in range(5)]
-        w_plane = [keep.tile([P, P], U8, name=f"w_plane{t}", align_bytes=64) for t in range(5)]
+        def load_other_gates():
+            for d in range(LISTS):
+                staged = stage[1 - d][:].rearrange("p j c -> p (j c)")
+                nc.sync.dma_start(out=staged, in_=gate[d, :, BANK:T])
+                nc.scalar.activation(out=neg_gate[d][:, BANK:T], in_=staged, func=COPY, scale=-1.0)
 
-        def quantise_weight(t):
-            grouped = keep.tile([P, P, PACK], BF16, name=f"w_grouped{t}", align_bytes=64)
-            if t in (2, 3, 4):
-                nc.scalar.copy(out=grouped[:], in_=w_raw[t].rearrange("p j c -> p c j"))
-            else:
+        def quantise_weight(w):
+            if w < EARLY_WEIGHTS:
+                grouped = keep.tile([P, P, PACK], BF16, name=f"w_grouped{w}", align_bytes=64)[:]
                 nc.vector.tensor_copy(
-                    out=grouped[:].rearrange("p (c i) j -> p c j i", i=4),
-                    in_=w_raw[t].rearrange("p j (c i) -> p c j i", i=4),
+                    out=grouped.rearrange("p (c n) j -> p c j n", n=4),
+                    in_=w_raw[w].rearrange("p j (c n) -> p c j n", n=4),
                 )
+            else:
+                spare = first_terms[w - EARLY_WEIGHTS][:, 0 : P * PACK // 2].bitcast(BF16)
+                grouped = spare.rearrange("p (c j) -> p c j", j=PACK)
+                nc.scalar.copy(out=grouped, in_=w_raw[w].rearrange("p j c -> p c j"))
             nc.vector.quantize_mx(
-                out=w_codes[t][:].bitcast(FP8X4),
-                scales=w_plane[t][:],
-                in_=grouped[:].rearrange("p c j -> p (c j)"),
+                out=w_codes[w][:].bitcast(FP8X4),
+                scales=w_scales[w][:],
+                in_=grouped.rearrange("p c j -> p (c j)"),
             )
 
-        h = [keep.tile([P, T], F32, name=f"h{t}") for t in range(4)]
-
         def project(t):
-            for c in range(2):
-                cols = slice(c * BANK, (c + 1) * BANK)
-                acc = banks[4 + 2 * (t % 2) + c]
+            for half in range(T // BANK):
+                cols = slice(half * BANK, (half + 1) * BANK)
+                acc = banks[WORK_BANKS[half]]
                 nc.tensor.matmul_mx(
                     out=acc[:],
                     lhsT=w_codes[t][:].bitcast(FP8X4),
-                    lhsT_scale=w_plane[t][:],
+                    lhsT_scale=w_scales[t][:],
                     rhs=x_codes[:, cols].bitcast(FP8X4),
-                    rhs_scale=x_plane[:, cols],
+                    rhs_scale=x_scale_rows[:, cols],
                     start=True,
                     stop=True,
                 )
-                if t == 0 and c == 0:
-                    nc.vector.tensor_copy(out=h[t][:, cols], in_=acc[:])
-                else:
-                    nc.scalar.copy(out=h[t][:, cols], in_=acc[:])
-
-        spread_gate(0)
-        spread_gate(1)
-        for t in range(4):
-            quantise_weight(t)
-            project(t)
-        quantise_weight(4)
-
-        ring = keep.tile([P, RING], F32, name="ring")
+                nc.scalar.copy(out=h[t][:, cols], in_=acc[:])
 
         def sum_bank(block, t):
-            return banks[LAST_BANK if (block, t) == (T // P - 1, 3) else SUM_BANKS[block]]
+            return banks[LAST_BANK if (block, t) == (LAST_BLOCK, LAST_PART) else SUM_BANKS[block]]
+
+        def add_turned(block, t, source, start, stop):
+            nc.tensor.matmul(
+                sum_bank(block, t)[:, t * P : (t + 1) * P], source, ident[:], start=start, stop=stop, is_transpose=True
+            )
+
+        def own_rows(block, t):
+            opens = t == 0 or (block, t) == (LAST_BLOCK, LAST_PART)
+            add_turned(block, t, h[t][:, block * P : (block + 1) * P], opens, False)
 
         def gather_and_sum(v0, width, t):
             terms = []
-            for d in range(2):
-                at = (8 * v0 + (2 * t + d) * width) % RING
-                term = ring[:, at : at + width]
+            for d in range(LISTS):
+                at = (PARTS * LISTS * v0 + (LISTS * t + d) * width) % RING
+                term = first_terms[d][:] if (v0, t) == (0, 0) else ring[:, at : at + width]
                 nc.vector.tensor_tensor(
                     term,
                     h[t][:].indirect(lists[d][:, v0 // LIST_ROWS : (v0 + width) // LIST_ROWS]),
@@ -145,63 +154,86 @@ def tile_picked_wlapl_none_l_kernel(
                     MULT,
                 )
                 terms.append(term)
-            sources = [h[t][:, v0 : v0 + width], terms[0], terms[1]]
-            for s, source in enumerate(sources):
+            for d in range(LISTS):
                 for b in range(width // P):
-                    nc.tensor.matmul(
-                        sum_bank(v0 // P + b, t)[:, t * P : (t + 1) * P],
-                        source[:, b * P : (b + 1) * P],
-                        ident[:],
-                        start=(s == 0),
-                        stop=(s == 2),
-                        is_transpose=True,
-                    )
+                    block = v0 // P + b
+                    closes = d == LISTS - 1 and (t == LAST_PART or (block, t) == (LAST_BLOCK, LAST_PART - 1))
+                    add_turned(block, t, terms[d][:, b * P : (b + 1) * P], False, closes)
 
-        def finish(v0, width, turn):
+        def finish(chunk, v0, width):
             blocks = width // P
-            z_bf = keep.tile([P, width, PACK], BF16, name=f"z_bf{v0}", align_bytes=64)
+            z_bf = keep.tile([P, width, PACK], BF16, name=f"z_bf{chunk}", align_bytes=64)
             z_words = z_bf[:].rearrange("p v j -> p (v j)").bitcast(F32).rearrange("p (b v u) -> p b v u", u=2, v=P)
-            back = banks[BACK_BANKS[turn % 2]][:].rearrange("p (b u v) -> p b u v", u=2, v=P)
-            for b in range(blocks):
-                rows = keep.tile([P, 2, P, 2], BF16, name=f"z_rows{v0}_{b}")
-                block = v0 // P + b
-                for t0, t1 in ((0, 3), (3, 4)) if block == T // P - 1 else ((0, 4),):
-                    nc.scalar.copy(
-                        out=rows[:, :, 32 * t0 : 32 * t1, :],
-                        in_=sum_bank(block, t0)[:, t0 * P : t1 * P].rearrange("v (p u e) -> v u p e", u=2, e=2),
-                    )
-                words = rows[:].rearrange("v u p e -> v (u p e)").bitcast(F32)
-                for u in range(2):
-                    nc.tensor.transpose(back[:, b, u, :], words[:, u * P : (u + 1) * P], ident[:])
-            nc.scalar.copy(out=z_words, in_=back[:, 0:blocks, :, :].rearrange("p b u v -> p b v u"))
-            z_codes = keep.tile([P, width], U32, name=f"z_codes{v0}", align_bytes=64)
-            z_plane = keep.tile([P, width], U8, name=f"z_plane{v0}", align_bytes=64)
+            for b0 in range(0, blocks, 2):
+                pair = min(2, blocks - b0)
+                back = banks[WORK_BANKS[(chunk + b0 // 2) % 2]][:].rearrange("p (b u v) -> p b u v", u=2, v=P)
+                for b in range(pair):
+                    block = v0 // P + b0 + b
+                    rows = keep.tile([P, 2, P, 2], BF16, name=f"z_rows{block}")
+                    spans = ((0, LAST_PART), (LAST_PART, PARTS)) if block == LAST_BLOCK else ((0, PARTS),)
+                    for t0, t1 in spans:
+                        nc.scalar.copy(
+                            out=rows[:, :, t0 * P // PACK : t1 * P // PACK, :],
+                            in_=sum_bank(block, t0)[:, t0 * P : t1 * P].rearrange("v (p u e) -> v u p e", u=2, e=2),
+                        )
+                    words = rows[:].rearrange("v u p e -> v (u p e)").bitcast(F32)
+                    for u in range(2):
+                        nc.tensor.transpose(back[:, b, u, :], words[:, u * P : (u + 1) * P], ident[:])
+                nc.scalar.copy(
+                    out=z_words[:, b0 : b0 + pair, :, :], in_=back[:, 0:pair, :, :].rearrange("p b u v -> p b v u")
+                )
+            z_codes = keep.tile([P, width], U32, name=f"z_codes{chunk}", align_bytes=64)
+            z_scales = keep.tile([P, width], U8, name=f"z_scales{chunk}", align_bytes=64)
             nc.vector.quantize_mx(
                 out=z_codes[:].bitcast(FP8X4),
-                scales=z_plane[:],
+                scales=z_scales[:],
                 in_=z_bf[:].rearrange("p v j -> p (v j)"),
             )
             acc = banks[SUM_BANKS[v0 // P]]
             nc.tensor.matmul_mx(
                 out=acc[:, 0:width],
-                lhsT=w_codes[4][:].bitcast(FP8X4),
-                lhsT_scale=w_plane[4][:],
+                lhsT=w_codes[W2][:].bitcast(FP8X4),
+                lhsT_scale=w_scales[W2][:],
                 rhs=z_codes[:].bitcast(FP8X4),
-                rhs_scale=z_plane[:],
+                rhs_scale=z_scales[:],
                 start=True,
                 stop=True,
             )
-            result = keep.tile([P, width], F32, name=f"result{v0}")
+            result = keep.tile([P, width], F32, name=f"result{chunk}")
             nc.scalar.copy(out=result[:], in_=acc[:, 0:width])
             queue = nc.scalar if v0 + width == T else nc.sync
             queue.dma_start(out=out[:, v0 : v0 + width], in_=result[:])
 
-        v0 = 0
-        turn = 0
-        for width in CHUNKS:
-            for t in range(4):
-                gather_and_sum(v0, width, t)
-            for f0 in range(v0, v0 + width, 2 * P):
-                finish(f0, min(2 * P, width), turn)
-                turn = turn + 1
-            v0 = v0 + width
+        spread_first_gates()
+        for t in range(EARLY_WEIGHTS):
+            quantise_weight(t)
+            nc.sync.dma_start(out=w_raw[t + 2], in_=w_source[t + 2])
+            project(t)
+
+        starts = [sum(CHUNKS[:chunk]) for chunk in range(len(CHUNKS))]
+        blocks_of = [range(v0 // P, (v0 + width) // P) for v0, width in zip(starts, CHUNKS)]
+
+        for t in range(PARTS):
+            for block in blocks_of[0]:
+                own_rows(block, t)
+            gather_and_sum(starts[0], CHUNKS[0], t)
+            for block in blocks_of[1]:
+                own_rows(block, t)
+            if t == 0:
+                quantise_weight(LAST_PART)
+                project(LAST_PART)
+                quantise_weight(W2)
+                load_other_gates()
+        finish(0, starts[0], CHUNKS[0])
+
+        for t in range(PARTS):
+            own_rows(LAST_BLOCK - 1, t)
+        for t in range(LAST_PART):
+            own_rows(LAST_BLOCK, t)
+
+        for chunk in range(1, len(CHUNKS)):
+            for t in range(PARTS):
+                gather_and_sum(starts[chunk], CHUNKS[chunk], t)
+            finish(chunk, starts[chunk], CHUNKS[chunk])
+            if chunk == 1:
+                own_rows(LAST_BLOCK, LAST_PART)

@@ -1,7 +1,6 @@
 from contextlib import ExitStack
 
 import concourse.mybir as mybir
-from concourse.masks import make_identity
 
 K, T, H, N = 512, 1024, 512, 128
 FLOPS = 2 * K * H * T + 2 * H * N * T
@@ -23,17 +22,21 @@ PARTS = H // P
 LISTS = 2
 LIST_ROWS = 16
 QUADRANT = 32
+QUARTER = T // 4
 W2 = PARTS
-EARLY_WEIGHTS = 3
-LAST_BLOCK = T // P - 1
-LAST_PART = PARTS - 1
-
-CHUNKS = (512, 256, 128, 128)
+BLOCKS = T // P
+HALVES = T // BANK
+GATE_RUN = T // P
 RING = 2048
-
-SUM_BANKS = (0, 1, 2, 3, 6, 7, 1, 3)
-LAST_BANK = 7
-WORK_BANKS = (4, 5)
+LATE_CHUNKS = (256, 128, 128)
+WORK_BANKS = (6, 7)
+STAGE_OF = (0, 0, 1, 0, 1)
+WEIGHT_BEFORE = {1: 1, 3: 2, 5: 3, 7: 4}
+Z_BEFORE = {}
+EARLY_ORDER = ((0, 0), (0, 1), (1, 0), (1, 1))
+SLOTS = {512: 4, 256: 4, 128: 6}
+Z_AFTER = {14: 0, 23: 1, 26: 2}
+PROBES = (None, None)
 
 
 def tile_picked_wlapl_none_l_kernel(
@@ -45,151 +48,233 @@ def tile_picked_wlapl_none_l_kernel(
         psum = ctx.enter_context(tc.psum_pool(name="psum", bufs=1))
         banks = [psum.tile([P, BANK], F32, name=f"bank{b}") for b in range(8)]
 
-        x_scale_rows = keep.tile([P, T], U8, name="x_scale_rows", align_bytes=64)
-        nc.gpsimd.memset(x_scale_rows[:].bitcast(I32), 0)
+        def probe(label, ap):
+            if label in PROBES:
+                n = PROBES.index(label)
+                assert n < 0
+
+        x_planes = keep.tile([P, QUARTER], U8, name="x_planes", align_bytes=64)
+        nc.gpsimd.memset(x_planes[:].bitcast(I32), 0)
 
         w1_rows = w1.rearrange("(p j) c -> p j c", j=PACK)
-        stage = [keep.tile([P, PACK, P], F32, name=f"stage{s}") for s in range(2)]
-        gate_stage = keep.tile([P, LISTS, 2 * PACK], F32, name="gate_stage")
-        gate_cols = gate_stage[:, :, 0:PACK]
-        w_raw = [stage[w % 2][:] for w in range(W2 + 1)]
         w_source = [w1_rows[:, :, t * P : (t + 1) * P] for t in range(PARTS)]
         w_source.append(w2.rearrange("(p j) c -> p j c", j=PACK))
-
-        x_codes = keep.tile([P, T], U32, name="x_codes", align_bytes=64)
+        staging = keep.tile([P, 3 * BANK + 16], F32, name="staging", align_bytes=64)
+        stage = [staging[:, s * BANK : (s + 1) * BANK].rearrange("p (j c) -> p j c", j=PACK) for s in range(2)]
+        gate_cols = staging[:, 2 * BANK - GATE_RUN : 2 * BANK + 32].rearrange("p (d j) -> p d j", d=LISTS)[:, :, 0:GATE_RUN]
+        ring = keep.tile([P, RING], F32, name="ring", align_bytes=64)
+        x_codes = [keep.tile([P, BANK], U32, name=f"x_codes{f}", align_bytes=64) for f in range(HALVES)]
         lists = [keep.tile([P, T // LIST_ROWS], U16, name=f"list{d}") for d in range(LISTS)]
-        nc.sync.dma_start(out=w_raw[0], in_=w_source[0])
-        nc.sync.dma_start(out=gate_cols, in_=gate[:, 0, 0:BANK].rearrange("d (p j) -> p d j", j=PACK))
-        nc.sync.dma_start(lists[0][:], pos1)
-        nc.sync.dma_start(lists[1][:], pos2)
-        nc.sync.dma_start(out=x_codes[:].bitcast(I32), in_=x_words[0].rearrange("p n j -> p (n j)").bitcast(I32))
-        nc.sync.dma_start(out=w_raw[1], in_=w_source[1])
+
+        nc.sync.dma_start(out=gate_cols, in_=gate[:, 0, :].rearrange("d (p j) -> p d j", j=GATE_RUN))
+        nc.sync.dma_start(out=stage[0], in_=w_source[0])
         for q in range(P // QUADRANT):
             nc.sync.dma_start(
-                out=x_scale_rows[QUADRANT * q : QUADRANT * q + 4, :].bitcast(I32),
-                in_=x_scales[0, 4 * q : 4 * q + 4, :].bitcast(I32),
+                out=x_planes[QUADRANT * q : QUADRANT * q + 16, :].bitcast(I32),
+                in_=x_scales[0, 4 * q : 4 * q + 4, :].bitcast(I32).rearrange("r (a c) -> a r c", a=4),
             )
+        x_source = x_words[0].rearrange("p n j -> p (n j)").bitcast(I32)
+        for half in range(HALVES):
+            nc.sync.dma_start(out=x_codes[half][:].bitcast(I32), in_=x_source[:, half * BANK : (half + 1) * BANK])
+        nc.sync.dma_start(lists[0][:], pos1)
+        nc.sync.dma_start(lists[1][:], pos2)
+        probe("scales", x_planes[:, 0:1])
+        probe("x", x_codes[1][:, 0:1].bitcast(U8)[:, 0:1])
+        probe("gate", gate_cols[:, 0, 0:1])
 
         ident = keep.tile([P, P], F32, name="ident")
-        make_identity(nc, ident[:])
+        zeros = keep.tile([P, P], F32, name="zeros", tag="first", align_bytes=64)[:]
+        nc.gpsimd.memset(zeros, 0.0)
+        nc.gpsimd.affine_select(
+            out=ident[:],
+            in_=zeros,
+            compare_op=mybir.AluOpType.not_equal,
+            fill=1.0,
+            base=0,
+            pattern=[[-1, P]],
+            channel_multiplier=1,
+        )
 
+        first_grouped = keep.tile([P, P * PACK], BF16, name="first_grouped", tag="first", align_bytes=64)
         neg_gate = [keep.tile([P, T], F32, name=f"neg_gate{d}") for d in range(LISTS)]
         w_codes = [keep.tile([P, P], U32, name=f"w_codes{w}", align_bytes=64) for w in range(W2 + 1)]
         w_scales = [keep.tile([P, P], U8, name=f"w_scales{w}", align_bytes=64) for w in range(W2 + 1)]
-        first_terms = [keep.tile([P, BANK], F32, name=f"first_term{d}", align_bytes=64) for d in range(LISTS)]
         h = [keep.tile([P, T], F32, name=f"h{t}") for t in range(PARTS)]
-        ring = keep.tile([P, RING], F32, name="ring")
+        rows = keep.tile([P, BLOCKS, 2, P, 2], BF16, name="rows")
+        row_words = rows[:].rearrange("v b u p e -> v (b u p e)").bitcast(F32)
+        widths = (BANK,) + LATE_CHUNKS
+        z_bf = [keep.tile([P, width * PACK], BF16, name=f"z_bf{c}", align_bytes=64) for c, width in enumerate(widths)]
+        pending = {}
+        state = {"at": 0, "count": 0}
 
-        def spread_first_gates():
-            for d in range(LISTS):
-                bank = banks[WORK_BANKS[d]][:].rearrange("r (j p) -> r j p", j=PACK)
-                for j in range(PACK):
-                    nc.tensor.transpose(bank[:, j, :], gate_cols[:, d, j : j + 1].to_broadcast([P, P]), ident[:])
-                nc.scalar.activation(
-                    out=neg_gate[d][:, 0:BANK].rearrange("r (p j) -> r p j", j=PACK),
-                    in_=bank.rearrange("r j p -> r p j"),
-                    func=COPY,
-                    scale=-1.0,
-                )
+        def spread_gate(d, f, b):
+            bank = banks[b][:].rearrange("r (j p) -> r j p", j=PACK)
+            for j in range(PACK):
+                column = gate_cols[:, d, PACK * f + j : PACK * f + j + 1]
+                nc.tensor.transpose(bank[:, j, :], column.to_broadcast([P, P]), ident[:])
 
-        def load_other_gates():
-            for d in range(LISTS):
-                staged = stage[1 - d][:].rearrange("p j c -> p (j c)")
-                nc.sync.dma_start(out=staged, in_=gate[d, :, BANK:T])
-                nc.scalar.activation(out=neg_gate[d][:, BANK:T], in_=staged, func=COPY, scale=-1.0)
+        def fetch_gate(d, f, b, engine):
+            bank = banks[b][:].rearrange("r (j p) -> r j p", j=PACK)
+            target = neg_gate[d][:].rearrange("r (p f j) -> r p f j", f=2, j=PACK)[:, :, f, :]
+            if engine == "scalar":
+                nc.scalar.activation(out=target, in_=bank.rearrange("r j p -> r p j"), func=COPY, scale=-1.0)
+            else:
+                nc.vector.tensor_scalar_mul(target, bank.rearrange("r j p -> r p j"), -1.0)
+            probe(f"g{d}{f}", neg_gate[d][:, 4 * f : 4 * f + 1])
 
-        def quantise_weight(w):
-            if w < EARLY_WEIGHTS:
-                grouped = keep.tile([P, P, PACK], BF16, name=f"w_grouped{w}", align_bytes=64)[:]
+        def load_weight(w):
+            nc.sync.dma_start(out=stage[STAGE_OF[w]], in_=w_source[w])
+
+        def quantise_weight(w, target):
+            source = stage[STAGE_OF[w]]
+            if w == 0:
                 nc.vector.tensor_copy(
-                    out=grouped.rearrange("p (c n) j -> p c j n", n=4),
-                    in_=w_raw[w].rearrange("p j (c n) -> p c j n", n=4),
+                    out=target.rearrange("p (c n j) -> p c j n", n=4, j=PACK),
+                    in_=source.rearrange("p j (c n) -> p c j n", n=4),
                 )
             else:
-                spare = first_terms[w - EARLY_WEIGHTS][:, 0 : P * PACK // 2].bitcast(BF16)
-                grouped = spare.rearrange("p (c j) -> p c j", j=PACK)
-                nc.scalar.copy(out=grouped, in_=w_raw[w].rearrange("p j c -> p c j"))
-            nc.vector.quantize_mx(
-                out=w_codes[w][:].bitcast(FP8X4),
-                scales=w_scales[w][:],
-                in_=grouped.rearrange("p c j -> p (c j)"),
+                nc.scalar.copy(out=target.rearrange("p (c j) -> p c j", j=PACK), in_=source.rearrange("p j c -> p c j"))
+            nc.vector.quantize_mx(out=w_codes[w][:].bitcast(FP8X4), scales=w_scales[w][:], in_=target)
+            probe(f"q{w}", w_scales[w][:, 0:1])
+
+        def project_quarter(t, a, acc):
+            nc.tensor.matmul_mx(
+                out=acc,
+                lhsT=w_codes[t][:].bitcast(FP8X4),
+                lhsT_scale=w_scales[t][:],
+                rhs=x_codes[a // 2][:, a % 2 * QUARTER : (a % 2 + 1) * QUARTER].bitcast(FP8X4),
+                rhs_scale=x_planes[4 * a : P, :],
+                start=True,
+                stop=True,
             )
+
+        def project_first():
+            for a, b in enumerate((6, 7, 4, 5)):
+                acc = banks[b][:, 0:QUARTER]
+                project_quarter(0, a, acc)
+                target = h[0][:, a * QUARTER : (a + 1) * QUARTER]
+                if a % 2 == 0:
+                    nc.vector.tensor_copy(out=target, in_=acc)
+                else:
+                    nc.scalar.copy(out=target, in_=acc)
+            probe("h0", h[0][:, T - 1 : T])
 
         def project(t):
-            for half in range(T // BANK):
-                cols = slice(half * BANK, (half + 1) * BANK)
+            for half in range(HALVES):
                 acc = banks[WORK_BANKS[half]]
-                nc.tensor.matmul_mx(
-                    out=acc[:],
-                    lhsT=w_codes[t][:].bitcast(FP8X4),
-                    lhsT_scale=w_scales[t][:],
-                    rhs=x_codes[:, cols].bitcast(FP8X4),
-                    rhs_scale=x_scale_rows[:, cols],
-                    start=True,
-                    stop=True,
-                )
-                nc.scalar.copy(out=h[t][:, cols], in_=acc[:])
+                for a in range(2):
+                    project_quarter(t, 2 * half + a, acc[:, a * QUARTER : (a + 1) * QUARTER])
+                nc.scalar.copy(out=h[t][:, half * BANK : (half + 1) * BANK], in_=acc[:])
+            probe(f"h{t}", h[t][:, T - 1 : T])
 
-        def sum_bank(block, t):
-            return banks[LAST_BANK if (block, t) == (LAST_BLOCK, LAST_PART) else SUM_BANKS[block]]
-
-        def add_turned(block, t, source, start, stop):
+        def add_turned(place, source, start, stop):
+            b, slot = place
             nc.tensor.matmul(
-                sum_bank(block, t)[:, t * P : (t + 1) * P], source, ident[:], start=start, stop=stop, is_transpose=True
+                banks[b][:, slot * P : (slot + 1) * P], source, ident[:], start=start, stop=stop, is_transpose=True
             )
 
-        def own_rows(block, t):
-            opens = t == 0 or (block, t) == (LAST_BLOCK, LAST_PART)
-            add_turned(block, t, h[t][:, block * P : (block + 1) * P], opens, False)
+        def gather(t, d, v0, width):
+            count = state["count"]
+            if count == 1:
+                term = staging[:, 2 * BANK + 16 :]
+            elif count in Z_AFTER:
+                term = keep.tile([P, width], F32, name=f"term{count}", tag=f"codes{Z_AFTER[count]}", align_bytes=64)[:]
+            else:
+                at = state["at"] if state["at"] + width <= SLOTS[width] * width else 0
+                state.update({"at": at + width})
+                term = ring[:, at : at + width]
+            if count in WEIGHT_BEFORE:
+                w = WEIGHT_BEFORE[count]
+                quantise_weight(w, term[:, 0 : P * PACK // 2].bitcast(BF16))
+                if w == 1:
+                    fetch_gate(1, 1, 6, "scalar")
+                    fetch_gate(1, 0, 7, "scalar")
+                if w + 2 <= W2:
+                    load_weight(w + 2)
+                if w < W2:
+                    project(w)
+            state.update({"count": count + 1})
+            nc.vector.tensor_tensor(
+                term,
+                h[t][:].indirect(lists[d][:, v0 // LIST_ROWS : (v0 + width) // LIST_ROWS]),
+                neg_gate[d][:, v0 : v0 + width],
+                MULT,
+            )
+            probe(f"n{count}", term[:, 0:1])
+            return term
 
-        def gather_and_sum(v0, width, t):
-            terms = []
-            for d in range(LISTS):
-                at = (PARTS * LISTS * v0 + (LISTS * t + d) * width) % RING
-                term = first_terms[d][:] if (v0, t) == (0, 0) else ring[:, at : at + width]
-                nc.vector.tensor_tensor(
-                    term,
-                    h[t][:].indirect(lists[d][:, v0 // LIST_ROWS : (v0 + width) // LIST_ROWS]),
-                    neg_gate[d][:, v0 : v0 + width],
-                    MULT,
-                )
-                terms.append(term)
-            for d in range(LISTS):
-                for b in range(width // P):
-                    block = v0 // P + b
-                    closes = d == LISTS - 1 and (t == LAST_PART or (block, t) == (LAST_BLOCK, LAST_PART - 1))
-                    add_turned(block, t, terms[d][:, b * P : (b + 1) * P], False, closes)
+        def round_out(b, b0, blocks, t0, parts):
+            p0, p1 = t0 * P // PACK, (t0 + parts) * P // PACK
+            nc.scalar.copy(
+                out=rows[:, b0 : b0 + blocks, :, p0:p1, :].rearrange("v b u p e -> v u b p e"),
+                in_=banks[b][:, 0 : blocks * parts * P].rearrange("v (b p u e) -> v u b p e", b=blocks, u=2, e=2),
+            )
 
-        def finish(chunk, v0, width):
+        per = BANK // P
+
+        def wide_own(t, half, b):
+            for i in range(per):
+                block = half * per + i
+                add_turned((b, i), h[t][:, block * P : (block + 1) * P], i == 0, False)
+
+        def wide_terms(t, d, half, b):
+            term = gather(t, d, half * BANK, BANK)
+            for i in range(per):
+                add_turned((b, i), term[:, i * P : (i + 1) * P], False, d == LISTS - 1 and i == per - 1)
+            if d == LISTS - 1:
+                round_out(b, half * per, per, t, 1)
+
+        def late_place(block, t):
+            if (block, t) == (BLOCKS - 1, PARTS - 1):
+                return (3, 0)
+            return ((5, 0, 1, 2)[block - per], t - 1)
+
+        def late_own(block, t):
+            place = late_place(block, t)
+            add_turned(place, h[t][:, block * P : (block + 1) * P], place[1] == 0, False)
+
+        def late_chunk(v0, width):
             blocks = width // P
-            z_bf = keep.tile([P, width, PACK], BF16, name=f"z_bf{chunk}", align_bytes=64)
-            z_words = z_bf[:].rearrange("p v j -> p (v j)").bitcast(F32).rearrange("p (b v u) -> p b v u", u=2, v=P)
-            for b0 in range(0, blocks, 2):
-                pair = min(2, blocks - b0)
-                back = banks[WORK_BANKS[(chunk + b0 // 2) % 2]][:].rearrange("p (b u v) -> p b u v", u=2, v=P)
-                for b in range(pair):
-                    block = v0 // P + b0 + b
-                    rows = keep.tile([P, 2, P, 2], BF16, name=f"z_rows{block}")
-                    spans = ((0, LAST_PART), (LAST_PART, PARTS)) if block == LAST_BLOCK else ((0, PARTS),)
-                    for t0, t1 in spans:
-                        nc.scalar.copy(
-                            out=rows[:, :, t0 * P // PACK : t1 * P // PACK, :],
-                            in_=sum_bank(block, t0)[:, t0 * P : t1 * P].rearrange("v (p u e) -> v u p e", u=2, e=2),
-                        )
-                    words = rows[:].rearrange("v u p e -> v (u p e)").bitcast(F32)
+            b0 = v0 // P
+            last = b0 == BLOCKS - 1
+            for t in range(1, PARTS):
+                closing = t == PARTS - 1 or (last and t == PARTS - 2)
+                for d in range(LISTS):
+                    term = gather(t, d, v0, width)
+                    for i in range(blocks):
+                        add_turned(late_place(b0 + i, t), term[:, i * P : (i + 1) * P], False, closing and d == LISTS - 1)
+                    if state["count"] - 1 in Z_AFTER:
+                        multiply(Z_AFTER[state["count"] - 1])
+                if last and closing:
+                    t0 = 1 if t == PARTS - 2 else t
+                    round_out(late_place(b0, t)[0], b0, 1, t0, t + 1 - t0)
+            if not last:
+                for i in range(blocks):
+                    round_out(late_place(b0 + i, 1)[0], b0 + i, 1, 1, PARTS - 1)
+
+        def finish(chunk, v0, width, b):
+            blocks = width // P
+            b0 = v0 // P
+            z_words = z_bf[chunk][:].bitcast(F32).rearrange("p (b v u) -> p b v u", u=2, v=P)
+            for i0 in range(0, blocks, 2):
+                pair = min(2, blocks - i0)
+                back = banks[WORK_BANKS[(chunk + i0 // 2) % 2]][:].rearrange("p (b u v) -> p b u v", u=2, v=P)
+                for i in range(pair):
                     for u in range(2):
-                        nc.tensor.transpose(back[:, b, u, :], words[:, u * P : (u + 1) * P], ident[:])
+                        at = ((b0 + i0 + i) * 2 + u) * P
+                        nc.tensor.transpose(back[:, i, u, :], row_words[:, at : at + P], ident[:])
                 nc.scalar.copy(
-                    out=z_words[:, b0 : b0 + pair, :, :], in_=back[:, 0:pair, :, :].rearrange("p b u v -> p b v u")
+                    out=z_words[:, i0 : i0 + pair], in_=back[:, 0:pair, :, :].rearrange("p b u v -> p b v u")
                 )
-            z_codes = keep.tile([P, width], U32, name=f"z_codes{chunk}", align_bytes=64)
+            pending.update({chunk: (v0, width, b)})
+
+        def multiply(chunk):
+            v0, width, b = pending[chunk]
+            z_codes = keep.tile([P, width], U32, name=f"z_codes{chunk}", tag=f"codes{chunk}", align_bytes=64)
             z_scales = keep.tile([P, width], U8, name=f"z_scales{chunk}", align_bytes=64)
-            nc.vector.quantize_mx(
-                out=z_codes[:].bitcast(FP8X4),
-                scales=z_scales[:],
-                in_=z_bf[:].rearrange("p v j -> p (v j)"),
-            )
-            acc = banks[SUM_BANKS[v0 // P]]
+            nc.vector.quantize_mx(out=z_codes[:].bitcast(FP8X4), scales=z_scales[:], in_=z_bf[chunk][:])
+            probe(f"z{chunk}", z_scales[:, 0:1])
+            acc = banks[b]
             nc.tensor.matmul_mx(
                 out=acc[:, 0:width],
                 lhsT=w_codes[W2][:].bitcast(FP8X4),
@@ -204,36 +289,32 @@ def tile_picked_wlapl_none_l_kernel(
             queue = nc.scalar if v0 + width == T else nc.sync
             queue.dma_start(out=out[:, v0 : v0 + width], in_=result[:])
 
-        spread_first_gates()
-        for t in range(EARLY_WEIGHTS):
-            quantise_weight(t)
-            nc.sync.dma_start(out=w_raw[t + 2], in_=w_source[t + 2])
-            project(t)
+        spread_gate(0, 0, 2)
+        fetch_gate(0, 0, 2, "scalar")
+        spread_gate(0, 1, 3)
+        fetch_gate(0, 1, 3, "scalar")
+        quantise_weight(0, first_grouped[:])
+        load_weight(1)
+        load_weight(2)
+        project_first()
+        spread_gate(1, 1, 6)
+        spread_gate(1, 0, 7)
 
-        starts = [sum(CHUNKS[:chunk]) for chunk in range(len(CHUNKS))]
-        blocks_of = [range(v0 // P, (v0 + width) // P) for v0, width in zip(starts, CHUNKS)]
-
-        for t in range(PARTS):
-            for block in blocks_of[0]:
-                own_rows(block, t)
-            gather_and_sum(starts[0], CHUNKS[0], t)
-            for block in blocks_of[1]:
-                own_rows(block, t)
-            if t == 0:
-                quantise_weight(LAST_PART)
-                project(LAST_PART)
-                quantise_weight(W2)
-                load_other_gates()
-        finish(0, starts[0], CHUNKS[0])
-
-        for t in range(PARTS):
-            own_rows(LAST_BLOCK - 1, t)
-        for t in range(LAST_PART):
-            own_rows(LAST_BLOCK, t)
-
-        for chunk in range(1, len(CHUNKS)):
-            for t in range(PARTS):
-                gather_and_sum(starts[chunk], CHUNKS[chunk], t)
-            finish(chunk, starts[chunk], CHUNKS[chunk])
-            if chunk == 1:
-                own_rows(LAST_BLOCK, LAST_PART)
+        for half in range(HALVES):
+            wide_own(0, half, half)
+        for d, half in EARLY_ORDER:
+            wide_terms(0, d, half, half)
+        for t in range(1, PARTS):
+            wide_own(t, 0, t + 1)
+            for d in range(LISTS):
+                wide_terms(t, d, 0, t + 1)
+        finish(0, 0, BANK, 4)
+        for t in range(1, PARTS):
+            for block in range(per, BLOCKS):
+                late_own(block, t)
+        v0 = BANK
+        for chunk, width in enumerate(LATE_CHUNKS):
+            late_chunk(v0, width)
+            finish(chunk + 1, v0, width, late_place(v0 // P, 1)[0])
+            v0 = v0 + width
+        multiply(len(LATE_CHUNKS))

@@ -59,9 +59,9 @@ def tile_picked_wlapl_none_l_kernel(
         w1_rows = w1.rearrange("(p j) c -> p j c", j=PACK)
         w_source = [w1_rows[:, :, t * P : (t + 1) * P] for t in range(PARTS)]
         w_source.append(w2.rearrange("(p j) c -> p j c", j=PACK))
-        staging = keep.tile([P, 3 * BANK + 16], F32, name="staging", align_bytes=64)
-        stage = [staging[:, s * BANK : (s + 1) * BANK].rearrange("p (j c) -> p j c", j=PACK) for s in range(2)]
-        gate_cols = staging[:, 2 * BANK - GATE_RUN : 2 * BANK + 32].rearrange("p (d j) -> p d j", d=LISTS)[:, :, 0:GATE_RUN]
+        staging = keep.tile([P, BANK + 32], F32, name="staging", align_bytes=64)
+        gate_cols = staging[:, 8:48].rearrange("p (d j) -> p d j", d=LISTS)[:, :, 0:GATE_RUN]
+        stage = [keep.tile([P, PACK, P], F32, name=f"stage{w}", tag=f"stage{w}", align_bytes=64)[:] for w in range(W2 + 1)]
         ring = keep.tile([P, RING], F32, name="ring", align_bytes=64)
         x_codes = [keep.tile([P, BANK], U32, name=f"x_codes{f}", align_bytes=64) for f in range(HALVES)]
         lists = [keep.tile([P, T // LIST_ROWS], U16, name=f"list{d}") for d in range(LISTS)]
@@ -78,6 +78,8 @@ def tile_picked_wlapl_none_l_kernel(
             nc.sync.dma_start(out=x_codes[half][:].bitcast(I32), in_=x_source[:, half * BANK : (half + 1) * BANK])
         nc.sync.dma_start(lists[0][:], pos1)
         nc.sync.dma_start(lists[1][:], pos2)
+        for w in range(1, W2 + 1):
+            nc.sync.dma_start(out=stage[w], in_=w_source[w])
         probe("scales", x_planes[:, 0:1])
         probe("x", x_codes[1][:, 0:1].bitcast(U8)[:, 0:1])
         probe("gate", gate_cols[:, 0, 0:1])
@@ -122,18 +124,15 @@ def tile_picked_wlapl_none_l_kernel(
                 nc.vector.tensor_scalar_mul(target, bank.rearrange("r j p -> r p j"), -1.0)
             probe(f"g{d}{f}", neg_gate[d][:, 4 * f : 4 * f + 1])
 
-        def load_weight(w):
-            nc.sync.dma_start(out=stage[STAGE_OF[w]], in_=w_source[w])
+        def round_weight(w, target):
+            rounded = target.rearrange("p (c n j) -> p c j n", n=4, j=PACK)
+            source = stage[w].rearrange("p j (c n) -> p c j n", n=4)
+            if w == 0:
+                nc.vector.tensor_copy(out=rounded, in_=source)
+            else:
+                nc.scalar.copy(out=rounded, in_=source)
 
         def quantise_weight(w, target):
-            source = stage[STAGE_OF[w]]
-            if w == 0:
-                nc.vector.tensor_copy(
-                    out=target.rearrange("p (c n j) -> p c j n", n=4, j=PACK),
-                    in_=source.rearrange("p j (c n) -> p c j n", n=4),
-                )
-            else:
-                nc.scalar.copy(out=target.rearrange("p (c j) -> p c j", j=PACK), in_=source.rearrange("p j c -> p c j"))
             nc.vector.quantize_mx(out=w_codes[w][:].bitcast(FP8X4), scales=w_scales[w][:], in_=target)
             probe(f"q{w}", w_scales[w][:, 0:1])
 
@@ -173,26 +172,30 @@ def tile_picked_wlapl_none_l_kernel(
                 banks[b][:, slot * P : (slot + 1) * P], source, ident[:], start=start, stop=stop, is_transpose=True
             )
 
-        def gather(t, d, v0, width):
-            count = state["count"]
+        terms = {}
+
+        def term_of(count, width):
+            if count in terms:
+                return terms[count]
             if count == 1:
-                term = staging[:, 2 * BANK + 16 :]
+                term = staging[:, 32:]
+            elif count in (3, 5, 7):
+                term = keep.tile([P, BANK], F32, name=f"term{count}", tag=f"stage{count // 2}", align_bytes=64)[:]
             elif count in Z_AFTER:
                 term = keep.tile([P, width], F32, name=f"term{count}", tag=f"codes{Z_AFTER[count]}", align_bytes=64)[:]
             else:
                 at = state["at"] if state["at"] + width <= SLOTS[width] * width else 0
                 state.update({"at": at + width})
                 term = ring[:, at : at + width]
-            if count in WEIGHT_BEFORE:
-                w = WEIGHT_BEFORE[count]
-                quantise_weight(w, term[:, 0 : P * PACK // 2].bitcast(BF16))
-                if w == 1:
-                    fetch_gate(1, 1, 6, "scalar")
-                    fetch_gate(1, 0, 7, "scalar")
-                if w + 2 <= W2:
-                    load_weight(w + 2)
-                if w < W2:
-                    project(w)
+            terms.update({count: term})
+            return term
+
+        def grouped(w):
+            return term_of(2 * w - 1, BANK)[:, 0 : P * PACK // 2].bitcast(BF16)
+
+        def gather(t, d, v0, width):
+            count = state["count"]
+            term = term_of(count, width)
             state.update({"count": count + 1})
             nc.vector.tensor_tensor(
                 term,
@@ -293,21 +296,35 @@ def tile_picked_wlapl_none_l_kernel(
         fetch_gate(0, 0, 2, "scalar")
         spread_gate(0, 1, 3)
         fetch_gate(0, 1, 3, "scalar")
+        round_weight(0, first_grouped[:])
         quantise_weight(0, first_grouped[:])
-        load_weight(1)
-        load_weight(2)
         project_first()
         spread_gate(1, 1, 6)
         spread_gate(1, 0, 7)
+        round_weight(1, grouped(1))
+        quantise_weight(1, grouped(1))
+        fetch_gate(1, 1, 6, "scalar")
+        fetch_gate(1, 0, 7, "scalar")
+        project(1)
+        for w in range(2, W2 + 1):
+            round_weight(w, grouped(w))
 
         for half in range(HALVES):
             wide_own(0, half, half)
-        for d, half in EARLY_ORDER:
-            wide_terms(0, d, half, half)
+        wide_terms(0, 0, 0, 0)
+        wide_terms(0, 0, 1, 1)
+        wide_terms(0, 1, 0, 0)
+        quantise_weight(2, grouped(2))
+        project(2)
+        wide_terms(0, 1, 1, 1)
         for t in range(1, PARTS):
             wide_own(t, 0, t + 1)
-            for d in range(LISTS):
-                wide_terms(t, d, 0, t + 1)
+            wide_terms(t, 0, 0, t + 1)
+            if t + 2 <= W2:
+                quantise_weight(t + 2, grouped(t + 2))
+            if t + 2 < W2:
+                project(t + 2)
+            wide_terms(t, 1, 0, t + 1)
         finish(0, 0, BANK, 4)
         for t in range(1, PARTS):
             for block in range(per, BLOCKS):

@@ -35,7 +35,7 @@ WEIGHT_BEFORE = {1: 1, 3: 2, 5: 3, 7: 4}
 Z_BEFORE = {}
 EARLY_ORDER = ((0, 0), (0, 1), (1, 0), (1, 1))
 SLOTS = {512: 4, 256: 4, 128: 6}
-Z_AFTER = {14: 0, 23: 1, 26: 2}
+Z_AFTER = {16: 0, 25: 1, 28: 2}
 PROBES = (None, None)
 
 
@@ -255,20 +255,17 @@ def tile_picked_wlapl_none_l_kernel(
                 for i in range(blocks):
                     round_out(late_place(b0 + i, 1)[0], b0 + i, 1, 1, PARTS - 1)
 
-        def finish(chunk, v0, width, b):
-            blocks = width // P
-            b0 = v0 // P
+        def turn_back(chunk, b0, i0, pair):
             z_words = z_bf[chunk][:].bitcast(F32).rearrange("p (b v u) -> p b v u", u=2, v=P)
-            for i0 in range(0, blocks, 2):
-                pair = min(2, blocks - i0)
-                back = banks[WORK_BANKS[(chunk + i0 // 2) % 2]][:].rearrange("p (b u v) -> p b u v", u=2, v=P)
-                for i in range(pair):
-                    for u in range(2):
-                        at = ((b0 + i0 + i) * 2 + u) * P
-                        nc.tensor.transpose(back[:, i, u, :], row_words[:, at : at + P], ident[:])
-                nc.scalar.copy(
-                    out=z_words[:, i0 : i0 + pair], in_=back[:, 0:pair, :, :].rearrange("p b u v -> p b v u")
-                )
+            back = banks[WORK_BANKS[(chunk + i0 // 2) % 2]][:].rearrange("p (b u v) -> p b u v", u=2, v=P)
+            for i in range(pair):
+                for u in range(2):
+                    at = ((b0 + i0 + i) * 2 + u) * P
+                    nc.tensor.transpose(back[:, i, u, :], row_words[:, at : at + P], ident[:])
+            nc.scalar.copy(out=z_words[:, i0 : i0 + pair], in_=back[:, 0:pair, :, :].rearrange("p b u v -> p b v u"))
+
+        def finish(chunk, v0, width, b):
+            turn_back(chunk, v0 // P, 0, width // P)
             pending.update({chunk: (v0, width, b)})
 
         def multiply(chunk):
@@ -317,7 +314,7 @@ def tile_picked_wlapl_none_l_kernel(
         quantise_weight(2, grouped(2))
         project(2)
         wide_terms(0, 1, 1, 1)
-        for t in range(1, PARTS):
+        for t in range(1, PARTS - 1):
             wide_own(t, 0, t + 1)
             wide_terms(t, 0, 0, t + 1)
             if t + 2 <= W2:
@@ -325,7 +322,17 @@ def tile_picked_wlapl_none_l_kernel(
             if t + 2 < W2:
                 project(t + 2)
             wide_terms(t, 1, 0, t + 1)
-        finish(0, 0, BANK, 4)
+        for pair, b in enumerate((4, 3)):
+            for i in range(2):
+                block = 2 * pair + i
+                add_turned((b, i), h[PARTS - 1][:, block * P : (block + 1) * P], i == 0, False)
+            for d in range(LISTS):
+                term = gather(PARTS - 1, d, pair * QUARTER, QUARTER)
+                for i in range(2):
+                    add_turned((b, i), term[:, i * P : (i + 1) * P], False, d == LISTS - 1 and i == 1)
+            round_out(b, 2 * pair, 2, PARTS - 1, 1)
+            turn_back(0, 0, 2 * pair, 2)
+        pending.update({0: (0, BANK, 4)})
         for t in range(1, PARTS):
             for block in range(per, BLOCKS):
                 late_own(block, t)

@@ -59,14 +59,14 @@ def tile_picked_wlapl_none_l_kernel(
         w1_rows = w1.rearrange("(p j) c -> p j c", j=PACK)
         w_source = [w1_rows[:, :, t * P : (t + 1) * P] for t in range(PARTS)]
         w_source.append(w2.rearrange("(p j) c -> p j c", j=PACK))
-        staging = keep.tile([P, BANK + 32], F32, name="staging", align_bytes=64)
-        gate_cols = staging[:, 8:48].rearrange("p (d j) -> p d j", d=LISTS)[:, :, 0:GATE_RUN]
+        gate_cols = keep.tile([P, 1, GATE_RUN], F32, name="gate_cols")
+        raw_gate = [keep.tile([P, BANK], F32, name=f"raw_gate{f}") for f in range(HALVES)]
         stage = [keep.tile([P, PACK, P], F32, name=f"stage{w}", tag=f"stage{w}", align_bytes=64)[:] for w in range(W2 + 1)]
         ring = keep.tile([P, RING], F32, name="ring", align_bytes=64)
         x_codes = [keep.tile([P, BANK], U32, name=f"x_codes{f}", align_bytes=64) for f in range(HALVES)]
         lists = [keep.tile([P, T // LIST_ROWS], U16, name=f"list{d}") for d in range(LISTS)]
 
-        nc.sync.dma_start(out=gate_cols, in_=gate[:, 0, :].rearrange("d (p j) -> p d j", j=GATE_RUN))
+        nc.sync.dma_start(out=gate_cols[:, 0, :], in_=gate[0, 0, :].rearrange("(p j) -> p j", j=GATE_RUN))
         nc.sync.dma_start(out=stage[0], in_=w_source[0])
         for q in range(P // QUADRANT):
             nc.sync.dma_start(
@@ -80,6 +80,8 @@ def tile_picked_wlapl_none_l_kernel(
         nc.sync.dma_start(lists[1][:], pos2)
         for w in range(1, W2 + 1):
             nc.sync.dma_start(out=stage[w], in_=w_source[w])
+            if w <= HALVES:
+                nc.sync.dma_start(out=raw_gate[w - 1][:], in_=gate[1, :, (w - 1) * BANK : w * BANK])
         probe("scales", x_planes[:, 0:1])
         probe("x", x_codes[1][:, 0:1].bitcast(U8)[:, 0:1])
         probe("gate", gate_cols[:, 0, 0:1])
@@ -98,9 +100,10 @@ def tile_picked_wlapl_none_l_kernel(
         )
 
         first_grouped = keep.tile([P, P * PACK], BF16, name="first_grouped", tag="first", align_bytes=64)
-        neg_gate = [keep.tile([P, T], F32, name=f"neg_gate{d}") for d in range(LISTS)]
-        w_codes = [keep.tile([P, P], U32, name=f"w_codes{w}", align_bytes=64) for w in range(W2 + 1)]
-        w_scales = [keep.tile([P, P], U8, name=f"w_scales{w}", align_bytes=64) for w in range(W2 + 1)]
+        first_gate = keep.tile([P, T], F32, name="neg_gate0")
+        neg_gate = {(0, f): first_gate[:, f * BANK : (f + 1) * BANK] for f in range(HALVES)}
+        w_codes = [keep.tile([P, P], U32, name=f"w_codes{w}", tag=f"wc{w}", align_bytes=64) for w in range(W2 + 1)]
+        w_scales = [keep.tile([P, P], U8, name=f"w_scales{w}", tag=f"ws{w}", align_bytes=64) for w in range(W2 + 1)]
         h = [keep.tile([P, T], F32, name=f"h{t}") for t in range(PARTS)]
         rows = keep.tile([P, BLOCKS, 2, P, 2], BF16, name="rows")
         row_words = rows[:].rearrange("v b u p e -> v (b u p e)").bitcast(F32)
@@ -117,12 +120,17 @@ def tile_picked_wlapl_none_l_kernel(
 
         def fetch_gate(d, f, b, engine):
             bank = banks[b][:].rearrange("r (j p) -> r j p", j=PACK)
-            target = neg_gate[d][:].rearrange("r (p f j) -> r p f j", f=2, j=PACK)[:, :, f, :]
+            target = first_gate[:].rearrange("r (p f j) -> r p f j", f=2, j=PACK)[:, :, f, :]
             if engine == "scalar":
                 nc.scalar.activation(out=target, in_=bank.rearrange("r j p -> r p j"), func=COPY, scale=-1.0)
             else:
                 nc.vector.tensor_scalar_mul(target, bank.rearrange("r j p -> r p j"), -1.0)
-            probe(f"g{d}{f}", neg_gate[d][:, 4 * f : 4 * f + 1])
+            probe(f"g{d}{f}", first_gate[:, 4 * f : 4 * f + 1])
+
+        def negate_gate(f, tag):
+            tile = keep.tile([P, BANK], F32, name=f"neg_gate1{f}", tag=tag, align_bytes=64)
+            neg_gate.update({(1, f): tile[:]})
+            nc.scalar.activation(out=tile[:], in_=raw_gate[f][:], func=COPY, scale=-1.0)
 
         def round_weight(w, target):
             rounded = target.rearrange("p (c n j) -> p c j n", n=4, j=PACK)
@@ -178,9 +186,9 @@ def tile_picked_wlapl_none_l_kernel(
             if count in terms:
                 return terms[count]
             if count == 1:
-                term = staging[:, 32:]
+                term = keep.tile([P, BANK], F32, name="term1", tag="ws0", align_bytes=64)[:]
             elif count in (3, 5, 7):
-                term = keep.tile([P, BANK], F32, name=f"term{count}", tag=f"stage{count // 2}", align_bytes=64)[:]
+                term = keep.tile([P, BANK], F32, name=f"term{count}", tag={3: "wc0", 5: "first", 7: "stage3"}[count], align_bytes=64)[:]
             elif count in Z_AFTER:
                 term = keep.tile([P, width], F32, name=f"term{count}", tag=f"codes{Z_AFTER[count]}", align_bytes=64)[:]
             else:
@@ -200,7 +208,7 @@ def tile_picked_wlapl_none_l_kernel(
             nc.vector.tensor_tensor(
                 term,
                 h[t][:].indirect(lists[d][:, v0 // LIST_ROWS : (v0 + width) // LIST_ROWS]),
-                neg_gate[d][:, v0 : v0 + width],
+                neg_gate[d, v0 // BANK][:, v0 % BANK : v0 % BANK + width],
                 MULT,
             )
             probe(f"n{count}", term[:, 0:1])
@@ -296,14 +304,13 @@ def tile_picked_wlapl_none_l_kernel(
         round_weight(0, first_grouped[:])
         quantise_weight(0, first_grouped[:])
         project_first()
-        spread_gate(1, 1, 6)
-        spread_gate(1, 0, 7)
         round_weight(1, grouped(1))
         quantise_weight(1, grouped(1))
-        fetch_gate(1, 1, 6, "scalar")
-        fetch_gate(1, 0, 7, "scalar")
+        negate_gate(0, "stage1")
         project(1)
-        for w in range(2, W2 + 1):
+        round_weight(2, grouped(2))
+        negate_gate(1, "stage2")
+        for w in range(3, W2 + 1):
             round_weight(w, grouped(w))
 
         for half in range(HALVES):

@@ -54,7 +54,7 @@ def tile_picked_wlapl_none_l_kernel(
                 assert n < 0
 
         x_planes = keep.tile([P, QUARTER], U8, name="x_planes", align_bytes=64)
-        nc.gpsimd.memset(x_planes[:].bitcast(I32), 0)
+        nc.vector.memset(x_planes[:].bitcast(I32), 0)
 
         w1_rows = w1.rearrange("(p j) c -> p j c", j=PACK)
         w_source = [w1_rows[:, :, t * P : (t + 1) * P] for t in range(PARTS)]
@@ -88,7 +88,7 @@ def tile_picked_wlapl_none_l_kernel(
 
         ident = keep.tile([P, P], F32, name="ident")
         zeros = keep.tile([P, P], F32, name="zeros", tag="first", align_bytes=64)[:]
-        nc.gpsimd.memset(zeros, 0.0)
+        nc.vector.memset(zeros, 0.0)
         nc.gpsimd.affine_select(
             out=ident[:],
             in_=zeros,
@@ -329,6 +329,12 @@ def tile_picked_wlapl_none_l_kernel(
             if t + 2 < W2:
                 project(t + 2)
             wide_terms(t, 1, 0, t + 1)
+            for block in range(per, BLOCKS - 1):
+                late_own(block, t)
+        for t in range(1, PARTS - 1):
+            late_own(BLOCKS - 1, t)
+        for block in range(per, BLOCKS - 1):
+            late_own(block, PARTS - 1)
         for pair, b in enumerate((4, 3)):
             for i in range(2):
                 block = 2 * pair + i
@@ -340,9 +346,7 @@ def tile_picked_wlapl_none_l_kernel(
             round_out(b, 2 * pair, 2, PARTS - 1, 1)
             turn_back(0, 0, 2 * pair, 2)
         pending.update({0: (0, BANK, 4)})
-        for t in range(1, PARTS):
-            for block in range(per, BLOCKS):
-                late_own(block, t)
+        late_own(BLOCKS - 1, PARTS - 1)
         v0 = BANK
         for chunk, width in enumerate(LATE_CHUNKS):
             late_chunk(v0, width)

@@ -18,24 +18,16 @@ COPY = mybir.ActivationFunctionType.Copy
 P = 128
 PACK = 4
 BANK = 512
+PAIR = 2 * P
 PARTS = H // P
 LISTS = 2
 LIST_ROWS = 16
 QUADRANT = 32
 QUARTER = T // 4
-W2 = PARTS
-BLOCKS = T // P
-HALVES = T // BANK
 GATE_RUN = T // P
-RING = 2048
-LATE_CHUNKS = (256, 128, 128)
-WORK_BANKS = (6, 7)
-STAGE_OF = (0, 0, 1, 0, 1)
-WEIGHT_BEFORE = {1: 1, 3: 2, 5: 3, 7: 4}
-Z_BEFORE = {}
-EARLY_ORDER = ((0, 0), (0, 1), (1, 0), (1, 1))
-SLOTS = {512: 4, 256: 4, 128: 6}
-Z_AFTER = {16: 0, 25: 1, 28: 2}
+STRIP = 64
+STRIPS = 2
+LAST = T - STRIPS * STRIP
 PROBES = (None, None)
 
 
@@ -50,44 +42,51 @@ def tile_picked_wlapl_none_l_kernel(
 
         def probe(label, ap):
             if label in PROBES:
-                n = PROBES.index(label)
-                assert n < 0
+                clock = keep.tile([P, 1], ap.dtype, name=f"clock{PROBES.index(label)}")
+                nc.gpsimd.tensor_copy(out=clock[:], in_=ap)
 
-        x_planes = keep.tile([P, QUARTER], U8, name="x_planes", align_bytes=64)
-        nc.vector.memset(x_planes[:].bitcast(I32), 0)
+        def sbuf(name, width, dtype, tag=None):
+            return keep.tile([P, width], dtype, name=name, tag=tag or name, align_bytes=64)[:]
+
+        x_planes = sbuf("x_planes", QUARTER, U8)
+        nc.vector.memset(x_planes.bitcast(I32), 0)
 
         w1_rows = w1.rearrange("(p j) c -> p j c", j=PACK)
-        w_source = [w1_rows[:, :, t * P : (t + 1) * P] for t in range(PARTS)]
-        w_source.append(w2.rearrange("(p j) c -> p j c", j=PACK))
-        gate_cols = keep.tile([P, 1, GATE_RUN], F32, name="gate_cols")
-        raw_gate = [keep.tile([P, BANK], F32, name=f"raw_gate{f}") for f in range(HALVES)]
-        stage = [keep.tile([P, PACK, P], F32, name=f"stage{w}", tag=f"stage{w}", align_bytes=64)[:] for w in range(W2 + 1)]
-        ring = keep.tile([P, RING], F32, name="ring", align_bytes=64)
-        x_codes = [keep.tile([P, BANK], U32, name=f"x_codes{f}", align_bytes=64) for f in range(HALVES)]
+        late_terms = sbuf("late_terms", 2 * BANK, F32)
+        stage = [sbuf(f"stage{w}", PACK * P, F32) for w in range(PARTS)] + [late_terms[:, PAIR : PAIR + BANK]]
+        stage = [place.rearrange("p (j c) -> p j c", j=PACK) for place in stage]
+        gate_cols = sbuf("gate_cols", GATE_RUN, F32)
+        raw_gate = [sbuf(f"raw_gate{f}", BANK, F32) for f in range(2)]
+        x_codes = [sbuf("x_codes0", BANK, U32), sbuf("x_codes1", QUARTER, U32), sbuf("x_codes2", QUARTER, U32)]
+        x_quarters = [x_codes[0][:, 0:QUARTER], x_codes[0][:, QUARTER:BANK], x_codes[1], x_codes[2]]
         lists = [keep.tile([P, T // LIST_ROWS], U16, name=f"list{d}") for d in range(LISTS)]
 
-        nc.sync.dma_start(out=gate_cols[:, 0, :], in_=gate[0, 0, :].rearrange("(p j) -> p j", j=GATE_RUN))
-        nc.sync.dma_start(out=stage[0], in_=w_source[0])
+        nc.sync.dma_start(out=gate_cols, in_=gate[0, 0, :].rearrange("(p j) -> p j", j=GATE_RUN))
+        nc.sync.dma_start(out=stage[0], in_=w1_rows[:, :, 0:P])
+        x_source = x_words[0].rearrange("p n j -> p (n j)").bitcast(I32)
+        nc.sync.dma_start(out=x_codes[0].bitcast(I32), in_=x_source[:, 0:BANK])
         for q in range(P // QUADRANT):
             nc.sync.dma_start(
                 out=x_planes[QUADRANT * q : QUADRANT * q + 16, :].bitcast(I32),
                 in_=x_scales[0, 4 * q : 4 * q + 4, :].bitcast(I32).rearrange("r (a c) -> a r c", a=4),
             )
-        x_source = x_words[0].rearrange("p n j -> p (n j)").bitcast(I32)
-        for half in range(HALVES):
-            nc.sync.dma_start(out=x_codes[half][:].bitcast(I32), in_=x_source[:, half * BANK : (half + 1) * BANK])
-        nc.sync.dma_start(lists[0][:], pos1)
-        nc.sync.dma_start(lists[1][:], pos2)
-        for w in range(1, W2 + 1):
-            nc.sync.dma_start(out=stage[w], in_=w_source[w])
-            if w <= HALVES:
-                nc.sync.dma_start(out=raw_gate[w - 1][:], in_=gate[1, :, (w - 1) * BANK : w * BANK])
-        probe("scales", x_planes[:, 0:1])
-        probe("x", x_codes[1][:, 0:1].bitcast(U8)[:, 0:1])
-        probe("gate", gate_cols[:, 0, 0:1])
+        for a in (2, 3):
+            nc.sync.dma_start(out=x_quarters[a].bitcast(I32), in_=x_source[:, a * QUARTER : (a + 1) * QUARTER])
+        for t in range(1, PARTS):
+            nc.sync.dma_start(out=stage[t], in_=w1_rows[:, :, t * P : (t + 1) * P])
+            if t == 1:
+                nc.sync.dma_start(lists[0][:], pos1)
+                nc.sync.dma_start(lists[1][:], pos2)
+            if t % 2 == 1:
+                nc.sync.dma_start(out=raw_gate[t // 2], in_=gate[1, :, t // 2 * BANK : (t // 2 + 1) * BANK])
+        nc.sync.dma_start(out=stage[PARTS], in_=w2.rearrange("(p j) c -> p j c", j=PACK))
 
+        probe("x0", x_codes[0][:, 0:1])
+        probe("x1", x_codes[1][:, 0:1])
+        probe("sc", x_planes[:, 0:1])
+        probe("s0", stage[0][:, 0, 0:1])
         ident = keep.tile([P, P], F32, name="ident")
-        zeros = keep.tile([P, P], F32, name="zeros", tag="first", align_bytes=64)[:]
+        zeros = sbuf("zeros", P, F32, "first")
         nc.vector.memset(zeros, 0.0)
         nc.gpsimd.affine_select(
             out=ident[:],
@@ -99,257 +98,292 @@ def tile_picked_wlapl_none_l_kernel(
             channel_multiplier=1,
         )
 
-        first_grouped = keep.tile([P, P * PACK], BF16, name="first_grouped", tag="first", align_bytes=64)
-        first_gate = keep.tile([P, T], F32, name="neg_gate0")
-        neg_gate = {(0, f): first_gate[:, f * BANK : (f + 1) * BANK] for f in range(HALVES)}
-        w_codes = [keep.tile([P, P], U32, name=f"w_codes{w}", tag=f"wc{w}", align_bytes=64) for w in range(W2 + 1)]
-        w_scales = [keep.tile([P, P], U8, name=f"w_scales{w}", tag=f"ws{w}", align_bytes=64) for w in range(W2 + 1)]
-        h = [keep.tile([P, T], F32, name=f"h{t}") for t in range(PARTS)]
-        rows = keep.tile([P, BLOCKS, 2, P, 2], BF16, name="rows")
-        row_words = rows[:].rearrange("v b u p e -> v (b u p e)").bitcast(F32)
-        widths = (BANK,) + LATE_CHUNKS
-        z_bf = [keep.tile([P, width * PACK], BF16, name=f"z_bf{c}", align_bytes=64) for c, width in enumerate(widths)]
-        pending = {}
-        state = {"at": 0, "count": 0}
+        first_gate = sbuf("first_gate", T, F32)
+        second_gate = []
+        h = [keep.tile([P, T], F32, name=f"h{t}", tag=f"h{t}", align_bytes=64) for t in range(PARTS)]
+        work = sbuf("work", 9 * BANK, F32)
+        row_words = work[:, 4 * BANK : 4 * BANK + (T - P) * 2]
+        rows = row_words.bitcast(BF16).rearrange("v (b u p e) -> v b u p e", u=2, p=P, e=2)
+        ring = work[:, 0 : 4 * BANK]
+        zone = sbuf("zone", 1152, F32)
+        z_bf = [zone[:, 64 : 64 + 2 * BANK].bitcast(BF16)]
+        z_bf.extend(sbuf(f"z_bf{c}", width * PACK, BF16) for c, width in ((1, PAIR), (2, P), (3, P)))
+        own = sbuf("own", BANK, F32).rearrange("p (s t v) -> p s t v", s=STRIPS, t=PARTS)
+        first_terms = work[:, 6 * PAIR : 17 * PAIR].rearrange("p (s t v) -> p s t v", s=STRIPS, v=STRIP)[:, :, 0:PARTS, :]
+        strip_at = (288, 576)
+        count = []
 
-        def spread_gate(d, f, b):
+        def spread_gate(f, b):
             bank = banks[b][:].rearrange("r (j p) -> r j p", j=PACK)
             for j in range(PACK):
-                column = gate_cols[:, d, PACK * f + j : PACK * f + j + 1]
+                column = gate_cols[:, PACK * f + j : PACK * f + j + 1]
                 nc.tensor.transpose(bank[:, j, :], column.to_broadcast([P, P]), ident[:])
+            target = first_gate.rearrange("r (p f j) -> r p f j", f=2, j=PACK)[:, :, f, :]
+            nc.scalar.activation(out=target, in_=bank.rearrange("r j p -> r p j"), func=COPY, scale=-1.0)
 
-        def fetch_gate(d, f, b, engine):
-            bank = banks[b][:].rearrange("r (j p) -> r j p", j=PACK)
-            target = first_gate[:].rearrange("r (p f j) -> r p f j", f=2, j=PACK)[:, :, f, :]
-            if engine == "scalar":
-                nc.scalar.activation(out=target, in_=bank.rearrange("r j p -> r p j"), func=COPY, scale=-1.0)
-            else:
-                nc.vector.tensor_scalar_mul(target, bank.rearrange("r j p -> r p j"), -1.0)
-            probe(f"g{d}{f}", first_gate[:, 4 * f : 4 * f + 1])
+        def negate_gate(f):
+            second_gate.append(sbuf(f"second_gate{f}", BANK, F32))
+            nc.scalar.activation(out=second_gate[f], in_=raw_gate[f], func=COPY, scale=-1.0)
 
-        def negate_gate(f, tag):
-            tile = keep.tile([P, BANK], F32, name=f"neg_gate1{f}", tag=tag, align_bytes=64)
-            neg_gate.update({(1, f): tile[:]})
-            nc.scalar.activation(out=tile[:], in_=raw_gate[f][:], func=COPY, scale=-1.0)
+        def dealt(target, source):
+            return (
+                target.rearrange("p (s q j) -> p q s j", s=PACK, j=PACK),
+                source.rearrange("p j (q s) -> p q s j", s=PACK),
+            )
 
-        def round_weight(w, target):
-            rounded = target.rearrange("p (c n j) -> p c j n", n=4, j=PACK)
-            source = stage[w].rearrange("p j (c n) -> p c j n", n=4)
-            if w == 0:
-                nc.vector.tensor_copy(out=rounded, in_=source)
-            else:
-                nc.scalar.copy(out=rounded, in_=source)
+        def round_part(t, target):
+            rounded, source = dealt(target, stage[t])
+            nc.scalar.copy(out=rounded, in_=source)
 
-        def quantise_weight(w, target):
-            nc.vector.quantize_mx(out=w_codes[w][:].bitcast(FP8X4), scales=w_scales[w][:], in_=target)
-            probe(f"q{w}", w_scales[w][:, 0:1])
+        def quantise(name, values, tag=None):
+            width = values.shape[1] // PACK
+            codes = sbuf(f"{name}_codes", width, U32, tag)
+            scales = sbuf(f"{name}_scales", width, U8)
+            nc.vector.quantize_mx(out=codes.bitcast(FP8X4), scales=scales, in_=values)
+            probe(name, scales[:, 0:1])
+            return codes, scales
 
-        def project_quarter(t, a, acc):
+        def multiply(acc, weights, codes, scales):
             nc.tensor.matmul_mx(
                 out=acc,
-                lhsT=w_codes[t][:].bitcast(FP8X4),
-                lhsT_scale=w_scales[t][:],
-                rhs=x_codes[a // 2][:, a % 2 * QUARTER : (a % 2 + 1) * QUARTER].bitcast(FP8X4),
-                rhs_scale=x_planes[4 * a : P, :],
+                lhsT=weights[0].bitcast(FP8X4),
+                lhsT_scale=weights[1],
+                rhs=codes.bitcast(FP8X4),
+                rhs_scale=scales,
                 start=True,
                 stop=True,
             )
 
-        def project_first():
-            for a, b in enumerate((6, 7, 4, 5)):
-                acc = banks[b][:, 0:QUARTER]
-                project_quarter(0, a, acc)
-                target = h[0][:, a * QUARTER : (a + 1) * QUARTER]
-                if a % 2 == 0:
-                    nc.vector.tensor_copy(out=target, in_=acc)
-                else:
-                    nc.scalar.copy(out=target, in_=acc)
-            probe("h0", h[0][:, T - 1 : T])
+        def project_quarter(weights, a, acc):
+            multiply(acc, weights, x_quarters[a], x_planes[4 * a : P, :])
 
-        def project(t):
-            for half in range(HALVES):
-                acc = banks[WORK_BANKS[half]]
+        def project(weights, pair_of_banks):
+            for half, b in enumerate(pair_of_banks):
                 for a in range(2):
-                    project_quarter(t, 2 * half + a, acc[:, a * QUARTER : (a + 1) * QUARTER])
-                nc.scalar.copy(out=h[t][:, half * BANK : (half + 1) * BANK], in_=acc[:])
-            probe(f"h{t}", h[t][:, T - 1 : T])
+                    project_quarter(weights, 2 * half + a, banks[b][:, a * QUARTER : (a + 1) * QUARTER])
 
-        def add_turned(place, source, start, stop):
-            b, slot = place
+        def fetch_half(t, half, b):
+            nc.scalar.copy(out=h[t][:, half * BANK : (half + 1) * BANK], in_=banks[b][:])
+            probe(f"h{t}{half}", h[t][:, half * BANK : half * BANK + 1])
+
+        def add_turned(b, slot, source, start=False, stop=False):
             nc.tensor.matmul(
                 banks[b][:, slot * P : (slot + 1) * P], source, ident[:], start=start, stop=stop, is_transpose=True
             )
 
-        terms = {}
+        def add_own(t, block, b, slot):
+            add_turned(b, slot, h[t][:, block * P : (block + 1) * P], start=slot == 0)
 
-        def term_of(count, width):
-            if count in terms:
-                return terms[count]
-            if count == 1:
-                term = keep.tile([P, BANK], F32, name="term1", tag="ws0", align_bytes=64)[:]
-            elif count in (3, 5, 7):
-                term = keep.tile([P, BANK], F32, name=f"term{count}", tag={3: "wc0", 5: "first", 7: "stage3"}[count], align_bytes=64)[:]
-            elif count in Z_AFTER:
-                term = keep.tile([P, width], F32, name=f"term{count}", tag=f"codes{Z_AFTER[count]}", align_bytes=64)[:]
-            else:
-                at = state["at"] if state["at"] + width <= SLOTS[width] * width else 0
-                state.update({"at": at + width})
-                term = ring[:, at : at + width]
-            terms.update({count: term})
-            return term
-
-        def grouped(w):
-            return term_of(2 * w - 1, BANK)[:, 0 : P * PACK // 2].bitcast(BF16)
-
-        def gather(t, d, v0, width):
-            count = state["count"]
-            term = term_of(count, width)
-            state.update({"count": count + 1})
+        def gather(t, d, v0, term):
+            width = term.shape[1]
+            factor = first_gate[:, v0 : v0 + width] if d == 0 else second_gate[v0 // BANK][:, v0 % BANK : v0 % BANK + width]
             nc.vector.tensor_tensor(
-                term,
-                h[t][:].indirect(lists[d][:, v0 // LIST_ROWS : (v0 + width) // LIST_ROWS]),
-                neg_gate[d, v0 // BANK][:, v0 % BANK : v0 % BANK + width],
-                MULT,
+                term, h[t][:].indirect(lists[d][:, v0 // LIST_ROWS : (v0 + width) // LIST_ROWS]), factor, MULT
             )
-            probe(f"n{count}", term[:, 0:1])
-            return term
+            probe(f"n{len(count)}", term[:, 0:1])
+            count.append(1)
 
-        def round_out(b, b0, blocks, t0, parts):
-            p0, p1 = t0 * P // PACK, (t0 + parts) * P // PACK
+        def add_terms(term, places, stop):
+            for i, (b, slot) in enumerate(places):
+                closes = stop and b not in [later for later, unused in places[i + 1 :]]
+                add_turned(b, slot, term[:, i * P : (i + 1) * P], stop=closes)
+
+        def round_blocks(b, t, block, blocks):
             nc.scalar.copy(
-                out=rows[:, b0 : b0 + blocks, :, p0:p1, :].rearrange("v b u p e -> v u b p e"),
-                in_=banks[b][:, 0 : blocks * parts * P].rearrange("v (b p u e) -> v u b p e", b=blocks, u=2, e=2),
+                out=rows[:, block : block + blocks, :, t * QUADRANT : (t + 1) * QUADRANT, :].rearrange("v b u q e -> v u b q e"),
+                in_=banks[b][:, 0 : blocks * P].rearrange("v (b u e q) -> v u b q e", u=2, e=2, q=QUADRANT),
             )
+            probe(f"r{block}{t}", rows[:, block, 0, t * QUADRANT, 0:1])
 
-        per = BANK // P
+        def round_parts(b, block):
+            nc.scalar.copy(
+                out=rows[:, block, :, QUADRANT:P, :].rearrange("v u (t q) e -> v u t q e", q=QUADRANT),
+                in_=banks[b][:, 0 : (PARTS - 1) * P].rearrange("v (t u e q) -> v u t q e", u=2, e=2, q=QUADRANT),
+            )
+            probe(f"r{block}1", rows[:, block, 0, QUADRANT, 0:1])
 
-        def wide_own(t, half, b):
-            for i in range(per):
-                block = half * per + i
-                add_turned((b, i), h[t][:, block * P : (block + 1) * P], i == 0, False)
+        def turn_back(block, blocks, b):
+            for i in range(2 * blocks):
+                at = (2 * block + i) * P
+                nc.tensor.transpose(banks[b][:, i * P : (i + 1) * P], row_words[:, at : at + P], ident[:])
 
-        def wide_terms(t, d, half, b):
-            term = gather(t, d, half * BANK, BANK)
-            for i in range(per):
-                add_turned((b, i), term[:, i * P : (i + 1) * P], False, d == LISTS - 1 and i == per - 1)
-            if d == LISTS - 1:
-                round_out(b, half * per, per, t, 1)
+        def fetch_turned(block, blocks, b, target):
+            nc.scalar.copy(
+                out=target.bitcast(F32).rearrange("p (b v u) -> p b v u", u=2, v=P),
+                in_=banks[b][:, 0 : blocks * PAIR].rearrange("p (b u v) -> p b v u", u=2, v=P),
+            )
+            probe(f"c{block}", target[:, 0:1])
 
-        def late_place(block, t):
-            if (block, t) == (BLOCKS - 1, PARTS - 1):
-                return (3, 0)
-            return ((5, 0, 1, 2)[block - per], t - 1)
+        def by_strips(source):
+            return source.rearrange("p (s v) -> p s v", s=STRIPS)
 
-        def late_own(block, t):
-            place = late_place(block, t)
-            add_turned(place, h[t][:, block * P : (block + 1) * P], place[1] == 0, False)
+        def store(name, v0, width, copy, source, queue):
+            result = sbuf(name, width, F32)
+            copy(out=result.rearrange("m (s w g) -> m s w g", s=STRIPS, g=2), in_=source)
+            queue.dma_start(out=out[:, v0 : v0 + width], in_=result)
 
-        def late_chunk(v0, width):
-            blocks = width // P
-            b0 = v0 // P
-            last = b0 == BLOCKS - 1
+        def plain(acc):
+            return acc.rearrange("m (s w g) -> m s w g", s=STRIPS, g=2)
+
+        spread_gate(0, 2)
+        spread_gate(1, 3)
+        first_values = sbuf("first_values", PACK * P, BF16, "first")
+        rounded, source = dealt(first_values, stage[0])
+        nc.vector.tensor_copy(out=rounded, in_=source)
+        w_first = quantise("w0", first_values)
+        for a, b in enumerate((6, 7, 4, 5)):
+            acc = banks[b][:, 0:QUARTER]
+            project_quarter(w_first, a, acc)
+            copy = nc.vector.tensor_copy if a % 2 == 0 else nc.scalar.copy
+            copy(out=h[0][:, a * QUARTER : (a + 1) * QUARTER], in_=acc)
+        probe("h0", h[0][:, T - 1 : T])
+
+        second_values = sbuf("second_values", PACK * P, BF16, "w0_scales")
+        round_part(1, second_values)
+        w_second = quantise("w1", second_values)
+        later_values = sbuf("later_values", 2 * PACK * P, BF16, "w0_codes")
+        negate_gate(0)
+        for t in (2, 3):
+            round_part(t, later_values[:, (t - 2) * BANK : (t - 1) * BANK])
+        negate_gate(1)
+        term1 = sbuf("term1", 3 * PAIR, F32, "stage1")
+        term2 = sbuf("term2", BANK, F32)
+        term3 = sbuf("term3", BANK, F32, "stage3")
+
+        for block in range(7):
+            add_own(0, block, block // 4, block % 4)
+        first_half = [(0, slot) for slot in range(4)]
+        second_half = [(1, slot) for slot in range(3)]
+        gather(0, 0, 0, ring[:, 0:BANK])
+        add_terms(ring[:, 0:BANK], first_half, False)
+        project(w_second, (6, 7))
+        fetch_half(1, 0, 6)
+        fetch_half(1, 1, 7)
+        gather(0, 0, BANK, term1[:, 0:BANK])
+        add_terms(term1, second_half, False)
+        gather(0, 1, 0, term2)
+        add_terms(term2, first_half, True)
+        codes, scales = quantise("w23", later_values)
+        for t, pair_of_banks in ((2, (4, 5)), (3, (3, 2))):
+            project((codes[:, (t - 2) * P : (t - 1) * P], scales[:, (t - 2) * P : (t - 1) * P]), pair_of_banks)
+        for t, pair_of_banks in ((2, (4, 5)), (3, (3, 2))):
+            for half in range(2):
+                fetch_half(t, half, pair_of_banks[half])
+        gather(0, 1, BANK, term3)
+        add_terms(term3, second_half, True)
+
+        places = {1: [(6, slot) for slot in range(4)], 2: [(7, slot) for slot in range(4)]}
+        places.update({3: [(4, 0), (4, 1), (5, 0), (5, 1)]})
+        late_banks = {4: 3, 5: 2, 6: 0}
+        for t in range(1, PARTS):
+            for block, (b, slot) in enumerate(places[t]):
+                add_own(t, block, b, slot)
+        for block in (4, 5):
             for t in range(1, PARTS):
-                closing = t == PARTS - 1 or (last and t == PARTS - 2)
-                for d in range(LISTS):
-                    term = gather(t, d, v0, width)
-                    for i in range(blocks):
-                        add_turned(late_place(b0 + i, t), term[:, i * P : (i + 1) * P], False, closing and d == LISTS - 1)
-                    if state["count"] - 1 in Z_AFTER:
-                        multiply(Z_AFTER[state["count"] - 1])
-                if last and closing:
-                    t0 = 1 if t == PARTS - 2 else t
-                    round_out(late_place(b0, t)[0], b0, 1, t0, t + 1 - t0)
-            if not last:
-                for i in range(blocks):
-                    round_out(late_place(b0 + i, 1)[0], b0 + i, 1, 1, PARTS - 1)
+                add_own(t, block, late_banks[block], t - 1)
+        last_values = sbuf("last_values", PACK * P, BF16)
+        nc.scalar.copy(
+            out=last_values.rearrange("p (c n j) -> p c j n", n=4, j=PACK),
+            in_=stage[PARTS].rearrange("p j (c n) -> p c j n", n=4),
+        )
+        round_blocks(0, 0, 0, 4)
+        round_blocks(1, 0, 4, 3)
+        for t in range(PARTS):
+            nc.scalar.copy(out=own[:, :, t, :], in_=by_strips(h[t][:, LAST:T]))
+        for t in range(1, PARTS):
+            add_own(t, 6, late_banks[6], t - 1)
+        strip_places = {(0, 0): (1, 0), (0, 1): (1, 1), (1, 0): (4, 0), (1, 1): (5, 0)}
 
-        def turn_back(chunk, b0, i0, pair):
-            z_words = z_bf[chunk][:].bitcast(F32).rearrange("p (b v u) -> p b v u", u=2, v=P)
-            back = banks[WORK_BANKS[(chunk + i0 // 2) % 2]][:].rearrange("p (b u v) -> p b u v", u=2, v=P)
-            for i in range(pair):
-                for u in range(2):
-                    at = ((b0 + i0 + i) * 2 + u) * P
-                    nc.tensor.transpose(back[:, i, u, :], row_words[:, at : at + P], ident[:])
-            nc.scalar.copy(out=z_words[:, i0 : i0 + pair], in_=back[:, 0:pair, :, :].rearrange("p b u v -> p b v u"))
+        def every_second(staged, g):
+            return staged.rearrange("p t v -> p (t v)")[:, g::2]
 
-        def finish(chunk, v0, width, b):
-            turn_back(chunk, v0 // P, 0, width // P)
-            pending.update({chunk: (v0, width, b)})
+        for g in range(2):
+            add_turned(*strip_places[0, g], every_second(own[:, 0], g), start=g == 0)
+        for t in range(1, PARTS):
+            term = ring[:, t * BANK : (t + 1) * BANK]
+            gather(t, 0, 0, term)
+            add_terms(term, places[t], False)
+        w_last = quantise("w4", last_values)
+        term7, term8 = late_terms[:, 0:BANK], late_terms[:, BANK : 2 * BANK]
+        gather(1, 1, 0, term7)
+        add_terms(term7, places[1], True)
+        round_blocks(6, 1, 0, 4)
+        gather(2, 1, 0, term8)
+        add_terms(term8, places[2], True)
+        round_blocks(7, 2, 0, 4)
+        for pair in range(2):
+            term = ring[:, 3 * BANK + pair * PAIR : 3 * BANK + (pair + 1) * PAIR]
+            gather(3, 1, pair * PAIR, term)
+            add_terms(term, places[3][2 * pair : 2 * pair + 2], True)
+            if pair == 0:
+                nc.scalar.copy(out=first_terms[:, 0, 0, :], in_=term1[:, BANK - P : BANK - STRIP])
+            round_blocks(4 + pair, 3, 2 * pair, 2)
+        for pair in range(2):
+            turn_back(2 * pair, 2, 6 + pair)
+            fetch_turned(2 * pair, 2, 6 + pair, z_bf[0][:, pair * 2 * BANK : (pair + 1) * 2 * BANK])
+        nc.scalar.copy(out=first_terms[:, 1, 0, :], in_=term1[:, BANK - STRIP : BANK])
+        for g in range(2):
+            add_turned(*strip_places[1, g], every_second(own[:, 1], g), start=True)
 
-        def multiply(chunk):
-            v0, width, b = pending[chunk]
-            z_codes = keep.tile([P, width], U32, name=f"z_codes{chunk}", tag=f"codes{chunk}", align_bytes=64)
-            z_scales = keep.tile([P, width], U8, name=f"z_scales{chunk}", align_bytes=64)
-            nc.vector.quantize_mx(out=z_codes[:].bitcast(FP8X4), scales=z_scales[:], in_=z_bf[chunk][:])
-            probe(f"z{chunk}", z_scales[:, 0:1])
-            acc = banks[b]
-            nc.tensor.matmul_mx(
-                out=acc[:, 0:width],
-                lhsT=w_codes[W2][:].bitcast(FP8X4),
-                lhsT_scale=w_scales[W2][:],
-                rhs=z_codes[:].bitcast(FP8X4),
-                rhs_scale=z_scales[:],
-                start=True,
-                stop=True,
+        slots = [
+            term7[:, 0:PAIR],
+            term1[:, 192 : 192 + PAIR],
+            term7[:, PAIR:BANK],
+            row_words[:, 0:PAIR],
+            row_words[:, PAIR:BANK],
+            row_words[:, BANK : BANK + PAIR],
+        ]
+        for n, term in enumerate(slots):
+            t, d = 1 + n // 2, n % 2
+            gather(t, d, BANK, term)
+            add_terms(term, [(late_banks[4], t - 1), (late_banks[5], t - 1)], n == len(slots) - 1)
+        for block in (4, 5):
+            round_parts(late_banks[block], block)
+        multiply(banks[6][:], w_last, *quantise("z0", z_bf[0]))
+        turn_back(4, 2, 7)
+
+        for t, term in ((1, term1[:, 448:704]), (2, zone[:, 256:512]), (3, zone[:, 544:800])):
+            gather(t, 0, LAST - P, term)
+            add_terms(term, [(late_banks[6], t - 1)], False)
+            nc.scalar.copy(out=first_terms[:, :, t, :], in_=by_strips(term[:, P:PAIR]))
+            if t == 1:
+                store("result0", 0, BANK, nc.scalar.copy, plain(banks[6][:]), nc.sync)
+        holes = zone[:, strip_at[0] : strip_at[0] + 576].rearrange("p (s v) -> p s v", s=STRIPS)[:, :, 0:STRIP]
+        nc.scalar.copy(out=holes, in_=by_strips(term3[:, BANK - P : BANK]))
+        fetch_turned(4, 2, 7, z_bf[1])
+        for t, term in ((1, slots[-1][:, 0:P]), (2, term1[:, 512:640]), (3, term1[:, 640:768])):
+            gather(t, 1, LAST - P, term)
+            add_terms(term, [(late_banks[6], t - 1)], t == PARTS - 1)
+        round_parts(late_banks[6], 6)
+        for s in range(STRIPS):
+            for g in range(2):
+                add_turned(*strip_places[s, g], every_second(first_terms[:, s], g))
+        for s in range(STRIPS):
+            at = strip_at[s]
+            for t in range(1, PARTS):
+                gather(t, 1, LAST + s * STRIP, zone[:, at + t * STRIP : at + (t + 1) * STRIP])
+            for g in range(2):
+                add_turned(*strip_places[s, g], zone[:, at + g : at + PAIR : 2], stop=s == 1 or g == 1)
+        turn_back(6, 1, 6)
+        fetch_turned(6, 1, 6, z_bf[2])
+        multiply(banks[3][:, 0:PAIR], w_last, *quantise("z1", z_bf[1], "h1"))
+        store("result1", BANK, PAIR, nc.scalar.copy, plain(banks[3][:, 0:PAIR]), nc.sync)
+
+        turned = [sbuf(f"turned{s}", PAIR, F32) for s in range(STRIPS)]
+        for s in range(STRIPS):
+            for g in range(2):
+                b, slot = strip_places[s, g]
+                nc.vector.transpose(turned[s][:, g * P : (g + 1) * P], banks[b][:, slot * P : (slot + 1) * P])
+                probe(f"t{s}{g}", turned[s][:, g * P : g * P + 1])
+        for s in range(STRIPS):
+            nc.vector.tensor_copy(
+                out=z_bf[3][:, s * PAIR : (s + 1) * PAIR].rearrange("p (g c n j) -> p g c j n", g=2, n=4, j=PACK),
+                in_=turned[s].rearrange("p (g j c n) -> p g c j n", g=2, j=PACK, n=4),
             )
-            result = keep.tile([P, width], F32, name=f"result{chunk}")
-            nc.scalar.copy(out=result[:], in_=acc[:, 0:width])
-            queue = nc.scalar if v0 + width == T else nc.sync
-            queue.dma_start(out=out[:, v0 : v0 + width], in_=result[:])
-
-        spread_gate(0, 0, 2)
-        fetch_gate(0, 0, 2, "scalar")
-        spread_gate(0, 1, 3)
-        fetch_gate(0, 1, 3, "scalar")
-        round_weight(0, first_grouped[:])
-        quantise_weight(0, first_grouped[:])
-        project_first()
-        round_weight(1, grouped(1))
-        quantise_weight(1, grouped(1))
-        negate_gate(0, "stage1")
-        project(1)
-        round_weight(2, grouped(2))
-        negate_gate(1, "stage2")
-        for w in range(3, W2 + 1):
-            round_weight(w, grouped(w))
-
-        for half in range(HALVES):
-            wide_own(0, half, half)
-        wide_terms(0, 0, 0, 0)
-        wide_terms(0, 0, 1, 1)
-        wide_terms(0, 1, 0, 0)
-        quantise_weight(2, grouped(2))
-        project(2)
-        wide_terms(0, 1, 1, 1)
-        for t in range(1, PARTS - 1):
-            wide_own(t, 0, t + 1)
-            wide_terms(t, 0, 0, t + 1)
-            if t + 2 <= W2:
-                quantise_weight(t + 2, grouped(t + 2))
-            if t + 2 < W2:
-                project(t + 2)
-            wide_terms(t, 1, 0, t + 1)
-            for block in range(per, BLOCKS - 1):
-                late_own(block, t)
-        for t in range(1, PARTS - 1):
-            late_own(BLOCKS - 1, t)
-        for block in range(per, BLOCKS - 1):
-            late_own(block, PARTS - 1)
-        for pair, b in enumerate((4, 3)):
-            for i in range(2):
-                block = 2 * pair + i
-                add_turned((b, i), h[PARTS - 1][:, block * P : (block + 1) * P], i == 0, False)
-            for d in range(LISTS):
-                term = gather(PARTS - 1, d, pair * QUARTER, QUARTER)
-                for i in range(2):
-                    add_turned((b, i), term[:, i * P : (i + 1) * P], False, d == LISTS - 1 and i == 1)
-            round_out(b, 2 * pair, 2, PARTS - 1, 1)
-            turn_back(0, 0, 2 * pair, 2)
-        pending.update({0: (0, BANK, 4)})
-        late_own(BLOCKS - 1, PARTS - 1)
-        v0 = BANK
-        for chunk, width in enumerate(LATE_CHUNKS):
-            late_chunk(v0, width)
-            finish(chunk + 1, v0, width, late_place(v0 // P, 1)[0])
-            v0 = v0 + width
-        multiply(len(LATE_CHUNKS))
+        third = quantise("z2", z_bf[2], "turned0")
+        fourth = quantise("z3", z_bf[3])
+        multiply(banks[0][:, 0:P], w_last, *third)
+        multiply(banks[1][:, 0:P], w_last, *fourth)
+        store("result2", LAST - P, P, nc.vector.tensor_copy, plain(banks[0][:, 0:P]), nc.sync)
+        last_columns = banks[1][:, 0:P].rearrange("m (s g w) -> m s w g", s=STRIPS, g=2)
+        store("result3", LAST, P, nc.scalar.copy, last_columns, nc.scalar)

@@ -13,6 +13,7 @@ U16 = mybir.dt.uint16
 U8 = mybir.dt.uint8
 FP8X4 = mybir.dt.float8_e4m3fn_x4
 MULT = mybir.AluOpType.mult
+SUBTRACT = mybir.AluOpType.subtract
 COPY = mybir.ActivationFunctionType.Copy
 
 P = 128
@@ -52,11 +53,9 @@ def tile_picked_wlapl_none_l_kernel(
         nc.vector.memset(x_planes.bitcast(I32), 0)
 
         w1_rows = w1.rearrange("(p j) c -> p j c", j=PACK)
-        late_terms = sbuf("late_terms", 2 * BANK, F32)
-        stage = [sbuf(f"stage{w}", PACK * P, F32) for w in range(PARTS)] + [late_terms[:, PAIR : PAIR + BANK]]
-        stage = [place.rearrange("p (j c) -> p j c", j=PACK) for place in stage]
+        stage = [sbuf(f"stage{w}", PACK * P, F32).rearrange("p (j c) -> p j c", j=PACK) for w in range(PARTS + 1)]
         gate_cols = sbuf("gate_cols", GATE_RUN, F32)
-        raw_gate = [sbuf(f"raw_gate{f}", BANK, F32) for f in range(2)]
+        second_gate = [sbuf(f"second_gate{f}", BANK, F32) for f in range(2)]
         x_codes = [sbuf("x_codes0", BANK, U32), sbuf("x_codes1", QUARTER, U32), sbuf("x_codes2", QUARTER, U32)]
         x_quarters = [x_codes[0][:, 0:QUARTER], x_codes[0][:, QUARTER:BANK], x_codes[1], x_codes[2]]
         lists = [keep.tile([P, T // LIST_ROWS], U16, name=f"list{d}") for d in range(LISTS)]
@@ -78,13 +77,9 @@ def tile_picked_wlapl_none_l_kernel(
                 nc.sync.dma_start(lists[0][:], pos1)
                 nc.sync.dma_start(lists[1][:], pos2)
             if t % 2 == 1:
-                nc.sync.dma_start(out=raw_gate[t // 2], in_=gate[1, :, t // 2 * BANK : (t // 2 + 1) * BANK])
+                nc.sync.dma_start(out=second_gate[t // 2], in_=gate[1, :, t // 2 * BANK : (t // 2 + 1) * BANK])
         nc.sync.dma_start(out=stage[PARTS], in_=w2.rearrange("(p j) c -> p j c", j=PACK))
 
-        probe("x0", x_codes[0][:, 0:1])
-        probe("x1", x_codes[1][:, 0:1])
-        probe("sc", x_planes[:, 0:1])
-        probe("s0", stage[0][:, 0, 0:1])
         ident = keep.tile([P, P], F32, name="ident")
         zeros = sbuf("zeros", P, F32, "first")
         nc.vector.memset(zeros, 0.0)
@@ -99,19 +94,16 @@ def tile_picked_wlapl_none_l_kernel(
         )
 
         first_gate = sbuf("first_gate", T, F32)
-        second_gate = []
         h = [keep.tile([P, T], F32, name=f"h{t}", tag=f"h{t}", align_bytes=64) for t in range(PARTS)]
-        work = sbuf("work", 9 * BANK, F32)
-        row_words = work[:, 4 * BANK : 4 * BANK + (T - P) * 2]
-        rows = row_words.bitcast(BF16).rearrange("v (b u p e) -> v b u p e", u=2, p=P, e=2)
-        ring = work[:, 0 : 4 * BANK]
-        zone = sbuf("zone", 1152, F32)
-        z_bf = [zone[:, 64 : 64 + 2 * BANK].bitcast(BF16)]
-        z_bf.extend(sbuf(f"z_bf{c}", width * PACK, BF16) for c, width in ((1, PAIR), (2, P), (3, P)))
-        own = sbuf("own", BANK, F32).rearrange("p (s t v) -> p s t v", s=STRIPS, t=PARTS)
-        first_terms = work[:, 6 * PAIR : 17 * PAIR].rearrange("p (s t v) -> p s t v", s=STRIPS, v=STRIP)[:, :, 0:PARTS, :]
-        strip_at = (288, 576)
-        count = []
+        row_words = sbuf("row_words", (T - P) * 2, F32)
+        rows = row_words.bitcast(BF16).rearrange("v (g p e) -> v g p e", p=P, e=2)
+        first_wide = [sbuf(f"first_wide{t}", LAST, F32) for t in range(2)]
+        second_wide = [sbuf(f"second_wide{t}", T, F32) for t in range(2)]
+        first_work = sbuf("first_work", 2 * (P + BANK), F32)
+        first_ring = [first_work[:, r * (P + BANK) + P : (r + 1) * (P + BANK)] for r in range(2)]
+        second_ring = [sbuf(f"second_ring{r}", BANK, F32) for r in range(2)]
+        strip_first = first_work.rearrange("p (s t v) -> p s t v", s=STRIPS, v=STRIP)[:, :, 0:PARTS, :]
+        strip_rest = sbuf("strip_rest", BANK, F32).rearrange("p (s t v) -> p s t v", s=STRIPS, t=PARTS)
 
         def spread_gate(f, b):
             bank = banks[b][:].rearrange("r (j p) -> r j p", j=PACK)
@@ -121,23 +113,16 @@ def tile_picked_wlapl_none_l_kernel(
             target = first_gate.rearrange("r (p f j) -> r p f j", f=2, j=PACK)[:, :, f, :]
             nc.scalar.activation(out=target, in_=bank.rearrange("r j p -> r p j"), func=COPY, scale=-1.0)
 
-        def negate_gate(f):
-            second_gate.append(sbuf(f"second_gate{f}", BANK, F32))
-            nc.scalar.activation(out=second_gate[f], in_=raw_gate[f], func=COPY, scale=-1.0)
-
-        def dealt(target, source):
-            return (
-                target.rearrange("p (s q j) -> p q s j", s=PACK, j=PACK),
-                source.rearrange("p j (q s) -> p q s j", s=PACK),
+        def round_part(t, values):
+            nc.vector.tensor_copy(
+                out=values.rearrange("p (s q j) -> p q s j", s=PACK, j=PACK),
+                in_=stage[t].rearrange("p j (q s) -> p q s j", s=PACK),
             )
+            return values
 
-        def round_part(t, target):
-            rounded, source = dealt(target, stage[t])
-            nc.scalar.copy(out=rounded, in_=source)
-
-        def quantise(name, values, tag=None):
+        def quantise(name, values):
             width = values.shape[1] // PACK
-            codes = sbuf(f"{name}_codes", width, U32, tag)
+            codes = sbuf(f"{name}_codes", width, U32)
             scales = sbuf(f"{name}_scales", width, U8)
             nc.vector.quantize_mx(out=codes.bitcast(FP8X4), scales=scales, in_=values)
             probe(name, scales[:, 0:1])
@@ -157,233 +142,258 @@ def tile_picked_wlapl_none_l_kernel(
         def project_quarter(weights, a, acc):
             multiply(acc, weights, x_quarters[a], x_planes[4 * a : P, :])
 
+        def project_half(weights, half, b):
+            for a in range(2):
+                project_quarter(weights, 2 * half + a, banks[b][:, a * QUARTER : (a + 1) * QUARTER])
+
         def project(weights, pair_of_banks):
             for half, b in enumerate(pair_of_banks):
-                for a in range(2):
-                    project_quarter(weights, 2 * half + a, banks[b][:, a * QUARTER : (a + 1) * QUARTER])
+                project_half(weights, half, b)
 
         def fetch_half(t, half, b):
             nc.scalar.copy(out=h[t][:, half * BANK : (half + 1) * BANK], in_=banks[b][:])
             probe(f"h{t}{half}", h[t][:, half * BANK : half * BANK + 1])
+
+        def fetch_part(t, pair_of_banks):
+            for half, b in enumerate(pair_of_banks):
+                fetch_half(t, half, b)
 
         def add_turned(b, slot, source, start=False, stop=False):
             nc.tensor.matmul(
                 banks[b][:, slot * P : (slot + 1) * P], source, ident[:], start=start, stop=stop, is_transpose=True
             )
 
-        def add_own(t, block, b, slot):
-            add_turned(b, slot, h[t][:, block * P : (block + 1) * P], start=slot == 0)
+        def add_blocks(b, slot, source, start=False, stop=False):
+            blocks = source.shape[1] // P
+            for i in range(blocks):
+                add_turned(b, slot + i, source[:, i * P : (i + 1) * P], start and i == 0, stop and i == blocks - 1)
 
-        def gather(t, d, v0, term):
+        def picked(t, d, v0, width):
+            return h[t][:].indirect(lists[d][:, v0 // LIST_ROWS : (v0 + width) // LIST_ROWS])
+
+        def gather_first(t, v0, term):
             width = term.shape[1]
-            factor = first_gate[:, v0 : v0 + width] if d == 0 else second_gate[v0 // BANK][:, v0 % BANK : v0 % BANK + width]
-            nc.vector.tensor_tensor(
-                term, h[t][:].indirect(lists[d][:, v0 // LIST_ROWS : (v0 + width) // LIST_ROWS]), factor, MULT
-            )
-            probe(f"n{len(count)}", term[:, 0:1])
-            count.append(1)
+            nc.vector.tensor_tensor(term, picked(t, 0, v0, width), first_gate[:, v0 : v0 + width], MULT)
+            probe(f"a{t}_{v0}", term[:, 0:1])
 
-        def add_terms(term, places, stop):
-            for i, (b, slot) in enumerate(places):
-                closes = stop and b not in [later for later, unused in places[i + 1 :]]
-                add_turned(b, slot, term[:, i * P : (i + 1) * P], stop=closes)
+        def gather_second(t, v0, term):
+            nc.scalar.activation(term, picked(t, 1, v0, term.shape[1]), COPY)
+            probe(f"b{t}_{v0}", term[:, 0:1])
 
-        def round_blocks(b, t, block, blocks):
-            nc.scalar.copy(
-                out=rows[:, block : block + blocks, :, t * QUADRANT : (t + 1) * QUADRANT, :].rearrange("v b u q e -> v u b q e"),
-                in_=banks[b][:, 0 : blocks * P].rearrange("v (b u e q) -> v u b q e", u=2, e=2, q=QUADRANT),
-            )
-            probe(f"r{block}{t}", rows[:, block, 0, t * QUADRANT, 0:1])
+        def gate_at(v0, width):
+            return second_gate[v0 // BANK][:, v0 % BANK : v0 % BANK + width]
 
-        def round_parts(b, block):
-            nc.scalar.copy(
-                out=rows[:, block, :, QUADRANT:P, :].rearrange("v u (t q) e -> v u t q e", q=QUADRANT),
-                in_=banks[b][:, 0 : (PARTS - 1) * P].rearrange("v (t u e q) -> v u t q e", u=2, e=2, q=QUADRANT),
+        def weigh(term, factor):
+            nc.vector.scalar_tensor_tensor(term, term, -1.0, factor, MULT, MULT)
+
+        def by_strips(source):
+            return source.rearrange("p (s v) -> p s v", s=STRIPS)
+
+        def weigh_strips(t, term):
+            nc.vector.tensor_tensor(strip_rest[:, :, t, :], by_strips(term), by_strips(gate_at(LAST, P)), MULT)
+
+        def weigh_last_strips():
+            terms = second_ring[1].rearrange("p (t b s v) -> p t b s v", t=2, s=STRIPS, v=STRIP)[:, :, 1]
+            factor = by_strips(gate_at(LAST, P)).unsqueeze(1).to_broadcast([P, 2, STRIPS, STRIP])
+            nc.vector.tensor_tensor(strip_rest[:, :, 2:PARTS, :].rearrange("p s t v -> p t s v"), terms, factor, MULT)
+
+        def subtract_strips(t):
+            nc.vector.tensor_tensor(strip_rest[:, :, t, :], by_strips(h[t][:, LAST:T]), strip_rest[:, :, t, :], SUBTRACT)
+
+        def round_sums(b, t, parts, block, blocks, copy=nc.scalar.copy):
+            target = rows[:, 2 * block : 2 * (block + blocks), t * QUADRANT : (t + parts) * QUADRANT, :]
+            copy(
+                out=target.rearrange("v g (t q) e -> v t g q e", q=QUADRANT),
+                in_=banks[b][:, 0 : parts * blocks * P].rearrange("v (t g e q) -> v t g q e", t=parts, e=2, q=QUADRANT),
             )
-            probe(f"r{block}1", rows[:, block, 0, QUADRANT, 0:1])
+            probe(f"r{t}_{block}", rows[:, 2 * block, t * QUADRANT, 0:1])
 
         def turn_back(block, blocks, b):
             for i in range(2 * blocks):
                 at = (2 * block + i) * P
                 nc.tensor.transpose(banks[b][:, i * P : (i + 1) * P], row_words[:, at : at + P], ident[:])
 
-        def fetch_turned(block, blocks, b, target):
+        def fetch_turned(block, blocks, b):
+            target = sbuf(f"z_values{block}", blocks * P * PACK, BF16)
             nc.scalar.copy(
                 out=target.bitcast(F32).rearrange("p (b v u) -> p b v u", u=2, v=P),
                 in_=banks[b][:, 0 : blocks * PAIR].rearrange("p (b u v) -> p b v u", u=2, v=P),
             )
             probe(f"c{block}", target[:, 0:1])
+            return target
 
-        def by_strips(source):
-            return source.rearrange("p (s v) -> p s v", s=STRIPS)
-
-        def store(name, v0, width, copy, source, queue):
-            result = sbuf(name, width, F32)
+        def store(v0, width, copy, source, queue):
+            result = sbuf(f"result{v0}", width, F32)
             copy(out=result.rearrange("m (s w g) -> m s w g", s=STRIPS, g=2), in_=source)
             queue.dma_start(out=out[:, v0 : v0 + width], in_=result)
 
         def plain(acc):
             return acc.rearrange("m (s w g) -> m s w g", s=STRIPS, g=2)
 
+        def every_second(staged, g):
+            return staged.rearrange("p t v -> p (t v)")[:, g::2]
+
         spread_gate(0, 2)
         spread_gate(1, 3)
-        first_values = sbuf("first_values", PACK * P, BF16, "first")
-        rounded, source = dealt(first_values, stage[0])
-        nc.vector.tensor_copy(out=rounded, in_=source)
-        w_first = quantise("w0", first_values)
+        weights = quantise("w0", round_part(0, sbuf("values0", BANK, BF16, "first")))
         for a, b in enumerate((6, 7, 4, 5)):
             acc = banks[b][:, 0:QUARTER]
-            project_quarter(w_first, a, acc)
+            project_quarter(weights, a, acc)
             copy = nc.vector.tensor_copy if a % 2 == 0 else nc.scalar.copy
             copy(out=h[0][:, a * QUARTER : (a + 1) * QUARTER], in_=acc)
         probe("h0", h[0][:, T - 1 : T])
 
-        second_values = sbuf("second_values", PACK * P, BF16, "w0_scales")
-        round_part(1, second_values)
-        w_second = quantise("w1", second_values)
-        later_values = sbuf("later_values", 2 * PACK * P, BF16, "w0_codes")
-        negate_gate(0)
+        product_banks = {1: (5, 5), 2: (6, 7), 3: (4, 5)}
+        wide_banks = {0: (0, 1), 1: (2, 3)}
+        chunks = ((0, 2, 6, 5), (2, 2, 7, 4), (4, 2, 0, 5), (6, 1, 1, 1))
+        strip_banks = (2, 3)
+
+        def open_wide(t):
+            add_blocks(wide_banks[t][0], 0, h[t][:, 0:BANK], start=True)
+            add_blocks(wide_banks[t][1], 0, h[t][:, BANK:LAST], start=True)
+
+        def gather_rest(t):
+            gather_first(t, BANK, first_wide[t][:, BANK:LAST])
+            add_blocks(wide_banks[t][1], 0, first_wide[t][:, BANK:LAST])
+            for s in range(STRIPS):
+                gather_first(t, LAST + s * STRIP, strip_first[:, s, t, :])
+
+        def weigh_wide(t, half):
+            v0, v1 = half * BANK, min((half + 1) * BANK, LAST)
+            weigh(second_wide[t][:, v0:v1], gate_at(v0, v1 - v0))
+            add_blocks(wide_banks[t][half], 0, second_wide[t][:, v0:v1], stop=True)
+
+        def open_chunk(c):
+            block, blocks, b, unused = chunks[c]
+            for t in (2, 3):
+                add_blocks(b, (t - 2) * blocks, h[t][:, block * P : (block + blocks) * P], start=t == 2)
+
+        def gather_chunk(c):
+            block, blocks, b, unused = chunks[c]
+            for t in (2, 3):
+                gather_second(t, block * P, second_ring[c % 2][:, (t - 2) * PAIR : (t - 1) * PAIR])
+            for t in (2, 3):
+                term = first_ring[c % 2][:, (t - 2) * PAIR : (t - 1) * PAIR] if blocks == 2 else first_ring[t - 2][:, 0:P]
+                gather_first(t, block * P, term)
+                add_blocks(b, (t - 2) * blocks, term)
+
+        def weigh_chunk(c):
+            block, blocks, b, unused = chunks[c]
+            width = blocks * P
+            terms = second_ring[c % 2].rearrange("p (t v) -> p t v", t=2)[:, :, 0:width]
+            weigh(terms, gate_at(block * P, width).unsqueeze(1).to_broadcast([P, 2, width]))
+            for t in (2, 3):
+                add_blocks(b, (t - 2) * blocks, terms[:, t - 2, :], stop=t == 3)
+
+        def round_chunk(c):
+            block, blocks, b, back = chunks[c]
+            round_sums(b, 2, 2, block, blocks)
+            turn_back(block, blocks, back)
+
+        def fetch_chunk(c):
+            block, blocks, b, back = chunks[c]
+            return fetch_turned(block, blocks, back)
+
+        def finish_chunk(c, values):
+            block, blocks, b, back = chunks[c]
+            multiply(banks[b][:, 0 : blocks * P], w_last, *quantise(f"z{c}", values))
+
+        def store_chunk(c, copy):
+            block, blocks, b, back = chunks[c]
+            store(block * P, blocks * P, copy, plain(banks[b][:, 0 : blocks * P]), nc.sync)
+
+        values = round_part(1, sbuf("values1", BANK, BF16, "w0_codes"))
+        gather_first(0, 0, first_wide[0][:, 0:BANK])
+        weights = quantise("w1", values)
+        for half in range(2):
+            gather_second(0, half * BANK, second_wide[0][:, half * BANK : (half + 1) * BANK])
+            project_half(weights, half, product_banks[1][half])
+            fetch_half(1, half, product_banks[1][half])
+        open_wide(0)
+        add_blocks(wide_banks[0][0], 0, first_wide[0][:, 0:BANK])
+        values = sbuf("values23", 2 * BANK, BF16, "w1_codes")
         for t in (2, 3):
-            round_part(t, later_values[:, (t - 2) * BANK : (t - 1) * BANK])
-        negate_gate(1)
-        term1 = sbuf("term1", 3 * PAIR, F32, "stage1")
-        term2 = sbuf("term2", BANK, F32)
-        term3 = sbuf("term3", BANK, F32, "stage3")
-
-        for block in range(7):
-            add_own(0, block, block // 4, block % 4)
-        first_half = [(0, slot) for slot in range(4)]
-        second_half = [(1, slot) for slot in range(3)]
-        gather(0, 0, 0, ring[:, 0:BANK])
-        add_terms(ring[:, 0:BANK], first_half, False)
-        project(w_second, (6, 7))
-        fetch_half(1, 0, 6)
-        fetch_half(1, 1, 7)
-        gather(0, 0, BANK, term1[:, 0:BANK])
-        add_terms(term1, second_half, False)
-        gather(0, 1, 0, term2)
-        add_terms(term2, first_half, True)
-        codes, scales = quantise("w23", later_values)
-        for t, pair_of_banks in ((2, (4, 5)), (3, (3, 2))):
-            project((codes[:, (t - 2) * P : (t - 1) * P], scales[:, (t - 2) * P : (t - 1) * P]), pair_of_banks)
-        for t, pair_of_banks in ((2, (4, 5)), (3, (3, 2))):
-            for half in range(2):
-                fetch_half(t, half, pair_of_banks[half])
-        gather(0, 1, BANK, term3)
-        add_terms(term3, second_half, True)
-
-        places = {1: [(6, slot) for slot in range(4)], 2: [(7, slot) for slot in range(4)]}
-        places.update({3: [(4, 0), (4, 1), (5, 0), (5, 1)]})
-        late_banks = {4: 3, 5: 2, 6: 0}
-        for t in range(1, PARTS):
-            for block, (b, slot) in enumerate(places[t]):
-                add_own(t, block, b, slot)
-        for block in (4, 5):
-            for t in range(1, PARTS):
-                add_own(t, block, late_banks[block], t - 1)
-        last_values = sbuf("last_values", PACK * P, BF16)
-        nc.scalar.copy(
+            round_part(t, values[:, (t - 2) * BANK : (t - 1) * BANK])
+        gather_rest(0)
+        codes, scales = quantise("w23", values)
+        for t in (2, 3):
+            project((codes[:, (t - 2) * P : (t - 1) * P], scales[:, (t - 2) * P : (t - 1) * P]), product_banks[t])
+        for half in range(2):
+            gather_second(1, half * BANK, second_wide[1][:, half * BANK : (half + 1) * BANK])
+        for t in (2, 3):
+            fetch_part(t, product_banks[t])
+        weigh_wide(0, 0)
+        open_wide(1)
+        gather_first(1, 0, first_wide[1][:, 0:BANK])
+        add_blocks(wide_banks[1][0], 0, first_wide[1][:, 0:BANK])
+        weigh_wide(0, 1)
+        weigh_strips(0, second_wide[0][:, LAST:T])
+        gather_rest(1)
+        weigh_wide(1, 0)
+        subtract_strips(0)
+        weigh_wide(1, 1)
+        weigh_strips(1, second_wide[1][:, LAST:T])
+        last_values = sbuf("last_values", PACK * P, BF16, "w23_codes")
+        nc.vector.tensor_copy(
             out=last_values.rearrange("p (c n j) -> p c j n", n=4, j=PACK),
             in_=stage[PARTS].rearrange("p j (c n) -> p c j n", n=4),
         )
-        round_blocks(0, 0, 0, 4)
-        round_blocks(1, 0, 4, 3)
-        for t in range(PARTS):
-            nc.scalar.copy(out=own[:, :, t, :], in_=by_strips(h[t][:, LAST:T]))
-        for t in range(1, PARTS):
-            add_own(t, 6, late_banks[6], t - 1)
-        strip_places = {(0, 0): (1, 0), (0, 1): (1, 1), (1, 0): (4, 0), (1, 1): (5, 0)}
+        subtract_strips(1)
 
-        def every_second(staged, g):
-            return staged.rearrange("p t v -> p (t v)")[:, g::2]
-
-        for g in range(2):
-            add_turned(*strip_places[0, g], every_second(own[:, 0], g), start=g == 0)
-        for t in range(1, PARTS):
-            term = ring[:, t * BANK : (t + 1) * BANK]
-            gather(t, 0, 0, term)
-            add_terms(term, places[t], False)
+        open_chunk(0)
+        open_chunk(1)
+        gather_chunk(0)
         w_last = quantise("w4", last_values)
-        term7, term8 = late_terms[:, 0:BANK], late_terms[:, BANK : 2 * BANK]
-        gather(1, 1, 0, term7)
-        add_terms(term7, places[1], True)
-        round_blocks(6, 1, 0, 4)
-        gather(2, 1, 0, term8)
-        add_terms(term8, places[2], True)
-        round_blocks(7, 2, 0, 4)
-        for pair in range(2):
-            term = ring[:, 3 * BANK + pair * PAIR : 3 * BANK + (pair + 1) * PAIR]
-            gather(3, 1, pair * PAIR, term)
-            add_terms(term, places[3][2 * pair : 2 * pair + 2], True)
-            if pair == 0:
-                nc.scalar.copy(out=first_terms[:, 0, 0, :], in_=term1[:, BANK - P : BANK - STRIP])
-            round_blocks(4 + pair, 3, 2 * pair, 2)
-        for pair in range(2):
-            turn_back(2 * pair, 2, 6 + pair)
-            fetch_turned(2 * pair, 2, 6 + pair, z_bf[0][:, pair * 2 * BANK : (pair + 1) * 2 * BANK])
-        nc.scalar.copy(out=first_terms[:, 1, 0, :], in_=term1[:, BANK - STRIP : BANK])
-        for g in range(2):
-            add_turned(*strip_places[1, g], every_second(own[:, 1], g), start=True)
-
-        slots = [
-            term7[:, 0:PAIR],
-            term1[:, 192 : 192 + PAIR],
-            term7[:, PAIR:BANK],
-            row_words[:, 0:PAIR],
-            row_words[:, PAIR:BANK],
-            row_words[:, BANK : BANK + PAIR],
-        ]
-        for n, term in enumerate(slots):
-            t, d = 1 + n // 2, n % 2
-            gather(t, d, BANK, term)
-            add_terms(term, [(late_banks[4], t - 1), (late_banks[5], t - 1)], n == len(slots) - 1)
-        for block in (4, 5):
-            round_parts(late_banks[block], block)
-        multiply(banks[6][:], w_last, *quantise("z0", z_bf[0]))
-        turn_back(4, 2, 7)
-
-        for t, term in ((1, term1[:, 448:704]), (2, zone[:, 256:512]), (3, zone[:, 544:800])):
-            gather(t, 0, LAST - P, term)
-            add_terms(term, [(late_banks[6], t - 1)], False)
-            nc.scalar.copy(out=first_terms[:, :, t, :], in_=by_strips(term[:, P:PAIR]))
-            if t == 1:
-                store("result0", 0, BANK, nc.scalar.copy, plain(banks[6][:]), nc.sync)
-        holes = zone[:, strip_at[0] : strip_at[0] + 576].rearrange("p (s v) -> p s v", s=STRIPS)[:, :, 0:STRIP]
-        nc.scalar.copy(out=holes, in_=by_strips(term3[:, BANK - P : BANK]))
-        fetch_turned(4, 2, 7, z_bf[1])
-        for t, term in ((1, slots[-1][:, 0:P]), (2, term1[:, 512:640]), (3, term1[:, 640:768])):
-            gather(t, 1, LAST - P, term)
-            add_terms(term, [(late_banks[6], t - 1)], t == PARTS - 1)
-        round_parts(late_banks[6], 6)
+        round_sums(wide_banks[0][0], 0, 1, 0, 4)
+        weigh_chunk(0)
+        gather_chunk(1)
+        round_sums(wide_banks[1][0], 1, 1, 0, 4)
+        round_chunk(0)
+        round_sums(wide_banks[0][1], 0, 1, 4, 3, nc.vector.tensor_copy)
+        open_chunk(2)
+        open_chunk(3)
+        weigh_chunk(1)
+        gather_chunk(2)
+        round_sums(wide_banks[1][1], 1, 1, 4, 3)
+        weigh_chunk(2)
+        gather_chunk(3)
+        weigh_chunk(3)
+        first = fetch_chunk(0)
+        round_chunk(1)
+        round_chunk(2)
+        second = fetch_chunk(1)
+        round_chunk(3)
+        third = fetch_chunk(2)
+        fourth = fetch_chunk(3)
+        weigh_last_strips()
+        finish_chunk(0, first)
+        for t in (2, 3):
+            subtract_strips(t)
         for s in range(STRIPS):
             for g in range(2):
-                add_turned(*strip_places[s, g], every_second(first_terms[:, s], g))
+                add_turned(strip_banks[s], g, every_second(strip_rest[:, s], g), start=g == 0)
         for s in range(STRIPS):
-            at = strip_at[s]
-            for t in range(1, PARTS):
-                gather(t, 1, LAST + s * STRIP, zone[:, at + t * STRIP : at + (t + 1) * STRIP])
+            for t in (2, 3):
+                gather_first(t, LAST + s * STRIP, strip_first[:, s, t, :])
             for g in range(2):
-                add_turned(*strip_places[s, g], zone[:, at + g : at + PAIR : 2], stop=s == 1 or g == 1)
-        turn_back(6, 1, 6)
-        fetch_turned(6, 1, 6, z_bf[2])
-        multiply(banks[3][:, 0:PAIR], w_last, *quantise("z1", z_bf[1], "h1"))
-        store("result1", BANK, PAIR, nc.scalar.copy, plain(banks[3][:, 0:PAIR]), nc.sync)
-
+                add_turned(strip_banks[s], g, every_second(strip_first[:, s], g), stop=g == 1)
+        finish_chunk(1, second)
+        finish_chunk(2, third)
+        store_chunk(0, nc.scalar.copy)
+        store_chunk(1, nc.scalar.copy)
         turned = [sbuf(f"turned{s}", PAIR, F32) for s in range(STRIPS)]
+        strip_values = sbuf("strip_values", P * PACK, BF16)
         for s in range(STRIPS):
             for g in range(2):
-                b, slot = strip_places[s, g]
-                nc.vector.transpose(turned[s][:, g * P : (g + 1) * P], banks[b][:, slot * P : (slot + 1) * P])
-                probe(f"t{s}{g}", turned[s][:, g * P : g * P + 1])
+                nc.vector.transpose(turned[s][:, g * P : (g + 1) * P], banks[strip_banks[s]][:, g * P : (g + 1) * P])
         for s in range(STRIPS):
             nc.vector.tensor_copy(
-                out=z_bf[3][:, s * PAIR : (s + 1) * PAIR].rearrange("p (g c n j) -> p g c j n", g=2, n=4, j=PACK),
+                out=strip_values[:, s * PAIR : (s + 1) * PAIR].rearrange("p (g c n j) -> p g c j n", g=2, n=4, j=PACK),
                 in_=turned[s].rearrange("p (g j c n) -> p g c j n", g=2, j=PACK, n=4),
             )
-        third = quantise("z2", z_bf[2], "turned0")
-        fourth = quantise("z3", z_bf[3])
-        multiply(banks[0][:, 0:P], w_last, *third)
-        multiply(banks[1][:, 0:P], w_last, *fourth)
-        store("result2", LAST - P, P, nc.vector.tensor_copy, plain(banks[0][:, 0:P]), nc.sync)
-        last_columns = banks[1][:, 0:P].rearrange("m (s g w) -> m s w g", s=STRIPS, g=2)
-        store("result3", LAST, P, nc.scalar.copy, last_columns, nc.scalar)
+        finish_chunk(3, fourth)
+        multiply(banks[6][:, 0:P], w_last, *quantise("z4", strip_values))
+        store_chunk(2, nc.scalar.copy)
+        store_chunk(3, nc.vector.tensor_copy)
+        last_columns = banks[6][:, 0:P].rearrange("m (s g w) -> m s w g", s=STRIPS, g=2)
+        store(LAST, P, nc.scalar.copy, last_columns, nc.scalar)

@@ -13,7 +13,6 @@ U16 = mybir.dt.uint16
 U8 = mybir.dt.uint8
 FP8X4 = mybir.dt.float8_e4m3fn_x4
 MULT = mybir.AluOpType.mult
-SUBTRACT = mybir.AluOpType.subtract
 COPY = mybir.ActivationFunctionType.Copy
 
 P = 128
@@ -26,9 +25,6 @@ LIST_ROWS = 16
 QUADRANT = 32
 QUARTER = T // 4
 GATE_RUN = T // P
-STRIP = 64
-STRIPS = 2
-LAST = T - STRIPS * STRIP
 PROBES = (None, None)
 
 
@@ -95,15 +91,13 @@ def tile_picked_wlapl_none_l_kernel(
 
         first_gate = sbuf("first_gate", T, F32)
         h = [keep.tile([P, T], F32, name=f"h{t}", tag=f"h{t}", align_bytes=64) for t in range(PARTS)]
-        row_words = sbuf("row_words", (T - P) * 2, F32)
+        row_words = sbuf("row_words", T * 2, F32)
         rows = row_words.bitcast(BF16).rearrange("v (g p e) -> v g p e", p=P, e=2)
-        first_wide = [sbuf(f"first_wide{t}", LAST, F32) for t in range(2)]
+        first_wide = [sbuf(f"first_wide{t}", T, F32) for t in range(2)]
         second_wide = [sbuf(f"second_wide{t}", T, F32) for t in range(2)]
-        first_work = sbuf("first_work", 2 * (P + BANK), F32)
-        first_ring = [first_work[:, r * (P + BANK) + P : (r + 1) * (P + BANK)] for r in range(2)]
-        second_ring = [sbuf(f"second_ring{r}", BANK, F32) for r in range(2)]
-        strip_first = first_work.rearrange("p (s t v) -> p s t v", s=STRIPS, v=STRIP)[:, :, 0:PARTS, :]
-        strip_rest = sbuf("strip_rest", BANK, F32).rearrange("p (s t v) -> p s t v", s=STRIPS, t=PARTS)
+        first_ring = [sbuf(f"first_ring{r}", BANK, F32) for r in range(2)]
+        second_ring = [sbuf(f"second_ring{r}", BANK, F32) for r in range(3)]
+        second_ring = [second_ring[0], second_ring[1], second_ring[0], second_ring[2]]
 
         def spread_gate(f, b):
             bank = banks[b][:].rearrange("r (j p) -> r j p", j=PACK)
@@ -186,20 +180,6 @@ def tile_picked_wlapl_none_l_kernel(
         def weigh(term, factor):
             nc.vector.scalar_tensor_tensor(term, term, -1.0, factor, MULT, MULT)
 
-        def by_strips(source):
-            return source.rearrange("p (s v) -> p s v", s=STRIPS)
-
-        def weigh_strips(t, term):
-            nc.vector.tensor_tensor(strip_rest[:, :, t, :], by_strips(term), by_strips(gate_at(LAST, P)), MULT)
-
-        def weigh_last_strips():
-            terms = second_ring[1].rearrange("p (t b s v) -> p t b s v", t=2, s=STRIPS, v=STRIP)[:, :, 1]
-            factor = by_strips(gate_at(LAST, P)).unsqueeze(1).to_broadcast([P, 2, STRIPS, STRIP])
-            nc.vector.tensor_tensor(strip_rest[:, :, 2:PARTS, :].rearrange("p s t v -> p t s v"), terms, factor, MULT)
-
-        def subtract_strips(t):
-            nc.vector.tensor_tensor(strip_rest[:, :, t, :], by_strips(h[t][:, LAST:T]), strip_rest[:, :, t, :], SUBTRACT)
-
         def round_sums(b, t, parts, block, blocks, copy=nc.scalar.copy):
             target = rows[:, 2 * block : 2 * (block + blocks), t * QUADRANT : (t + parts) * QUADRANT, :]
             copy(
@@ -213,25 +193,22 @@ def tile_picked_wlapl_none_l_kernel(
                 at = (2 * block + i) * P
                 nc.tensor.transpose(banks[b][:, i * P : (i + 1) * P], row_words[:, at : at + P], ident[:])
 
-        def fetch_turned(block, blocks, b):
+        def fetch_turned(block, blocks, b, copy=nc.scalar.copy):
             target = sbuf(f"z_values{block}", blocks * P * PACK, BF16)
-            nc.scalar.copy(
+            copy(
                 out=target.bitcast(F32).rearrange("p (b v u) -> p b v u", u=2, v=P),
                 in_=banks[b][:, 0 : blocks * PAIR].rearrange("p (b u v) -> p b v u", u=2, v=P),
             )
             probe(f"c{block}", target[:, 0:1])
             return target
 
-        def store(v0, width, copy, source, queue):
-            result = sbuf(f"result{v0}", width, F32)
-            copy(out=result.rearrange("m (s w g) -> m s w g", s=STRIPS, g=2), in_=source)
-            queue.dma_start(out=out[:, v0 : v0 + width], in_=result)
+        def finish(block, blocks, b, values):
+            multiply(banks[b][:, 0 : blocks * P], w_last, *quantise(f"z{block}", values))
 
-        def plain(acc):
-            return acc.rearrange("m (s w g) -> m s w g", s=STRIPS, g=2)
-
-        def every_second(staged, g):
-            return staged.rearrange("p t v -> p (t v)")[:, g::2]
+        def store(block, blocks, b, copy, queue):
+            result = sbuf(f"result{block}", blocks * P, F32)
+            copy(out=result, in_=banks[b][:, 0 : blocks * P])
+            queue.dma_start(out=out[:, block * P : (block + blocks) * P], in_=result)
 
         spread_gate(0, 2)
         spread_gate(1, 3)
@@ -245,76 +222,63 @@ def tile_picked_wlapl_none_l_kernel(
 
         product_banks = {1: (5, 5), 2: (6, 7), 3: (4, 5)}
         wide_banks = {0: (0, 1), 1: (2, 3)}
-        chunks = ((0, 2, 6, 5), (2, 2, 7, 4), (4, 2, 0, 5), (6, 1, 1, 1))
-        strip_banks = (2, 3)
+        chunk_banks = (6, 7, 0)
+        back_banks = (4, 5, 4)
+        pair_bank, last_banks = 2, (1, 3)
 
         def open_wide(t):
-            add_blocks(wide_banks[t][0], 0, h[t][:, 0:BANK], start=True)
-            add_blocks(wide_banks[t][1], 0, h[t][:, BANK:LAST], start=True)
+            for half in range(2):
+                add_blocks(wide_banks[t][half], 0, h[t][:, half * BANK : (half + 1) * BANK], start=True)
 
-        def gather_rest(t):
-            gather_first(t, BANK, first_wide[t][:, BANK:LAST])
-            add_blocks(wide_banks[t][1], 0, first_wide[t][:, BANK:LAST])
-            for s in range(STRIPS):
-                gather_first(t, LAST + s * STRIP, strip_first[:, s, t, :])
+        def gather_wide(t, half):
+            term = first_wide[t][:, half * BANK : (half + 1) * BANK]
+            gather_first(t, half * BANK, term)
+            return term
 
         def weigh_wide(t, half):
-            v0, v1 = half * BANK, min((half + 1) * BANK, LAST)
-            weigh(second_wide[t][:, v0:v1], gate_at(v0, v1 - v0))
-            add_blocks(wide_banks[t][half], 0, second_wide[t][:, v0:v1], stop=True)
+            term = second_wide[t][:, half * BANK : (half + 1) * BANK]
+            weigh(term, second_gate[half])
+            add_blocks(wide_banks[t][half], 0, term, stop=True)
 
         def open_chunk(c):
-            block, blocks, b, unused = chunks[c]
             for t in (2, 3):
-                add_blocks(b, (t - 2) * blocks, h[t][:, block * P : (block + blocks) * P], start=t == 2)
+                add_blocks(chunk_banks[c], (t - 2) * 2, h[t][:, c * PAIR : (c + 1) * PAIR], start=t == 2)
 
-        def gather_chunk(c):
-            block, blocks, b, unused = chunks[c]
+        def gather_seconds(c):
             for t in (2, 3):
-                gather_second(t, block * P, second_ring[c % 2][:, (t - 2) * PAIR : (t - 1) * PAIR])
+                gather_second(t, c * PAIR, second_ring[c][:, (t - 2) * PAIR : (t - 1) * PAIR])
+
+        def gather_firsts(c):
             for t in (2, 3):
-                term = first_ring[c % 2][:, (t - 2) * PAIR : (t - 1) * PAIR] if blocks == 2 else first_ring[t - 2][:, 0:P]
-                gather_first(t, block * P, term)
-                add_blocks(b, (t - 2) * blocks, term)
+                term = first_ring[c % 2][:, (t - 2) * PAIR : (t - 1) * PAIR]
+                gather_first(t, c * PAIR, term)
+                add_blocks(chunk_banks[c], (t - 2) * 2, term)
+
+        def weigh_pair(c):
+            terms = second_ring[c].rearrange("p (t v) -> p t v", t=2)
+            weigh(terms, gate_at(c * PAIR, PAIR).unsqueeze(1).to_broadcast([P, 2, PAIR]))
 
         def weigh_chunk(c):
-            block, blocks, b, unused = chunks[c]
-            width = blocks * P
-            terms = second_ring[c % 2].rearrange("p (t v) -> p t v", t=2)[:, :, 0:width]
-            weigh(terms, gate_at(block * P, width).unsqueeze(1).to_broadcast([P, 2, width]))
-            for t in (2, 3):
-                add_blocks(b, (t - 2) * blocks, terms[:, t - 2, :], stop=t == 3)
+            weigh_pair(c)
+            add_blocks(chunk_banks[c], 0, second_ring[c], stop=True)
 
         def round_chunk(c):
-            block, blocks, b, back = chunks[c]
-            round_sums(b, 2, 2, block, blocks)
-            turn_back(block, blocks, back)
-
-        def fetch_chunk(c):
-            block, blocks, b, back = chunks[c]
-            return fetch_turned(block, blocks, back)
-
-        def finish_chunk(c, values):
-            block, blocks, b, back = chunks[c]
-            multiply(banks[b][:, 0 : blocks * P], w_last, *quantise(f"z{c}", values))
-
-        def store_chunk(c, copy):
-            block, blocks, b, back = chunks[c]
-            store(block * P, blocks * P, copy, plain(banks[b][:, 0 : blocks * P]), nc.sync)
+            round_sums(chunk_banks[c], 2, 2, 2 * c, 2)
+            turn_back(2 * c, 2, back_banks[c])
 
         values = round_part(1, sbuf("values1", BANK, BF16, "w0_codes"))
-        gather_first(0, 0, first_wide[0][:, 0:BANK])
+        term = gather_wide(0, 0)
         weights = quantise("w1", values)
         for half in range(2):
             gather_second(0, half * BANK, second_wide[0][:, half * BANK : (half + 1) * BANK])
             project_half(weights, half, product_banks[1][half])
             fetch_half(1, half, product_banks[1][half])
         open_wide(0)
-        add_blocks(wide_banks[0][0], 0, first_wide[0][:, 0:BANK])
+        add_blocks(wide_banks[0][0], 0, term)
         values = sbuf("values23", 2 * BANK, BF16, "w1_codes")
         for t in (2, 3):
             round_part(t, values[:, (t - 2) * BANK : (t - 1) * BANK])
-        gather_rest(0)
+        term = gather_wide(0, 1)
         codes, scales = quantise("w23", values)
         for t in (2, 3):
             project((codes[:, (t - 2) * P : (t - 1) * P], scales[:, (t - 2) * P : (t - 1) * P]), product_banks[t])
@@ -322,78 +286,69 @@ def tile_picked_wlapl_none_l_kernel(
             gather_second(1, half * BANK, second_wide[1][:, half * BANK : (half + 1) * BANK])
         for t in (2, 3):
             fetch_part(t, product_banks[t])
+        add_blocks(wide_banks[0][1], 0, term)
         weigh_wide(0, 0)
         open_wide(1)
-        gather_first(1, 0, first_wide[1][:, 0:BANK])
-        add_blocks(wide_banks[1][0], 0, first_wide[1][:, 0:BANK])
+        add_blocks(wide_banks[1][0], 0, gather_wide(1, 0))
         weigh_wide(0, 1)
-        weigh_strips(0, second_wide[0][:, LAST:T])
-        gather_rest(1)
+        add_blocks(wide_banks[1][1], 0, gather_wide(1, 1))
         weigh_wide(1, 0)
-        subtract_strips(0)
         weigh_wide(1, 1)
-        weigh_strips(1, second_wide[1][:, LAST:T])
         last_values = sbuf("last_values", PACK * P, BF16, "w23_codes")
         nc.vector.tensor_copy(
             out=last_values.rearrange("p (c n j) -> p c j n", n=4, j=PACK),
             in_=stage[PARTS].rearrange("p j (c n) -> p c j n", n=4),
         )
-        subtract_strips(1)
 
         open_chunk(0)
         open_chunk(1)
-        gather_chunk(0)
+        gather_seconds(0)
+        gather_firsts(0)
         w_last = quantise("w4", last_values)
         round_sums(wide_banks[0][0], 0, 1, 0, 4)
         weigh_chunk(0)
-        gather_chunk(1)
+        gather_seconds(1)
+        gather_firsts(1)
         round_sums(wide_banks[1][0], 1, 1, 0, 4)
         round_chunk(0)
-        round_sums(wide_banks[0][1], 0, 1, 4, 3, nc.vector.tensor_copy)
         open_chunk(2)
-        open_chunk(3)
         weigh_chunk(1)
-        gather_chunk(2)
-        round_sums(wide_banks[1][1], 1, 1, 4, 3)
+        gather_seconds(2)
+        gather_firsts(2)
+        round_sums(wide_banks[0][1], 0, 1, 4, 4, nc.vector.tensor_copy)
+        gather_seconds(3)
         weigh_chunk(2)
-        gather_chunk(3)
-        weigh_chunk(3)
-        first = fetch_chunk(0)
+        add_blocks(pair_bank, 0, h[2][:, 3 * PAIR : T], start=True)
+        gather_first(2, 3 * PAIR, first_ring[1][:, 0:PAIR])
+        add_blocks(pair_bank, 0, first_ring[1][:, 0:PAIR])
+        round_sums(wide_banks[1][1], 1, 1, 4, 4, nc.vector.tensor_copy)
+        weigh_pair(3)
+        add_blocks(pair_bank, 0, second_ring[3][:, 0:PAIR], stop=True)
+        for i, b in enumerate(last_banks):
+            add_blocks(b, 0, h[3][:, (6 + i) * P : (7 + i) * P], start=True)
+            add_blocks(b, 0, second_ring[3][:, PAIR + i * P : PAIR + (i + 1) * P])
+        first = fetch_turned(0, 2, back_banks[0])
         round_chunk(1)
         round_chunk(2)
-        second = fetch_chunk(1)
-        round_chunk(3)
-        third = fetch_chunk(2)
-        fourth = fetch_chunk(3)
-        weigh_last_strips()
-        finish_chunk(0, first)
-        for t in (2, 3):
-            subtract_strips(t)
-        for s in range(STRIPS):
-            for g in range(2):
-                add_turned(strip_banks[s], g, every_second(strip_rest[:, s], g), start=g == 0)
-        for s in range(STRIPS):
-            for t in (2, 3):
-                gather_first(t, LAST + s * STRIP, strip_first[:, s, t, :])
-            for g in range(2):
-                add_turned(strip_banks[s], g, every_second(strip_first[:, s], g), stop=g == 1)
-        finish_chunk(1, second)
-        finish_chunk(2, third)
-        store_chunk(0, nc.scalar.copy)
-        store_chunk(1, nc.scalar.copy)
-        turned = [sbuf(f"turned{s}", PAIR, F32) for s in range(STRIPS)]
-        strip_values = sbuf("strip_values", P * PACK, BF16)
-        for s in range(STRIPS):
-            for g in range(2):
-                nc.vector.transpose(turned[s][:, g * P : (g + 1) * P], banks[strip_banks[s]][:, g * P : (g + 1) * P])
-        for s in range(STRIPS):
-            nc.vector.tensor_copy(
-                out=strip_values[:, s * PAIR : (s + 1) * PAIR].rearrange("p (g c n j) -> p g c j n", g=2, n=4, j=PACK),
-                in_=turned[s].rearrange("p (g j c n) -> p g c j n", g=2, j=PACK, n=4),
-            )
-        finish_chunk(3, fourth)
-        multiply(banks[6][:, 0:P], w_last, *quantise("z4", strip_values))
-        store_chunk(2, nc.scalar.copy)
-        store_chunk(3, nc.vector.tensor_copy)
-        last_columns = banks[6][:, 0:P].rearrange("m (s g w) -> m s w g", s=STRIPS, g=2)
-        store(LAST, P, nc.scalar.copy, last_columns, nc.scalar)
+        round_sums(pair_bank, 2, 1, 6, 2)
+        second = fetch_turned(2, 2, back_banks[1])
+        third = fetch_turned(4, 2, back_banks[2])
+        for i, b in enumerate(last_banks):
+            term = first_ring[0][:, i * P : (i + 1) * P]
+            gather_first(3, (6 + i) * P, term)
+            add_blocks(b, 0, term, stop=True)
+            if i == 0:
+                finish(0, 2, chunk_banks[0], first)
+        for i, b in enumerate(last_banks):
+            round_sums(b, 3, 1, 6 + i, 1, nc.vector.tensor_copy)
+            turn_back(6 + i, 1, b)
+        finish(2, 2, chunk_banks[1], second)
+        fourth = fetch_turned(6, 1, last_banks[0], nc.vector.tensor_copy)
+        finish(4, 2, chunk_banks[2], third)
+        fifth = fetch_turned(7, 1, last_banks[1], nc.vector.tensor_copy)
+        finish(6, 1, pair_bank, fourth)
+        finish(7, 1, back_banks[1], fifth)
+        for c in range(3):
+            store(2 * c, 2, chunk_banks[c], nc.scalar.copy, nc.sync)
+        store(6, 1, pair_bank, nc.vector.tensor_copy, nc.sync)
+        store(7, 1, back_banks[1], nc.scalar.copy, nc.scalar)

@@ -72,8 +72,8 @@ def tile_picked_wlapl_none_l_kernel(
             if t == 1:
                 nc.sync.dma_start(lists[0][:], pos1)
                 nc.sync.dma_start(lists[1][:], pos2)
-            if t % 2 == 1:
-                nc.sync.dma_start(out=second_gate[t // 2], in_=gate[1, :, t // 2 * BANK : (t // 2 + 1) * BANK])
+        for f in range(2):
+            nc.sync.dma_start(out=second_gate[f], in_=gate[1, :, f * BANK : (f + 1) * BANK])
         nc.sync.dma_start(out=stage[PARTS], in_=w2.rearrange("(p j) c -> p j c", j=PACK))
 
         ident = keep.tile([P, P], F32, name="ident")
@@ -97,7 +97,7 @@ def tile_picked_wlapl_none_l_kernel(
         second_wide = [sbuf(f"second_wide{t}", T, F32) for t in range(2)]
         first_ring = [sbuf(f"first_ring{r}", BANK, F32) for r in range(2)]
         second_ring = [sbuf(f"second_ring{r}", BANK, F32) for r in range(3)]
-        second_ring = [second_ring[0], second_ring[1], second_ring[0], second_ring[2]]
+        second_ring = [second_ring[c % 3] for c in range(4)]
 
         def spread_gate(f, b):
             bank = banks[b][:].rearrange("r (j p) -> r j p", j=PACK)
@@ -114,9 +114,9 @@ def tile_picked_wlapl_none_l_kernel(
             )
             return values
 
-        def quantise(name, values):
+        def quantise(name, values, tag=None):
             width = values.shape[1] // PACK
-            codes = sbuf(f"{name}_codes", width, U32)
+            codes = sbuf(f"{name}_codes", width, U32, tag)
             scales = sbuf(f"{name}_scales", width, U8)
             nc.vector.quantize_mx(out=codes.bitcast(FP8X4), scales=scales, in_=values)
             probe(name, scales[:, 0:1])
@@ -202,8 +202,8 @@ def tile_picked_wlapl_none_l_kernel(
             probe(f"c{block}", target[:, 0:1])
             return target
 
-        def finish(block, blocks, b, values):
-            multiply(banks[b][:, 0 : blocks * P], w_last, *quantise(f"z{block}", values))
+        def finish(block, blocks, b, values, tag=None):
+            multiply(banks[b][:, 0 : blocks * P], w_last, *quantise(f"z{block}", values, tag))
 
         def store(block, blocks, b, copy, queue):
             result = sbuf(f"result{block}", blocks * P, F32)
@@ -329,26 +329,29 @@ def tile_picked_wlapl_none_l_kernel(
             add_blocks(b, 0, second_ring[3][:, PAIR + i * P : PAIR + (i + 1) * P])
         first = fetch_turned(0, 2, back_banks[0])
         round_chunk(1)
-        round_chunk(2)
+        round_sums(chunk_banks[2], 2, 2, 4, 2)
         round_sums(pair_bank, 2, 1, 6, 2)
-        second = fetch_turned(2, 2, back_banks[1])
-        third = fetch_turned(4, 2, back_banks[2])
         for i, b in enumerate(last_banks):
             term = first_ring[0][:, i * P : (i + 1) * P]
             gather_first(3, (6 + i) * P, term)
             add_blocks(b, 0, term, stop=True)
             if i == 0:
-                finish(0, 2, chunk_banks[0], first)
+                early = quantise("z0", first)
+        turn_back(4, 2, back_banks[2])
+        multiply(banks[chunk_banks[0]][:, 0:PAIR], w_last, *early)
+        store(0, 2, chunk_banks[0], nc.scalar.copy, nc.sync)
+        second = fetch_turned(2, 2, back_banks[1])
+        third = fetch_turned(4, 2, back_banks[2])
         for i, b in enumerate(last_banks):
             round_sums(b, 3, 1, 6 + i, 1, nc.vector.tensor_copy)
             turn_back(6 + i, 1, b)
-        finish(2, 2, chunk_banks[1], second)
+        finish(2, 2, chunk_banks[1], second, "first_ring0")
         fourth = fetch_turned(6, 1, last_banks[0], nc.vector.tensor_copy)
+        fifth = fetch_turned(7, 1, last_banks[1])
         finish(4, 2, chunk_banks[2], third)
-        fifth = fetch_turned(7, 1, last_banks[1], nc.vector.tensor_copy)
         finish(6, 1, pair_bank, fourth)
         finish(7, 1, back_banks[1], fifth)
-        for c in range(3):
-            store(2 * c, 2, chunk_banks[c], nc.scalar.copy, nc.sync)
+        store(2, 2, chunk_banks[1], nc.scalar.copy, nc.sync)
+        store(4, 2, chunk_banks[2], nc.scalar.copy, nc.sync)
         store(6, 1, pair_bank, nc.vector.tensor_copy, nc.sync)
         store(7, 1, back_banks[1], nc.scalar.copy, nc.scalar)

@@ -25,6 +25,7 @@ LIST_ROWS = 16
 QUADRANT = 32
 QUARTER = T // 4
 GATE_RUN = T // P
+SHARED = T - PAIR
 PROBES = (None, None)
 
 
@@ -93,11 +94,9 @@ def tile_picked_wlapl_none_l_kernel(
         h = [keep.tile([P, T], F32, name=f"h{t}", tag=f"h{t}", align_bytes=64) for t in range(PARTS)]
         row_words = sbuf("row_words", T * 2, F32)
         rows = row_words.bitcast(BF16).rearrange("v (g p e) -> v g p e", p=P, e=2)
-        first_wide = [sbuf(f"first_wide{t}", T, F32) for t in range(2)]
         second_wide = [sbuf(f"second_wide{t}", T, F32) for t in range(2)]
         first_ring = [sbuf(f"first_ring{r}", BANK, F32) for r in range(2)]
         second_ring = [sbuf(f"second_ring{r}", BANK, F32) for r in range(3)]
-        second_ring = [second_ring[c % 3] for c in range(4)]
 
         def spread_gate(f, b):
             bank = banks[b][:].rearrange("r (j p) -> r j p", j=PACK)
@@ -107,8 +106,8 @@ def tile_picked_wlapl_none_l_kernel(
             target = first_gate.rearrange("r (p f j) -> r p f j", f=2, j=PACK)[:, :, f, :]
             nc.scalar.activation(out=target, in_=bank.rearrange("r j p -> r p j"), func=COPY, scale=-1.0)
 
-        def round_part(t, values):
-            nc.vector.tensor_copy(
+        def round_part(t, values, copy=nc.vector.tensor_copy):
+            copy(
                 out=values.rearrange("p (s q j) -> p q s j", s=PACK, j=PACK),
                 in_=stage[t].rearrange("p j (q s) -> p q s j", s=PACK),
             )
@@ -174,6 +173,11 @@ def tile_picked_wlapl_none_l_kernel(
             nc.scalar.activation(term, picked(t, 1, v0, term.shape[1]), COPY)
             probe(f"b{t}_{v0}", term[:, 0:1])
 
+        def gather_weighed(t, v0, term):
+            width = term.shape[1]
+            nc.vector.tensor_tensor(term, picked(t, 1, v0, width), last_gate[:, v0 - SHARED : v0 - SHARED + width], MULT)
+            probe(f"b{t}_{v0}", term[:, 0:1])
+
         def gate_at(v0, width):
             return second_gate[v0 // BANK][:, v0 % BANK : v0 % BANK + width]
 
@@ -220,7 +224,7 @@ def tile_picked_wlapl_none_l_kernel(
             copy(out=h[0][:, a * QUARTER : (a + 1) * QUARTER], in_=acc)
         probe("h0", h[0][:, T - 1 : T])
 
-        product_banks = {1: (5, 5), 2: (6, 7), 3: (4, 5)}
+        product_banks = {1: (5, 4), 2: (6, 7), 3: (5, 4)}
         wide_banks = {0: (0, 1), 1: (2, 3)}
         chunk_banks = (6, 7, 0)
         back_banks = (4, 5, 4)
@@ -231,14 +235,21 @@ def tile_picked_wlapl_none_l_kernel(
                 add_blocks(wide_banks[t][half], 0, h[t][:, half * BANK : (half + 1) * BANK], start=True)
 
         def gather_wide(t, half):
-            term = first_wide[t][:, half * BANK : (half + 1) * BANK]
+            term = sbuf(f"first_wide{t}{half}", BANK, F32, "stage1" if (t, half) == (0, 1) else None)
             gather_first(t, half * BANK, term)
             return term
 
+        def gather_wide_second(t, half):
+            gather_second(t, half * BANK, second_wide[t][:, half * BANK : min((half + 1) * BANK, SHARED)])
+
         def weigh_wide(t, half):
-            term = second_wide[t][:, half * BANK : (half + 1) * BANK]
-            weigh(term, second_gate[half])
-            add_blocks(wide_banks[t][half], 0, term, stop=True)
+            term = second_wide[t][:, half * BANK : min((half + 1) * BANK, SHARED)]
+            weigh(term, gate_at(half * BANK, term.shape[1]))
+            add_blocks(wide_banks[t][half], 0, term, stop=half == 0)
+
+        def close_wide(t):
+            gather_weighed(t, SHARED, second_wide[t][:, SHARED:T])
+            add_blocks(wide_banks[t][1], 2, second_wide[t][:, SHARED:T], stop=True)
 
         def open_chunk(c):
             for t in (2, 3):
@@ -254,23 +265,16 @@ def tile_picked_wlapl_none_l_kernel(
                 gather_first(t, c * PAIR, term)
                 add_blocks(chunk_banks[c], (t - 2) * 2, term)
 
-        def weigh_pair(c):
+        def weigh_chunk(c):
             terms = second_ring[c].rearrange("p (t v) -> p t v", t=2)
             weigh(terms, gate_at(c * PAIR, PAIR).unsqueeze(1).to_broadcast([P, 2, PAIR]))
-
-        def weigh_chunk(c):
-            weigh_pair(c)
             add_blocks(chunk_banks[c], 0, second_ring[c], stop=True)
 
-        def round_chunk(c):
-            round_sums(chunk_banks[c], 2, 2, 2 * c, 2)
-            turn_back(2 * c, 2, back_banks[c])
-
-        values = round_part(1, sbuf("values1", BANK, BF16, "w0_codes"))
+        values = round_part(1, sbuf("values1", BANK, BF16, "w0_codes"), nc.scalar.copy)
         term = gather_wide(0, 0)
         weights = quantise("w1", values)
         for half in range(2):
-            gather_second(0, half * BANK, second_wide[0][:, half * BANK : (half + 1) * BANK])
+            gather_wide_second(0, half)
             project_half(weights, half, product_banks[1][half])
             fetch_half(1, half, product_banks[1][half])
         open_wide(0)
@@ -283,7 +287,7 @@ def tile_picked_wlapl_none_l_kernel(
         for t in (2, 3):
             project((codes[:, (t - 2) * P : (t - 1) * P], scales[:, (t - 2) * P : (t - 1) * P]), product_banks[t])
         for half in range(2):
-            gather_second(1, half * BANK, second_wide[1][:, half * BANK : (half + 1) * BANK])
+            gather_wide_second(1, half)
         for t in (2, 3):
             fetch_part(t, product_banks[t])
         add_blocks(wide_banks[0][1], 0, term)
@@ -292,8 +296,12 @@ def tile_picked_wlapl_none_l_kernel(
         add_blocks(wide_banks[1][0], 0, gather_wide(1, 0))
         weigh_wide(0, 1)
         add_blocks(wide_banks[1][1], 0, gather_wide(1, 1))
+        last_gate = sbuf("last_gate", PAIR, F32, "w23_scales")
+        nc.vector.tensor_scalar(last_gate, gate_at(SHARED, PAIR), -1.0, None, MULT)
         weigh_wide(1, 0)
+        close_wide(0)
         weigh_wide(1, 1)
+        close_wide(1)
         last_values = sbuf("last_values", PACK * P, BF16, "w23_codes")
         nc.vector.tensor_copy(
             out=last_values.rearrange("p (c n j) -> p c j n", n=4, j=PACK),
@@ -310,48 +318,48 @@ def tile_picked_wlapl_none_l_kernel(
         gather_seconds(1)
         gather_firsts(1)
         round_sums(wide_banks[1][0], 1, 1, 0, 4)
-        round_chunk(0)
-        open_chunk(2)
+        round_sums(chunk_banks[0], 2, 2, 0, 2)
         weigh_chunk(1)
+        round_sums(chunk_banks[1], 2, 2, 2, 2)
+        turn_back(0, 2, back_banks[0])
+        first = fetch_turned(0, 2, back_banks[0])
+        open_chunk(2)
         gather_seconds(2)
         gather_firsts(2)
-        round_sums(wide_banks[0][1], 0, 1, 4, 4, nc.vector.tensor_copy)
-        gather_seconds(3)
+        round_sums(wide_banks[0][1], 0, 1, 4, 4)
+        round_sums(wide_banks[1][1], 1, 1, 4, 4)
         weigh_chunk(2)
-        add_blocks(pair_bank, 0, h[2][:, 3 * PAIR : T], start=True)
-        gather_first(2, 3 * PAIR, first_ring[1][:, 0:PAIR])
+        turn_back(2, 2, back_banks[1])
+        add_blocks(pair_bank, 0, h[2][:, SHARED:T], start=True)
+        gather_first(2, SHARED, first_ring[1][:, 0:PAIR])
         add_blocks(pair_bank, 0, first_ring[1][:, 0:PAIR])
-        round_sums(wide_banks[1][1], 1, 1, 4, 4, nc.vector.tensor_copy)
-        weigh_pair(3)
-        add_blocks(pair_bank, 0, second_ring[3][:, 0:PAIR], stop=True)
+        gather_weighed(2, SHARED, first_ring[1][:, PAIR:BANK])
+        add_blocks(pair_bank, 0, first_ring[1][:, PAIR:BANK], stop=True)
+        gather_first(3, SHARED, first_ring[0][:, 0:PAIR])
+        last_terms = sbuf("last_terms", PAIR, F32, "second_ring2")
         for i, b in enumerate(last_banks):
             add_blocks(b, 0, h[3][:, (6 + i) * P : (7 + i) * P], start=True)
-            add_blocks(b, 0, second_ring[3][:, PAIR + i * P : PAIR + (i + 1) * P])
-        first = fetch_turned(0, 2, back_banks[0])
-        round_chunk(1)
+            add_blocks(b, 0, first_ring[0][:, i * P : (i + 1) * P])
+            gather_weighed(3, (6 + i) * P, last_terms[:, i * P : (i + 1) * P])
+            add_blocks(b, 0, last_terms[:, i * P : (i + 1) * P], stop=True)
+        early = quantise("z0", first, "first_ring0")
         round_sums(chunk_banks[2], 2, 2, 4, 2)
         round_sums(pair_bank, 2, 1, 6, 2)
-        for i, b in enumerate(last_banks):
-            term = first_ring[0][:, i * P : (i + 1) * P]
-            gather_first(3, (6 + i) * P, term)
-            add_blocks(b, 0, term, stop=True)
-            if i == 0:
-                early = quantise("z0", first)
         turn_back(4, 2, back_banks[2])
         multiply(banks[chunk_banks[0]][:, 0:PAIR], w_last, *early)
-        store(0, 2, chunk_banks[0], nc.scalar.copy, nc.sync)
         second = fetch_turned(2, 2, back_banks[1])
         third = fetch_turned(4, 2, back_banks[2])
         for i, b in enumerate(last_banks):
             round_sums(b, 3, 1, 6 + i, 1, nc.vector.tensor_copy)
             turn_back(6 + i, 1, b)
-        finish(2, 2, chunk_banks[1], second, "first_ring0")
+        finish(2, 2, chunk_banks[1], second, "second_ring2")
         fourth = fetch_turned(6, 1, last_banks[0], nc.vector.tensor_copy)
         fifth = fetch_turned(7, 1, last_banks[1])
         finish(4, 2, chunk_banks[2], third)
         finish(6, 1, pair_bank, fourth)
         finish(7, 1, back_banks[1], fifth)
+        store(0, 2, chunk_banks[0], nc.scalar.copy, nc.sync)
         store(2, 2, chunk_banks[1], nc.scalar.copy, nc.sync)
-        store(4, 2, chunk_banks[2], nc.scalar.copy, nc.sync)
+        store(4, 2, chunk_banks[2], nc.vector.tensor_copy, nc.sync)
         store(6, 1, pair_bank, nc.vector.tensor_copy, nc.sync)
         store(7, 1, back_banks[1], nc.scalar.copy, nc.scalar)

@@ -324,13 +324,14 @@ def tile_picked_wlapl_none_l_kernel(
         turn_back(0, 2, back_banks[0])
         first = fetch_turned(0, 2, back_banks[0])
         open_chunk(2)
+        add_blocks(pair_bank, 0, h[2][:, SHARED:T], start=True)
         gather_seconds(2)
         gather_firsts(2)
-        round_sums(wide_banks[0][1], 0, 1, 4, 4)
-        round_sums(wide_banks[1][1], 1, 1, 4, 4)
+        for i, b in enumerate(last_banks):
+            round_sums(wide_banks[i][1], i, 1, 4, 4)
+            add_blocks(b, 0, h[3][:, (6 + i) * P : (7 + i) * P], start=True)
         weigh_chunk(2)
         turn_back(2, 2, back_banks[1])
-        add_blocks(pair_bank, 0, h[2][:, SHARED:T], start=True)
         gather_first(2, SHARED, first_ring[1][:, 0:PAIR])
         add_blocks(pair_bank, 0, first_ring[1][:, 0:PAIR])
         gather_weighed(2, SHARED, first_ring[1][:, PAIR:BANK])
@@ -338,20 +339,21 @@ def tile_picked_wlapl_none_l_kernel(
         gather_first(3, SHARED, first_ring[0][:, 0:PAIR])
         last_terms = sbuf("last_terms", PAIR, F32, "second_ring2")
         for i, b in enumerate(last_banks):
-            add_blocks(b, 0, h[3][:, (6 + i) * P : (7 + i) * P], start=True)
             add_blocks(b, 0, first_ring[0][:, i * P : (i + 1) * P])
+        for i, b in enumerate(last_banks):
             gather_weighed(3, (6 + i) * P, last_terms[:, i * P : (i + 1) * P])
             add_blocks(b, 0, last_terms[:, i * P : (i + 1) * P], stop=True)
-        early = quantise("z0", first, "first_ring0")
         round_sums(chunk_banks[2], 2, 2, 4, 2)
         round_sums(pair_bank, 2, 1, 6, 2)
         turn_back(4, 2, back_banks[2])
-        multiply(banks[chunk_banks[0]][:, 0:PAIR], w_last, *early)
         second = fetch_turned(2, 2, back_banks[1])
         third = fetch_turned(4, 2, back_banks[2])
         for i, b in enumerate(last_banks):
             round_sums(b, 3, 1, 6 + i, 1, nc.vector.tensor_copy)
             turn_back(6 + i, 1, b)
+            if i == 0:
+                early = quantise("z0", first, "first_ring0")
+        multiply(banks[chunk_banks[0]][:, 0:PAIR], w_last, *early)
         finish(2, 2, chunk_banks[1], second, "second_ring2")
         fourth = fetch_turned(6, 1, last_banks[0], nc.vector.tensor_copy)
         fifth = fetch_turned(7, 1, last_banks[1])

@@ -92,11 +92,17 @@ def tile_picked_wlapl_none_l_kernel(
 
         first_gate = sbuf("first_gate", T, F32)
         h = [keep.tile([P, T], F32, name=f"h{t}", tag=f"h{t}", align_bytes=64) for t in range(PARTS)]
-        row_words = sbuf("row_words", T * 2, F32)
-        rows = row_words.bitcast(BF16).rearrange("v (g p e) -> v g p e", p=P, e=2)
+        row_words = []
         second_wide = [sbuf(f"second_wide{t}", T, F32) for t in range(2)]
-        first_ring = [sbuf(f"first_ring{r}", BANK, F32) for r in range(2)]
-        second_ring = [sbuf(f"second_ring{r}", BANK, F32) for r in range(3)]
+        stair = sbuf("stair", 3 * P + T, F32)
+        step = sbuf("step", 3 * P, F32)
+        first_ring = [
+            (stair[:, PAIR:BANK], step[:, 0:PAIR]),
+            (stair[:, P : 3 * P], step[:, P:]),
+            (stair[:, 0:PAIR], stair[:, PAIR:BANK]),
+        ]
+        second_slot = sbuf("second_slot", BANK, F32)
+        second_ring = [second_slot, second_wide[0][:, 0:BANK], second_wide[1][:, 0:BANK]]
 
         def spread_gate(f, b):
             bank = banks[b][:].rearrange("r (j p) -> r j p", j=PACK)
@@ -181,24 +187,28 @@ def tile_picked_wlapl_none_l_kernel(
         def gate_at(v0, width):
             return second_gate[v0 // BANK][:, v0 % BANK : v0 % BANK + width]
 
-        def weigh(term, factor):
-            nc.vector.scalar_tensor_tensor(term, term, -1.0, factor, MULT, MULT)
+        def weigh(term, factor, picked_values=None):
+            source = term if picked_values is None else picked_values
+            nc.vector.scalar_tensor_tensor(term, source, -1.0, factor, MULT, MULT)
 
         def round_sums(b, t, parts, block, blocks, copy=nc.scalar.copy):
-            target = rows[:, 2 * block : 2 * (block + blocks), t * QUADRANT : (t + parts) * QUADRANT, :]
+            rows = row_words[block // 4].bitcast(BF16).rearrange("v (g p e) -> v g p e", p=P, e=2)
+            at = 2 * (block % 4)
+            target = rows[:, at : at + 2 * blocks, t * QUADRANT : (t + parts) * QUADRANT, :]
             copy(
                 out=target.rearrange("v g (t q) e -> v t g q e", q=QUADRANT),
                 in_=banks[b][:, 0 : parts * blocks * P].rearrange("v (t g e q) -> v t g q e", t=parts, e=2, q=QUADRANT),
             )
-            probe(f"r{t}_{block}", rows[:, 2 * block, t * QUADRANT, 0:1])
+            probe(f"r{t}_{block}", rows[:, at, t * QUADRANT, 0:1])
 
         def turn_back(block, blocks, b):
             for i in range(2 * blocks):
-                at = (2 * block + i) * P
-                nc.tensor.transpose(banks[b][:, i * P : (i + 1) * P], row_words[:, at : at + P], ident[:])
+                at = (2 * (block % 4) + i) * P
+                nc.tensor.transpose(banks[b][:, i * P : (i + 1) * P], row_words[block // 4][:, at : at + P], ident[:])
 
-        def fetch_turned(block, blocks, b, copy=nc.scalar.copy):
-            target = sbuf(f"z_values{block}", blocks * P * PACK, BF16)
+        def fetch_turned(block, blocks, b, copy=nc.scalar.copy, target=None):
+            if target is None:
+                target = sbuf(f"z_values{block}", blocks * P * PACK, BF16)
             copy(
                 out=target.bitcast(F32).rearrange("p (b v u) -> p b v u", u=2, v=P),
                 in_=banks[b][:, 0 : blocks * PAIR].rearrange("p (b u v) -> p b v u", u=2, v=P),
@@ -209,8 +219,8 @@ def tile_picked_wlapl_none_l_kernel(
         def finish(block, blocks, b, values, tag=None):
             multiply(banks[b][:, 0 : blocks * P], w_last, *quantise(f"z{block}", values, tag))
 
-        def store(block, blocks, b, copy, queue):
-            result = sbuf(f"result{block}", blocks * P, F32)
+        def store(block, blocks, b, copy, queue, tag=None):
+            result = sbuf(f"result{block}", blocks * P, F32, tag)
             copy(out=result, in_=banks[b][:, 0 : blocks * P])
             queue.dma_start(out=out[:, block * P : (block + blocks) * P], in_=result)
 
@@ -226,9 +236,9 @@ def tile_picked_wlapl_none_l_kernel(
 
         product_banks = {1: (5, 4), 2: (6, 7), 3: (5, 4)}
         wide_banks = {0: (0, 1), 1: (2, 3)}
-        chunk_banks = (6, 7, 0)
-        back_banks = (4, 5, 4)
-        pair_bank, last_banks = 2, (1, 3)
+        chunk_banks = (6, 7, 5)
+        back_banks = (0, 2, 0)
+        pair_bank, last_banks = 4, (1, 3)
 
         def open_wide(t):
             for half in range(2):
@@ -251,24 +261,27 @@ def tile_picked_wlapl_none_l_kernel(
             gather_weighed(t, SHARED, second_wide[t][:, SHARED:T])
             add_blocks(wide_banks[t][1], 2, second_wide[t][:, SHARED:T], stop=True)
 
-        def open_chunk(c):
-            for t in (2, 3):
+        def open_chunks(t):
+            for c in range(t):
                 add_blocks(chunk_banks[c], (t - 2) * 2, h[t][:, c * PAIR : (c + 1) * PAIR], start=t == 2)
 
         def gather_seconds(c):
             for t in (2, 3):
                 gather_second(t, c * PAIR, second_ring[c][:, (t - 2) * PAIR : (t - 1) * PAIR])
 
-        def gather_firsts(c):
+        def gather_firsts(c, stop):
             for t in (2, 3):
-                term = first_ring[c % 2][:, (t - 2) * PAIR : (t - 1) * PAIR]
+                term = first_ring[c][t - 2]
                 gather_first(t, c * PAIR, term)
-                add_blocks(chunk_banks[c], (t - 2) * 2, term)
+                add_blocks(chunk_banks[c], (t - 2) * 2, term, stop=stop and t == 3)
 
-        def weigh_chunk(c):
-            terms = second_ring[c].rearrange("p (t v) -> p t v", t=2)
-            weigh(terms, gate_at(c * PAIR, PAIR).unsqueeze(1).to_broadcast([P, 2, PAIR]))
-            add_blocks(chunk_banks[c], 0, second_ring[c], stop=True)
+        def weigh_chunk(c, terms, stop):
+            weigh(
+                terms.rearrange("p (t v) -> p t v", t=2),
+                gate_at(c * PAIR, PAIR).unsqueeze(1).to_broadcast([P, 2, PAIR]),
+                second_ring[c].rearrange("p (t v) -> p t v", t=2),
+            )
+            add_blocks(chunk_banks[c], 0, terms, stop=stop)
 
         values = round_part(1, sbuf("values1", BANK, BF16, "w0_codes"), nc.scalar.copy)
         term = gather_wide(0, 0)
@@ -296,72 +309,77 @@ def tile_picked_wlapl_none_l_kernel(
         add_blocks(wide_banks[1][0], 0, gather_wide(1, 0))
         weigh_wide(0, 1)
         add_blocks(wide_banks[1][1], 0, gather_wide(1, 1))
+        open_chunks(2)
         last_gate = sbuf("last_gate", PAIR, F32, "w23_scales")
         nc.vector.tensor_scalar(last_gate, gate_at(SHARED, PAIR), -1.0, None, MULT)
         weigh_wide(1, 0)
         close_wide(0)
+        add_blocks(chunk_banks[2], 0, h[2][:, BANK:SHARED], start=True)
+        open_chunks(3)
+        add_blocks(pair_bank, 0, h[2][:, SHARED:T], start=True)
         weigh_wide(1, 1)
         close_wide(1)
-        last_values = sbuf("last_values", PACK * P, BF16, "w23_codes")
+
+        gather_seconds(0)
+        gather_firsts(0, False)
+        weigh_chunk(0, second_ring[0], True)
+        gather_seconds(1)
+        row_words.append(sbuf("row_words0", T, F32, "w23_codes"))
+        round_sums(wide_banks[0][0], 0, 1, 0, 4)
+        weigh_chunk(1, second_ring[1], False)
+        gather_firsts(1, True)
+        gather_seconds(2)
+        round_sums(wide_banks[1][0], 1, 1, 0, 4)
+        round_sums(chunk_banks[0], 2, 2, 0, 2)
+        weigh_chunk(2, second_ring[1], False)
+        turn_back(0, 2, back_banks[0])
+        round_sums(chunk_banks[1], 2, 2, 2, 2)
+        gather_firsts(2, True)
+        row_words.append(sbuf("row_words1", T, F32, "second_slot"))
+        for i, b in enumerate(last_banks):
+            round_sums(wide_banks[i][1], i, 1, 4, 4)
+            add_blocks(b, 0, h[3][:, (6 + i) * P : (7 + i) * P], start=True)
+        joint = second_wide[0][:, PAIR:T].bitcast(BF16)
+        fetch_turned(0, 2, back_banks[0], target=joint[:, BANK:])
+        round_sums(chunk_banks[2], 2, 2, 4, 2)
+        turn_back(2, 2, back_banks[1])
+        middle = stair[:, 3 * P :].bitcast(BF16)
+        fetch_turned(2, 2, back_banks[1], target=middle[:, 0:T])
+        gather_first(2, SHARED, first_ring[1][1])
+        add_blocks(pair_bank, 0, first_ring[1][1])
+        gather_weighed(2, SHARED, second_ring[1][:, PAIR:BANK])
+        add_blocks(pair_bank, 0, second_ring[1][:, PAIR:BANK], stop=True)
+        turn_back(4, 2, back_banks[2])
+        gather_first(3, SHARED, first_ring[2][0])
+        last_terms = [first_ring[1][1][:, i * P : (i + 1) * P] for i in range(2)]
+        for i, b in enumerate(last_banks):
+            add_blocks(b, 0, first_ring[2][0][:, i * P : (i + 1) * P])
+        for i, b in enumerate(last_banks):
+            gather_weighed(3, (6 + i) * P, last_terms[i])
+            add_blocks(b, 0, last_terms[i], stop=True)
+        last_values = joint[:, 0:BANK]
         nc.vector.tensor_copy(
             out=last_values.rearrange("p (c n j) -> p c j n", n=4, j=PACK),
             in_=stage[PARTS].rearrange("p j (c n) -> p c j n", n=4),
         )
-
-        open_chunk(0)
-        open_chunk(1)
-        gather_seconds(0)
-        gather_firsts(0)
-        w_last = quantise("w4", last_values)
-        round_sums(wide_banks[0][0], 0, 1, 0, 4)
-        weigh_chunk(0)
-        gather_seconds(1)
-        gather_firsts(1)
-        round_sums(wide_banks[1][0], 1, 1, 0, 4)
-        round_sums(chunk_banks[0], 2, 2, 0, 2)
-        weigh_chunk(1)
-        round_sums(chunk_banks[1], 2, 2, 2, 2)
-        turn_back(0, 2, back_banks[0])
-        first = fetch_turned(0, 2, back_banks[0])
-        open_chunk(2)
-        add_blocks(pair_bank, 0, h[2][:, SHARED:T], start=True)
-        gather_seconds(2)
-        gather_firsts(2)
-        for i, b in enumerate(last_banks):
-            round_sums(wide_banks[i][1], i, 1, 4, 4)
-            add_blocks(b, 0, h[3][:, (6 + i) * P : (7 + i) * P], start=True)
-        weigh_chunk(2)
-        turn_back(2, 2, back_banks[1])
-        gather_first(2, SHARED, first_ring[1][:, 0:PAIR])
-        add_blocks(pair_bank, 0, first_ring[1][:, 0:PAIR])
-        gather_weighed(2, SHARED, first_ring[1][:, PAIR:BANK])
-        add_blocks(pair_bank, 0, first_ring[1][:, PAIR:BANK], stop=True)
-        gather_first(3, SHARED, first_ring[0][:, 0:PAIR])
-        last_terms = sbuf("last_terms", PAIR, F32, "second_ring2")
-        for i, b in enumerate(last_banks):
-            add_blocks(b, 0, first_ring[0][:, i * P : (i + 1) * P])
-        for i, b in enumerate(last_banks):
-            gather_weighed(3, (6 + i) * P, last_terms[:, i * P : (i + 1) * P])
-            add_blocks(b, 0, last_terms[:, i * P : (i + 1) * P], stop=True)
-        round_sums(chunk_banks[2], 2, 2, 4, 2)
         round_sums(pair_bank, 2, 1, 6, 2)
-        turn_back(4, 2, back_banks[2])
-        second = fetch_turned(2, 2, back_banks[1])
-        third = fetch_turned(4, 2, back_banks[2])
+        fetch_turned(4, 2, back_banks[2], target=middle[:, T:])
         for i, b in enumerate(last_banks):
             round_sums(b, 3, 1, 6 + i, 1, nc.vector.tensor_copy)
             turn_back(6 + i, 1, b)
-            if i == 0:
-                early = quantise("z0", first, "first_ring0")
-        multiply(banks[chunk_banks[0]][:, 0:PAIR], w_last, *early)
-        finish(2, 2, chunk_banks[1], second, "second_ring2")
-        fourth = fetch_turned(6, 1, last_banks[0], nc.vector.tensor_copy)
+        fourth = fetch_turned(6, 1, last_banks[0])
         fifth = fetch_turned(7, 1, last_banks[1])
-        finish(4, 2, chunk_banks[2], third)
+        codes, scales = quantise("z0", joint, "step")
+        w_last = (codes[:, 0:P], scales[:, 0:P])
+        multiply(banks[chunk_banks[0]][:, 0:PAIR], w_last, codes[:, P:], scales[:, P:])
+        codes, scales = quantise("z2", middle)
+        for c in range(2):
+            span = slice(c * PAIR, (c + 1) * PAIR)
+            multiply(banks[chunk_banks[c + 1]][:, 0:PAIR], w_last, codes[:, span], scales[:, span])
         finish(6, 1, pair_bank, fourth)
         finish(7, 1, back_banks[1], fifth)
         store(0, 2, chunk_banks[0], nc.scalar.copy, nc.sync)
-        store(2, 2, chunk_banks[1], nc.scalar.copy, nc.sync)
-        store(4, 2, chunk_banks[2], nc.vector.tensor_copy, nc.sync)
+        store(2, 2, chunk_banks[1], nc.vector.tensor_copy, nc.sync)
+        store(4, 2, chunk_banks[2], nc.scalar.copy, nc.sync)
         store(6, 1, pair_bank, nc.vector.tensor_copy, nc.sync)
         store(7, 1, back_banks[1], nc.scalar.copy, nc.scalar)

from contextlib import ExitStack

import concourse.mybir as mybir

K, T, H, N = 512, 1024, 512, 128
FLOPS = 2 * K * H * T + 2 * H * N * T

F32 = mybir.dt.float32
BF16 = mybir.dt.bfloat16
I32 = mybir.dt.int32
U32 = mybir.dt.uint32
U16 = mybir.dt.uint16
U8 = mybir.dt.uint8
FP8X4 = mybir.dt.float8_e4m3fn_x4
MULT = mybir.AluOpType.mult
COPY = mybir.ActivationFunctionType.Copy

P = 128
PACK = 4
BANK = 512
PAIR = 2 * P
PARTS = H // P
LISTS = 2
LIST_ROWS = 16
QUADRANT = 32
QUARTER = T // 4
GATE_RUN = T // P
SHARED = T - PAIR
PROBES = (None, None)


def tile_picked_wlapl_none_l_kernel(
    tc, x_words, x_scales, w1, w2, gate, pos1, pos2, out
):
    nc = tc.nc
    with ExitStack() as ctx:
        keep = ctx.enter_context(tc.tile_pool(name="keep", bufs=1))
        psum = ctx.enter_context(tc.psum_pool(name="psum", bufs=1))
        banks = [psum.tile([P, BANK], F32, name=f"bank{b}") for b in range(8)]

        def probe(label, ap):
            if label in PROBES:
                clock = keep.tile([P, 1], ap.dtype, name=f"clock{PROBES.index(label)}")
                nc.gpsimd.tensor_copy(out=clock[:], in_=ap)

        def sbuf(name, width, dtype, tag=None):
            return keep.tile([P, width], dtype, name=name, tag=tag or name, align_bytes=64)[:]

        x_planes = sbuf("x_planes", QUARTER, U8)
        nc.vector.memset(x_planes.bitcast(I32), 0)

        w1_rows = w1.rearrange("(p j) c -> p j c", j=PACK)
        stage = [sbuf(f"stage{w}", PACK * P, F32).rearrange("p (j c) -> p j c", j=PACK) for w in range(PARTS + 1)]
        gate_cols = sbuf("gate_cols", GATE_RUN, F32)
        second_gate = [sbuf(f"second_gate{f}", BANK, F32) for f in range(2)]
        x_codes = [sbuf("x_codes0", BANK, U32), sbuf("x_codes1", QUARTER, U32), sbuf("x_codes2", QUARTER, U32)]
        x_quarters = [x_codes[0][:, 0:QUARTER], x_codes[0][:, QUARTER:BANK], x_codes[1], x_codes[2]]
        lists = [keep.tile([P, T // LIST_ROWS], U16, name=f"list{d}") for d in range(LISTS)]

        nc.sync.dma_start(out=gate_cols, in_=gate[0, 0, :].rearrange("(p j) -> p j", j=GATE_RUN))
        nc.sync.dma_start(out=stage[0], in_=w1_rows[:, :, 0:P])
        x_source = x_words[0].rearrange("p n j -> p (n j)").bitcast(I32)
        nc.sync.dma_start(out=x_codes[0].bitcast(I32), in_=x_source[:, 0:BANK])
        for q in range(P // QUADRANT):
            nc.sync.dma_start(
                out=x_planes[QUADRANT * q : QUADRANT * q + 16, :].bitcast(I32),
                in_=x_scales[0, 4 * q : 4 * q + 4, :].bitcast(I32).rearrange("r (a c) -> a r c", a=4),
            )
        for a in (2, 3):
            nc.sync.dma_start(out=x_quarters[a].bitcast(I32), in_=x_source[:, a * QUARTER : (a + 1) * QUARTER])
        for t in range(1, PARTS):
            nc.sync.dma_start(out=stage[t], in_=w1_rows[:, :, t * P : (t + 1) * P])
            if t == 1:
                nc.sync.dma_start(lists[0][:], pos1)
                nc.sync.dma_start(lists[1][:], pos2)
        for f in range(2):
            nc.sync.dma_start(out=second_gate[f], in_=gate[1, :, f * BANK : (f + 1) * BANK])
        nc.sync.dma_start(out=stage[PARTS], in_=w2.rearrange("(p j) c -> p j c", j=PACK))

        ident = keep.tile([P, P], F32, name="ident")
        zeros = sbuf("zeros", P, F32, "first")
        nc.vector.memset(zeros, 0.0)
        nc.gpsimd.affine_select(
            out=ident[:],
            in_=zeros,
            compare_op=mybir.AluOpType.not_equal,
            fill=1.0,
            base=0,
            pattern=[[-1, P]],
            channel_multiplier=1,
        )

        first_gate = sbuf("first_gate", T, F32)
        h = [keep.tile([P, T], F32, name=f"h{t}", tag=f"h{t}", align_bytes=64) for t in range(PARTS)]
        row_words = []
        second_wide = [sbuf(f"second_wide{t}", T, F32) for t in range(2)]
        stair = sbuf("stair", 3 * P + T, F32)
        step = sbuf("step", 3 * P, F32)
        first_ring = [
            (stair[:, PAIR:BANK], step[:, 0:PAIR]),
            (stair[:, P : 3 * P], step[:, P:]),
            (stair[:, 0:PAIR], stair[:, PAIR:BANK]),
        ]
        second_slot = sbuf("second_slot", BANK, F32)
        second_ring = [second_slot, second_wide[0][:, 0:BANK], second_wide[1][:, 0:BANK]]

        def spread_gate(f, b):
            bank = banks[b][:].rearrange("r (j p) -> r j p", j=PACK)
            for j in range(PACK):
                column = gate_cols[:, PACK * f + j : PACK * f + j + 1]
                nc.tensor.transpose(bank[:, j, :], column.to_broadcast([P, P]), ident[:])
            target = first_gate.rearrange("r (p f j) -> r p f j", f=2, j=PACK)[:, :, f, :]
            nc.scalar.activation(out=target, in_=bank.rearrange("r j p -> r p j"), func=COPY, scale=-1.0)

        def round_part(t, values, copy=nc.vector.tensor_copy):
            copy(
                out=values.rearrange("p (s q j) -> p q s j", s=PACK, j=PACK),
                in_=stage[t].rearrange("p j (q s) -> p q s j", s=PACK),
            )
            return values

        def quantise(name, values, tag=None):
            width = values.shape[1] // PACK
            codes = sbuf(f"{name}_codes", width, U32, tag)
            scales = sbuf(f"{name}_scales", width, U8)
            nc.vector.quantize_mx(out=codes.bitcast(FP8X4), scales=scales, in_=values)
            probe(name, scales[:, 0:1])
            return codes, scales

        def multiply(acc, weights, codes, scales):
            nc.tensor.matmul_mx(
                out=acc,
                lhsT=weights[0].bitcast(FP8X4),
                lhsT_scale=weights[1],
                rhs=codes.bitcast(FP8X4),
                rhs_scale=scales,
                start=True,
                stop=True,
            )

        def project_quarter(weights, a, acc):
            multiply(acc, weights, x_quarters[a], x_planes[4 * a : P, :])

        def project_half(weights, half, b):
            for a in range(2):
                project_quarter(weights, 2 * half + a, banks[b][:, a * QUARTER : (a + 1) * QUARTER])

        def project(weights, pair_of_banks):
            for half, b in enumerate(pair_of_banks):
                project_half(weights, half, b)

        def fetch_half(t, half, b):
            nc.scalar.copy(out=h[t][:, half * BANK : (half + 1) * BANK], in_=banks[b][:])
            probe(f"h{t}{half}", h[t][:, half * BANK : half * BANK + 1])

        def fetch_part(t, pair_of_banks):
            for half, b in enumerate(pair_of_banks):
                fetch_half(t, half, b)

        def add_turned(b, slot, source, start=False, stop=False):
            nc.tensor.matmul(
                banks[b][:, slot * P : (slot + 1) * P], source, ident[:], start=start, stop=stop, is_transpose=True
            )

        def add_blocks(b, slot, source, start=False, stop=False):
            blocks = source.shape[1] // P
            for i in range(blocks):
                add_turned(b, slot + i, source[:, i * P : (i + 1) * P], start and i == 0, stop and i == blocks - 1)

        def picked(t, d, v0, width):
            return h[t][:].indirect(lists[d][:, v0 // LIST_ROWS : (v0 + width) // LIST_ROWS])

        def gather_first(t, v0, term):
            width = term.shape[1]
            nc.vector.tensor_tensor(term, picked(t, 0, v0, width), first_gate[:, v0 : v0 + width], MULT)
            probe(f"a{t}_{v0}", term[:, 0:1])

        def gather_second(t, v0, term):
            nc.scalar.activation(term, picked(t, 1, v0, term.shape[1]), COPY)
            probe(f"b{t}_{v0}", term[:, 0:1])

        def gather_weighed(t, v0, term):
            width = term.shape[1]
            nc.vector.tensor_tensor(term, picked(t, 1, v0, width), last_gate[:, v0 - SHARED : v0 - SHARED + width], MULT)
            probe(f"b{t}_{v0}", term[:, 0:1])

        def gate_at(v0, width):
            return second_gate[v0 // BANK][:, v0 % BANK : v0 % BANK + width]

        def weigh(term, factor, picked_values=None):
            source = term if picked_values is None else picked_values
            nc.vector.scalar_tensor_tensor(term, source, -1.0, factor, MULT, MULT)

        def round_sums(b, t, parts, block, blocks, copy=nc.scalar.copy):
            rows = row_words[block // 4].bitcast(BF16).rearrange("v (g p e) -> v g p e", p=P, e=2)
            at = 2 * (block % 4)
            target = rows[:, at : at + 2 * blocks, t * QUADRANT : (t + parts) * QUADRANT, :]
            copy(
                out=target.rearrange("v g (t q) e -> v t g q e", q=QUADRANT),
                in_=banks[b][:, 0 : parts * blocks * P].rearrange("v (t g e q) -> v t g q e", t=parts, e=2, q=QUADRANT),
            )
            probe(f"r{t}_{block}", rows[:, at, t * QUADRANT, 0:1])

        def turn_back(block, blocks, b):
            for i in range(2 * blocks):
                at = (2 * (block % 4) + i) * P
                nc.tensor.transpose(banks[b][:, i * P : (i + 1) * P], row_words[block // 4][:, at : at + P], ident[:])

        def fetch_turned(block, blocks, b, copy=nc.scalar.copy, target=None):
            if target is None:
                target = sbuf(f"z_values{block}", blocks * P * PACK, BF16)
            copy(
                out=target.bitcast(F32).rearrange("p (b v u) -> p b v u", u=2, v=P),
                in_=banks[b][:, 0 : blocks * PAIR].rearrange("p (b u v) -> p b v u", u=2, v=P),
            )
            probe(f"c{block}", target[:, 0:1])
            return target

        def finish(block, blocks, b, values, tag=None):
            multiply(banks[b][:, 0 : blocks * P], w_last, *quantise(f"z{block}", values, tag))

        def store(block, blocks, b, copy, queue, tag=None):
            result = sbuf(f"result{block}", blocks * P, F32, tag)
            copy(out=result, in_=banks[b][:, 0 : blocks * P])
            queue.dma_start(out=out[:, block * P : (block + blocks) * P], in_=result)

        spread_gate(0, 2)
        spread_gate(1, 3)
        weights = quantise("w0", round_part(0, sbuf("values0", BANK, BF16, "first")))
        for a, b in enumerate((6, 7, 4, 5)):
            acc = banks[b][:, 0:QUARTER]
            project_quarter(weights, a, acc)
            copy = nc.vector.tensor_copy if a % 2 == 0 else nc.scalar.copy
            copy(out=h[0][:, a * QUARTER : (a + 1) * QUARTER], in_=acc)
        probe("h0", h[0][:, T - 1 : T])

        product_banks = {1: (5, 4), 2: (6, 7), 3: (5, 4)}
        wide_banks = {0: (0, 1), 1: (2, 3)}
        chunk_banks = (6, 7, 5)
        back_banks = (0, 2, 0)
        pair_bank, last_banks = 4, (1, 3)

        def open_wide(t):
            for half in range(2):
                add_blocks(wide_banks[t][half], 0, h[t][:, half * BANK : (half + 1) * BANK], start=True)

        def gather_wide(t, half):
            term = sbuf(f"first_wide{t}{half}", BANK, F32, "stage1" if (t, half) == (0, 1) else None)
            gather_first(t, half * BANK, term)
            return term

        def gather_wide_second(t, half):
            gather_second(t, half * BANK, second_wide[t][:, half * BANK : min((half + 1) * BANK, SHARED)])

        def weigh_wide(t, half):
            term = second_wide[t][:, half * BANK : min((half + 1) * BANK, SHARED)]
            weigh(term, gate_at(half * BANK, term.shape[1]))
            add_blocks(wide_banks[t][half], 0, term, stop=half == 0)

        def close_wide(t):
            gather_weighed(t, SHARED, second_wide[t][:, SHARED:T])
            add_blocks(wide_banks[t][1], 2, second_wide[t][:, SHARED:T], stop=True)

        def open_chunks(t):
            for c in range(t):
                add_blocks(chunk_banks[c], (t - 2) * 2, h[t][:, c * PAIR : (c + 1) * PAIR], start=t == 2)

        def gather_seconds(c):
            for t in (2, 3):
                gather_second(t, c * PAIR, second_ring[c][:, (t - 2) * PAIR : (t - 1) * PAIR])

        def gather_firsts(c, stop):
            for t in (2, 3):
                term = first_ring[c][t - 2]
                gather_first(t, c * PAIR, term)
                add_blocks(chunk_banks[c], (t - 2) * 2, term, stop=stop and t == 3)

        def weigh_chunk(c, terms, stop):
            weigh(
                terms.rearrange("p (t v) -> p t v", t=2),
                gate_at(c * PAIR, PAIR).unsqueeze(1).to_broadcast([P, 2, PAIR]),
                second_ring[c].rearrange("p (t v) -> p t v", t=2),
            )
            add_blocks(chunk_banks[c], 0, terms, stop=stop)

        values = round_part(1, sbuf("values1", BANK, BF16, "w0_codes"), nc.scalar.copy)
        term = gather_wide(0, 0)
        weights = quantise("w1", values)
        for half in range(2):
            gather_wide_second(0, half)
            project_half(weights, half, product_banks[1][half])
            fetch_half(1, half, product_banks[1][half])
        open_wide(0)
        add_blocks(wide_banks[0][0], 0, term)
        values = sbuf("values23", 2 * BANK, BF16, "w1_codes")
        for t in (2, 3):
            round_part(t, values[:, (t - 2) * BANK : (t - 1) * BANK])
        term = gather_wide(0, 1)
        codes, scales = quantise("w23", values)
        for t in (2, 3):
            project((codes[:, (t - 2) * P : (t - 1) * P], scales[:, (t - 2) * P : (t - 1) * P]), product_banks[t])
        for half in range(2):
            gather_wide_second(1, half)
        for t in (2, 3):
            fetch_part(t, product_banks[t])
        add_blocks(wide_banks[0][1], 0, term)
        weigh_wide(0, 0)
        open_wide(1)
        add_blocks(wide_banks[1][0], 0, gather_wide(1, 0))
        weigh_wide(0, 1)
        add_blocks(wide_banks[1][1], 0, gather_wide(1, 1))
        open_chunks(2)
        last_gate = sbuf("last_gate", PAIR, F32, "w23_scales")
        nc.vector.tensor_scalar(last_gate, gate_at(SHARED, PAIR), -1.0, None, MULT)
        weigh_wide(1, 0)
        close_wide(0)
        add_blocks(chunk_banks[2], 0, h[2][:, BANK:SHARED], start=True)
        open_chunks(3)
        add_blocks(pair_bank, 0, h[2][:, SHARED:T], start=True)
        weigh_wide(1, 1)
        close_wide(1)

        gather_seconds(0)
        gather_firsts(0, False)
        weigh_chunk(0, second_ring[0], True)
        gather_seconds(1)
        row_words.append(sbuf("row_words0", T, F32, "w23_codes"))
        round_sums(wide_banks[0][0], 0, 1, 0, 4)
        weigh_chunk(1, second_ring[1], False)
        gather_firsts(1, True)
        gather_seconds(2)
        round_sums(wide_banks[1][0], 1, 1, 0, 4)
        round_sums(chunk_banks[0], 2, 2, 0, 2)
        weigh_chunk(2, second_ring[1], False)
        turn_back(0, 2, back_banks[0])
        round_sums(chunk_banks[1], 2, 2, 2, 2)
        gather_firsts(2, True)
        row_words.append(sbuf("row_words1", T, F32, "second_slot"))
        for i, b in enumerate(last_banks):
            round_sums(wide_banks[i][1], i, 1, 4, 4)
            add_blocks(b, 0, h[3][:, (6 + i) * P : (7 + i) * P], start=True)
        joint = second_wide[0][:, PAIR:T].bitcast(BF16)
        fetch_turned(0, 2, back_banks[0], target=joint[:, BANK:])
        round_sums(chunk_banks[2], 2, 2, 4, 2)
        turn_back(2, 2, back_banks[1])
        middle = stair[:, 3 * P :].bitcast(BF16)
        fetch_turned(2, 2, back_banks[1], target=middle[:, 0:T])
        gather_first(2, SHARED, first_ring[1][1])
        add_blocks(pair_bank, 0, first_ring[1][1])
        gather_weighed(2, SHARED, second_ring[1][:, PAIR:BANK])
        add_blocks(pair_bank, 0, second_ring[1][:, PAIR:BANK], stop=True)
        turn_back(4, 2, back_banks[2])
        gather_first(3, SHARED, first_ring[2][0])
        last_terms = [first_ring[1][1][:, i * P : (i + 1) * P] for i in range(2)]
        for i, b in enumerate(last_banks):
            add_blocks(b, 0, first_ring[2][0][:, i * P : (i + 1) * P])
        for i, b in enumerate(last_banks):
            gather_weighed(3, (6 + i) * P, last_terms[i])
            add_blocks(b, 0, last_terms[i], stop=True)
        last_values = joint[:, 0:BANK]
        nc.vector.tensor_copy(
            out=last_values.rearrange("p (c n j) -> p c j n", n=4, j=PACK),
            in_=stage[PARTS].rearrange("p j (c n) -> p c j n", n=4),
        )
        round_sums(pair_bank, 2, 1, 6, 2)
        fetch_turned(4, 2, back_banks[2], target=middle[:, T:])
        for i, b in enumerate(last_banks):
            round_sums(b, 3, 1, 6 + i, 1, nc.vector.tensor_copy)
            turn_back(6 + i, 1, b)
        fourth = fetch_turned(6, 1, last_banks[0])
        fifth = fetch_turned(7, 1, last_banks[1])
        codes, scales = quantise("z0", joint, "step")
        w_last = (codes[:, 0:P], scales[:, 0:P])
        multiply(banks[chunk_banks[0]][:, 0:PAIR], w_last, codes[:, P:], scales[:, P:])
        codes, scales = quantise("z2", middle)
        for c in range(2):
            span = slice(c * PAIR, (c + 1) * PAIR)
            multiply(banks[chunk_banks[c + 1]][:, 0:PAIR], w_last, codes[:, span], scales[:, span])
        finish(6, 1, pair_bank, fourth)
        finish(7, 1, back_banks[1], fifth)
        store(0, 2, chunk_banks[0], nc.scalar.copy, nc.sync)
        store(2, 2, chunk_banks[1], nc.vector.tensor_copy, nc.sync)
        store(4, 2, chunk_banks[2], nc.scalar.copy, nc.sync)
        store(6, 1, pair_bank, nc.vector.tensor_copy, nc.sync)
        store(7, 1, back_banks[1], nc.scalar.copy, nc.scalar)
